import numpy as np, ml_dtypes
CORES = [3,11,19,27,35,43,51,59]
N = 8
BF = ml_dtypes.bfloat16
def gentries(a):
    return np.ascontiguousarray(a.reshape(8, 16, -1).transpose(0, 2, 1)).reshape(8, -1)
def gtable(e):
    e = np.asarray(e); return np.ascontiguousarray(e.reshape(8, -1, 16).transpose(0, 2, 1)).reshape(128, -1).astype(np.int32)
A, H, S, ST, RO, R = 2048, 4096, 128, 5, 3, 11
def atoms(rng, reach):
    off = np.concatenate([np.arange(-reach, 0), np.arange(1, reach + 1)])
    ch = off[np.argsort(rng.random((8, A, 2 * reach)), axis=-1)[..., :16]]
    ch = ch * (rng.random((8, A, 1)) >= 0.03125)
    pos = (np.arange(A)[None, :, None] + ch) % A
    nb = np.zeros((8, 16, A), np.int64)
    for g in range(8):
        o = rng.permutation(A); nb[g][:, o] = o[pos[g]].T
    return nb
def parts(rng, reach=R):
    nb = atoms(rng, reach); e = rng.integers(0, 256, (N, 8, 16, H)); s0 = rng.integers(0, A, (N, 8, RO, S))
    return nb, e, s0, rng.integers(0, 256, (N, 8, 16, S)), rng.integers(70 * ST, 210 * ST, (N, 8, 16))
def layers(rng):
    m = (A - 1) // (2 * ST - 1); lay = rng.permutation(A - 1)[:m * (2 * ST - 1)].reshape(2 * ST - 1, m); nb = rng.integers(0, A, (16, A))
    nb[:8, lay[0]] = rng.choice(lay[1], (8, m)); nb[8:, lay[0]] = rng.choice(lay[ST], (8, m))
    for i in range(1, 2 * ST - 1):
        nb[:, lay[i]] = A - 1 if i in (ST - 1, 2 * ST - 2) else rng.choice(lay[i + 1], (16, m))
    return nb, lay[0]
def owned(rng):
    n = 2 * ST; free = np.ones(A, bool); taken = np.zeros(H, bool); c = np.zeros((S, n), np.int64)
    for j in range(S):
        for m in range(n):
            x = rng.permutation(np.flatnonzero(free)); hs = []
            if m >= 2: hs.append(place(c[j, m - 2], c[j, m - 1], x))
            if m == n - 1: hs += [place(c[j, m - 1], x, c[j, 0]), place(x, c[j, 0], c[j, 1])]
            good = np.ones(x.shape, bool)
            for a in range(len(hs)):
                good &= ~taken[hs[a]]
                for b in range(a): good &= hs[a] != hs[b]
            i = int(np.argmax(good)); c[j, m] = x[i]; free[x[i]] = False
            for h in hs: taken[h[i]] = True
    nb = rng.integers(0, A, (16, A)); nb[:8, c[:, 0]] = c[:, 1]; nb[8:, c[:, 0]] = c[:, n - 1]
    for m in range(1, ST):
        nb[:, c[:, m]] = c[:, m + 1]; nb[:, c[:, n - m]] = c[:, n - m - 1]
    return nb, c[:, 0]
def pack(nb, e, s0, q, th):
    return {"nb": np.repeat(nb.reshape(1, 128, A), N, axis=0).astype(np.int32), "ang": e.reshape(N, 128, H).astype(np.float32).astype(BF),
            "st": np.stack([gtable(a.reshape(8, -1)) for a in s0]), "q": q.reshape(N, 128, S).astype(np.float32).astype(BF), "th": th.reshape(N, 128, 1).astype(np.int32)}
def setup_inputs(rng):
    return pack(*parts(rng))
def setup_inputs_ties(rng):
    nb, e, s0, q, th = parts(rng); v = np.arange(A)[None, :]
    nb[0] = 8 * (v >> 3) + rng.integers(0, 8, (16, A)); e[:, 0] = rng.choice(np.array([0, 192, 255, 255, 255]), (N, 1, H)); q[:, 0] = 0
    e[:, 1] = 10 * rng.integers(0, 2, (N, 16, H)); q[:, 1] = 10 * rng.integers(0, 2, (N, 16, S)); th[:, 1] = 10 * rng.integers(1, ST + 1, (N, 16))
    e[:, 2] = rng.choice(np.array([0, 3, 4, 255]), (N, 1, H)); q[:, 2] = 4; th[:, 2] = rng.integers(255, 520, (N, 1))
    e[:, 3] = 7; q[:, 3] = rng.integers(0, 256, (N, 16, S)); th[:, 3] = 7 * rng.integers(3, 2 * ST, (N, 16))
    e[:, 4] = rng.choice(np.array([100, 156]), (N, 16, H)); q[:, 4] = 128
    e[:, 5] = e[:, 5] * rng.integers(0, 2, (N, 16, H))
    for r in range(N):
        for g, n in ((5, 9), (6, 8), (7, 16)): th[r, g] = np.where(rng.permutation(16) < n, 0, 4095)
    return pack(nb, e, s0, q, th)
def setup_inputs_repeats(rng):
    nb, e, s0, q, th = parts(rng, 8)
    s0[:, ::2] = rng.choice(np.array([0, A - 1, A // 2, 5]), (N, 4, RO, S))
    e[:, 1::2] = e[:1, 1::2].copy(); q[:, 2::4] = q[:, 2::4, :, :1].copy()
    return pack(nb, e, s0, q, th >> 1)
def setup_inputs_stuck(rng):
    nb, e, s0, q, th = parts(rng); v = np.arange(A)[None, :]; k = np.arange(16)[:, None]
    nb[0] = 4 * (v >> 2) + rng.integers(0, 4, (16, A))
    nb[1, :8] = v; nb[2, 8:] = v
    nb[3] = v ^ rng.integers(0, 2, (16, A)); nb[3, ::8] = v ^ 1; nb[4] = v
    nb[5] = nb[5][rng.integers(0, 4, (16, A)), np.repeat(v, 16, axis=0)]
    nb[6] = 8 * (v >> 3) + rng.integers(0, 8, (16, A))
    x = v & 127; nb[7] = np.where(x == 0, v + 16 + k, np.where((x < 16) | (x >= 16 * (ST - 2)), v - x, v + 16))
    for g in (0, 3, 4, 6): th[:, g] = rng.integers(0, 800, (N, 16))
    s0[:, :, :, 0] = 0; s0[:, :, :, S - 1] = A - 1
    s0[:, 7] = 128 * rng.integers(0, A >> 7, (N, RO, S)) + rng.integers(1, 16, (N, RO, S))
    s0[0, 3] = rng.integers(256, A, (RO, 1)); th[0, 3] = 0
    return pack(nb, e, s0, q, th)
def setup_inputs_far(rng):
    nb, e, s0, q, th = parts(rng)
    for g in range(8):
        nb[g], a = layers(rng); s0[:, g] = rng.choice(a, (N, RO, S))
    if 2 * ST * S <= A:
        nb[1], a = owned(rng); s0[:, 1] = a[np.argsort(rng.random((N, RO, S)), axis=-1)]
    th = rng.integers(200 * ST, 300 * ST, (N, 8, 16)); th[2:, 5] = 4095; th[2:, 6] = 0; th[:2] = 0
    e[:, 2] = rng.integers(224, 256, (N, 16, H)); th[:, 2] = rng.integers(min(2048, 448 * ST), 448 * ST + 1, (N, 16))
    e[:, 3] = 255; th[:, 3] = 510 * ST; th[2:, 3, :8] = 510 * ST + 1
    return pack(nb, e, s0, q, th)
def setup_inputs_spread(rng):
    nb, e, s0, q, th = parts(rng); v = np.arange(A)[None, :]; k = np.arange(16)[:, None]
    e = (np.exp2(8 * rng.random((N, 8, 1, H))) * rng.random((N, 8, 16, H))).astype(np.int64)
    q = (np.exp2(8 * rng.random((N, 8, 1, S))) * rng.random((N, 8, 16, S))).astype(np.int64)
    th = np.minimum(np.exp2(12 * rng.random((N, 8, 16))).astype(np.int64), 4095)
    s0 = np.minimum((A * rng.random((N, 8, RO, S)) ** 3).astype(np.int64), A - 1)
    c = v & 3; nb[0] = 4 * rng.integers(0, A >> 2, (16, A)) + np.where(c >= 2, c, np.where(k < 8, 2, 3))
    s0[:, 0] = 4 * (s0[:, 0] >> 2) + rng.integers(0, 2, (N, RO, S))
    nb[2:4] = rng.integers(0, A, (2, 16, A))
    return pack(nb, e, s0, q, th)
def check_inputs(d):
    bad = []
    for k, lo, hi in (("nb", 0, A - 1), ("ang", 0, 255), ("st", 0, A - 1), ("q", 0, 255), ("th", 0, 4095)):
        v = np.asarray(d[k]).astype(np.float64)
        if not np.all((v >= lo) & (v <= hi)): bad.append("range of " + k)
        elif not np.all(v == np.floor(v)): bad.append(k + " holds numbers that aren't whole")
    if np.any(d["nb"] != d["nb"][:1]): bad.append("nb isn't alike on all ranks")
    return bad
def place(p, v, n):
    return ((((2 * p + 1) * (2 * n + 1)) >> 4) + 37 * v) & (H - 1)
def walk(e, v0, w, rows, nbr):
    path = [v0]; kk = np.arange(16)[None, :, None]
    for i in range(ST):
        v = path[i]; p = path[max(i - 1, 0)]
        n = np.take_along_axis(nbr, v[:, None, :], 2)
        h = place(p[:, None, :], v[:, None, :], n)
        x = np.take_along_axis(e, h.reshape(8, 1, 16 * S), 2).reshape(8, 16, 16, S)
        sc = np.add.reduce(np.abs(x - w[:, :, None, :]), axis=1)
        bar = np.any(np.stack(path)[:, :, None, :] == n[None], axis=0)
        if i == 0: bar = bar | (kk < rows) | (kk >= rows + 8)
        sc = np.where(bar, 2 ** 20, sc); k = np.argmin(sc, axis=1)[:, None, :]
        ok = np.take_along_axis(sc, k, 1)[:, 0] < 2 ** 20
        path.append(np.where(ok, np.take_along_axis(n, k, 1)[:, 0], v))
    return np.stack(path)
def reference(nb, ang, st, q, th):
    e = np.asarray(ang, np.float32).astype(np.int32).reshape(N, 8, 16, H); w = np.asarray(q, np.float32).astype(np.int32).reshape(N, 8, 16, S)
    lim = th.astype(np.int64).reshape(N, 8, 16, 1); nbr = nb.astype(np.int64).reshape(N, 8, 16, A)
    sl = np.stack([gentries(a) for a in st]).astype(np.int64).reshape(N, 8, RO, S)
    rings = np.zeros((N, 8, 16, RO, S), np.int64); m = np.arange(16)[None, :, None]
    for t in range(RO):
        new = []
        for r in range(N):
            s = (r + 1 + t % (N - 1)) % N
            pa = walk(e[r], sl[r, :, t], w[r], 0, nbr[r]); pb = walk(e[s], sl[r, :, t], w[r], 8, nbr[s])
            eq = pa[1:, None] == pb[None, 1:]; eq[0, 0] = False
            eq = eq.reshape(ST * ST, 8, S); found = np.any(eq, axis=0); f = np.argmax(eq, axis=0)
            i = f // ST + 1; j = f - (i - 1) * ST + 1; ln = np.where(found, i + j, 0)[:, None, :]; i = i[:, None, :]
            ca = np.take_along_axis(pa.transpose(1, 0, 2), np.minimum(m, i), 1); cb = np.take_along_axis(pb.transpose(1, 0, 2), np.clip(ln - m, 0, ST), 1)
            c = np.where(m <= i, ca, cb); live = m < ln
            before = np.take_along_axis(c, np.clip(np.where(m == 0, ln - 1, m - 1), 0, 15), 1)
            after = np.take_along_axis(c, np.clip(np.where(m == ln - 1, 0, m + 1), 0, 15), 1)
            h = place(before, c, after)
            x = np.take_along_axis(e[r], h.reshape(8, 1, 16 * S), 2).reshape(8, 16, 16, S)
            tot = np.add.reduce(np.where(live[:, None], x, 0), axis=2)
            heavy = found & (np.add.reduce((tot >= lim[r]).astype(np.int64), axis=1) >= 9)
            use = live & heavy[:, None, :]; gg = np.broadcast_to(np.arange(8)[:, None, None], h.shape)
            mark = np.zeros((8, H), bool); mark[gg[use], h[use]] = True
            new.append(np.where(mark[:, None, :], e[r] - (e[r] >> 2), e[r])); rings[r, :, :, t] = np.where(live, c, -1)
        e = np.stack(new)
    return {"ye": e.reshape(N, 128, H).astype(np.float32).astype(BF), "yr": rings.reshape(N, 128, RO * S).astype(np.float32)}

@@ -1,0 +1,666 @@
+import numpy as np
+from concourse.bass import DstId, RemoteDMATransfer
+from concourse.mybir import dt, AluOpType, AxisListType, ActivationFunctionType
+
+AL = AluOpType
+AF = ActivationFunctionType
+RO, ST, N = 3, 5, 8
+TW = 4112
+F, B, I32, U16 = "float32", "bfloat16", "int32", "uint16"
+PHYS = {F: "vf", B: "vb", I32: "vi", U16: "vu"}
+SIZE = {F: 0, B: 0, I32: 0, U16: 0}
+VB = {}
+
+
+def _sb(dtype, **kw):
+    for k, n in kw.items():
+        VB[k] = (PHYS[dtype], SIZE[dtype], n)
+        SIZE[dtype] += (n + 31) // 32 * 32
+
+
+def _over(k, base, n):
+    VB[k] = (VB[base][0], VB[base][1], n)
+
+
+_sb(B, tab=TW, bits=TW, qa=2048, difa=2048, difb=2048, ada=2048, adb=2048, ibf=128, gk=8, penr=128, xsa=512, xsb=512,
+    tie=128, oneb=128, indn=128, indnl=128, indnh=128, xr=1280, hb=1280, ehi=512, elo=512,
+    ge=128, ohl=5120, flg=512, fx=256, la=2048, wid=960, negib=128, lt=128, rl=4096)
+_sb(F, nbw=2048, win2=2048, idf=128, indf=128, indl=128, indh=128, ind6=128, ind6l=128, ind6h=128, id6=128,
+    c0=128, onef=128, rs=128, rs0=128, dm=272, corrn=1, corrw=1, mlo=1, mhi=1, mhi8=1, mhi128=1, pf=1, gf=1, fi=1, cf=128, cg=128, cr=272,
+    cg8=8, rsc=128, rs0c=128, sel=2048, thf=1, nhc=8,
+    pw=1, p0=1, p1=1, p2=1, m6=1, m12=1, wh=1, wbm=4, lr=272, lsc=272, thr=80,
+    ft=32, fI=32, fJ=32, fT=32, fU=32, fV=32, tw=32, gy=2048, yo=128, narr=272, varr=272, bj=208, tj=272, eq=208, neq=208,
+    hp=208, ek=208, scj=208, hr=80, mk=80, off=80, of=128, na=128, nb2=128, xma=128, xmb=128, xm=128, cm=128, tp=128)
+_sb(F, eg=512, ex=512, ea=512, eb=512, wc=240)
+_sb(I32, e1=4096, sti=24, pi=1, gi=1, ii=1, b0=1, b1=1, b2=1, ei=512, wi=1, wi2=1, fii=32, pack=208, hji=272,
+    j8=8, hj=8, win24=32, c128=128, c8=8, stin=24, zpi=128, hpi=128, thi=1)
+_over("nbi", "e1", 2048)
+_over("ohh", "difa", 5120)
+_over("rh", "ohl", 4096)
+_sb(U16, qown=128, qpar=128, qmix=128, LP=18, LV=18, LN=18, LB=14, LM=6, off80=80, fl=8, ofu=128, nlb=40, ls=8, ls0=8)
+for _x in "ab":
+    _sb(F, **{"t1" + _x: 128, "nn" + _x: 128, "rv" + _x: 128, "r" + _x: 128, "ks" + _x: 128, "w" + _x: 128, "sc" + _x: 128})
+    _sb(I32, **{"zi" + _x: 128, "hi" + _x: 128})
+    _sb(U16, **{"vl" + _x: 8, "hl" + _x: 128})
+    _sb(B, **{"pn" + _x: 640, "unb" + _x: 128, "mk" + _x: 128})
+for _t in range(RO):
+    if _t < 2:
+        _sb(B, **{"qm%d" % _t: 2048, "qb%d" % _t: 2048})
+        _sb(F, **{"xa%d" % _t: 1536})
+    _sb(B, **{"qw%d" % _t: 256, "unp%d" % _t: 128, "pnp%d" % _t: 128})
+    _sb(F, **{"xb%d" % _t: 640, "aw%d" % _t: 88, "bo%d" % _t: 40, "nm%d" % _t: 128, "rpa%d" % _t: 128, "rpb%d" % _t: 128})
+    _sb(U16, **{"h0%d" % _t: 128, "va%d" % _t: 8, "vb%d" % _t: 8})
+_over("qm2", "qm0", 2048)
+_over("qb2", "qb0", 2048)
+_over("xa2", "xa0", 1536)
+SCRATCH = {PHYS[d]: ("sbuf", [128, SIZE[d]], d) for d in PHYS}
+for _i in range(8):
+    SCRATCH["pb%d" % _i] = ("psum", [128, 512], F)
+    VB["pb%d" % _i] = ("pb%d" % _i, 0, 512)
+NDMA = 24
+SEMAPHORES = ["sV", "sS", "sP", "sG", "ls"] + ["d%d" % i for i in range(NDMA)] + ["rq%d" % i for i in range(RO)] + \
+    ["rs%d" % i for i in range(RO)] + ["rb%d" % i for i in range(RO)]
+CACHE = {}
+BIG = 16777216.0
+CB = -296.0 - 8388608.0
+SCHUNKS = (3,)
+
+
+def program(g, core, T, topo):
+    rank = T.rank_of(core)
+    ops = []
+    dn = [0]
+
+    def X(n, a, b, s=1, p=None):
+        ph, o, _ = VB[n]
+        ps = slice(None) if p is None else slice(p[0], p[1])
+        cs = slice(o + a, o + b, s) if s > 1 else slice(o + a, o + b)
+        return (T[ph][ps, cs], [(ph, o + a, o + b)])
+
+    def W(n):
+        return X(n, 0, VB[n][2])
+
+    def IX(n, a, b, o, c, d):
+        w, l = X(n, a, b), X(o, c, d)
+        return (w[0].indirect(l[0]), w[1] + l[1])
+
+    def add(e, fn, r, w, c, **kw):
+        ops.append(dict(e=e, fn=fn, r=[y for x in r for y in x[1]], w=[y for x in w for y in x[1]], c=c, **kw))
+        return len(ops) - 1
+
+    def sc(s):
+        return (s[0], [s]) if isinstance(s, tuple) else (s, [])
+
+    def vts(o, a, s1, s2, o0, o1=None, n=128, k=1.0):
+        (v1, r1), (v2, r2) = sc(s1), sc(s2)
+        if o1 is None:
+            f = lambda: [g.vector.tensor_scalar(out=o[0], in0=a[0], scalar1=v1, scalar2=None, op0=o0)]
+        else:
+            f = lambda: [g.vector.tensor_scalar(out=o[0], in0=a[0], scalar1=v1, scalar2=v2, op0=o0, op1=o1)]
+        add("V", f, [a] + r1 + r2, [o], .05 + max(64, n * k) * .83e-3)
+
+    def vtt(o, a, b, op, n=128, k=2.0):
+        add("V", lambda: [g.vector.tensor_tensor(out=o[0], in0=a[0], in1=b[0], op=op)], [a, b], [o], .05 + max(64, n * k) * .83e-3)
+
+    def vcp(o, a, n=128, k=1.0):
+        add("V", lambda: [g.vector.tensor_copy(out=o[0], in_=a[0])], [a], [o], .05 + max(64, n * k) * .83e-3)
+
+    def vms(o, v, n=128):
+        add("V", lambda: [g.vector.memset(o[0], v)], [], [o], .05 + max(64, n) * .83e-3)
+
+    def vscan(o, d0, d1, ini, o0, o1, n=128):
+        add("V", lambda: [g.vector.tensor_tensor_scan(out=o[0], data0=d0[0], data1=d1[0], initial=ini, op0=o0, op1=o1)],
+            [d0, d1], [o], .05 + max(64, n) * .83e-3)
+
+    def act(o, a, fn, n=128, k=1.0, bias=None, scale=None):
+        kw, r = {}, []
+        if bias is not None:
+            kw["bias"], rr = sc(bias)
+            r = r + rr
+        if scale is not None:
+            kw["scale"], rr = sc(scale)
+            r = r + rr
+        add("S", lambda: [g.scalar.activation(out=o[0], in_=a[0], func=fn, **kw)], [a] + r, [o], .065 + max(64, n * k) * .83e-3)
+
+    def mm(l, c):
+        add("P", lambda: [g.tensor.matmul(out=o[0], lhsT=a[0], rhs=b[0], start=s, stop=p) for o, a, b, s, p in l],
+            [x for m in l for x in m[1:3]], [m[0] for m in l], c * .45e-3 + .03)
+
+    def iota(o, pat, base, cm, n=64, small=False):
+        kw = {"allow_small_or_imprecise_dtypes": True} if small else {}
+        add("G", lambda: [g.iota(o[0], pattern=pat, base=base, channel_multiplier=cm, **kw)], [], [o], .13 + 2 * n * .83e-3)
+
+    def keep(o, pat, cm, n, base=0):
+        add("G", lambda: [g.affine_select(out=o[0], in_=o[0], pattern=pat, compare_op=AL.is_equal, fill=0.0, base=base, channel_multiplier=cm)],
+            [o], [o], .17 + 2 * n * .83e-3)
+
+    def dma(o, a, lat=2.5):
+        i = dn[0]
+        dn[0] += 1
+        add("Y", lambda: [g.sync.dma_start(out=o[0], in_=a[0])], [a], [o], .1, lat=lat, sem="d%d" % i)
+
+    def ext(n):
+        return (T[n][:], [])
+
+    outq = [T.cores[(rank + 1 + t % (N - 1)) % N] for t in range(RO)]
+    back = [T.cores[(rank - 1 - t % (N - 1)) % N] for t in range(RO)]
+    NE = 2
+
+    def engs(dst, first, n):
+        m = 0
+        for e in topo.engines(core, dst)[first:first + n]:
+            m |= 1 << e
+        return m
+
+    def exchange(kind):
+        tr = []
+        for t in range(RO):
+            a = topo.addr(outq[t])
+            src = X("qw%d" % t, 0, 128)[0] if kind == "q" else X("sti", 8 * t, 8 * t + 8)[0]
+            dst = X("qw%d" % t, 128, 256)[0] if kind == "q" else X("stin", 8 * t, 8 * t + 8)[0]
+            tr.append(RemoteDMATransfer(dst_ids=[DstId(rid=a[0], pnc=a[1])], dma_engine_mask=engs(outq[t], NE * t, NE),
+                                        remote_sem=T.sem["r%s%d" % (kind, t)], src=src, dst=dst))
+        g.remote_dma_fused(tr, local_sem=T.sem.ls)
+        return []
+
+    def sendb(t):
+        a = topo.addr(back[t])
+        g.remote_dma(out_ap=X("aw%d" % t, 48, 88)[0], in_ap=X("bo%d" % t, 0, 40)[0], remote_sem=T.sem["rb%d" % t], local_sem=T.sem.ls,
+                     pid=a[1], routing_id=a[0], dma_engine_mask=engs(back[t], 0, 4))
+        return []
+
+    lsn = NE * RO * 2 + 4 * RO
+
+    dma(W("sti"), ext("st"))
+    for t in range(RO):
+        dma(X("qw%d" % t, 0, 128), ext("q"))
+    dma(W("nbi"), ext("nb"), 5.0)
+    dma(X("tab", 0, 4096), ext("ang"), 6.0)
+    dma(W("thi"), ext("th"))
+    s1 = add("G", lambda: exchange("s"), [W("sti")], [], 1.0)
+    s2 = add("G", lambda: exchange("q"), [X("qw%d" % t, 0, 128) for t in range(RO)], [], 1.0)
+    for t in range(RO):
+        add("R", None, [], [X("stin", 8 * t, 8 * t + 8)], 3.0, mdep=[s1], sem="rs%d" % t, cnt=NE)
+        add("R", None, [], [X("qw%d" % t, 128, 256)], 3.0, mdep=[s2], sem="rq%d" % t, cnt=NE)
+
+    iota(W("pi"), [[0, 1]], 0, 1)
+    iota(W("cf"), [[1, 128]], 0, 0, 128, True)
+    iota(W("cg"), [[1, 8], [0, 16]], 0, 0, 128, True)
+    iota(W("cr"), [[0, 17], [1, 16]], 0, 0, 272, True)
+    iota(W("win2"), [[2, 2048]], 1, 0, 2048, True)
+    iota(W("c128"), [[1, 128]], 0, 0, 128)
+    vts(W("gi"), W("pi"), 4, None, AL.arith_shift_right)
+    vts(W("ii"), W("pi"), 15, None, AL.bitwise_and)
+    vcp(W("pf"), W("pi"))
+    vcp(W("gf"), W("gi"))
+    vcp(W("fi"), W("ii"))
+    P_, G_, I_ = W("pf"), W("gf"), W("fi")
+    vts(W("mhi"), I_, 8.0, None, AL.is_ge)
+    vts(W("mlo"), I_, 8.0, None, AL.is_lt)
+    vts(W("mhi128"), W("mhi"), 128.0, None, AL.mult)
+    vts(W("mhi8"), W("mhi"), 8.0, -8.0, AL.mult, AL.add)
+    vts(W("corrw"), I_, 8192.0, -122880.0, AL.mult, AL.add)
+    vts(W("corrn"), W("corrw"), -1.0, 1.0, AL.mult, AL.add)
+    vcp(W("qown"), W("c128"))
+    vts(W("qpar"), W("c128"), 128.0, None, AL.add)
+    vts(W("qmix"), W("c128"), W("mhi128"), None, AL.add)
+    iota(W("c8"), [[16, 8]], 15, 0, 8)
+    vcp(W("ls"), W("c8"))
+    vts(W("ls0"), W("c8"), W("mhi8"), None, AL.add)
+    vts(W("ibf"), W("cf"), P_, None, AL.is_equal)
+    vts(W("negib"), W("cf"), P_, -1.0, AL.is_equal, AL.mult)
+    vts(W("idf"), W("cf"), P_, None, AL.is_equal)
+    vts(W("id6"), W("cf"), P_, 296.0, AL.is_equal, AL.mult)
+    vts(W("penr"), W("cf"), P_, -131072.0, AL.is_equal, AL.mult)
+    vts(W("indf"), W("cg"), G_, None, AL.is_equal)
+    vts(W("indl"), W("cg"), G_, W("mlo"), AL.is_equal, AL.mult)
+    vts(W("indh"), W("cg"), G_, W("mhi"), AL.is_equal, AL.mult)
+    vts(W("ind6"), W("cg"), G_, 296.0, AL.is_equal, AL.mult)
+    vts(W("ind6l"), W("indl"), 296.0, None, AL.mult)
+    vts(W("ind6h"), W("indh"), 296.0, None, AL.mult)
+    vts(W("indn"), W("cg"), G_, -4096.0, AL.is_equal, AL.mult)
+    vts(W("indnl"), W("indl"), -4096.0, None, AL.mult)
+    vts(W("indnh"), W("indh"), -4096.0, None, AL.mult)
+    vms(W("oneb"), 1.0)
+    vms(W("onef"), 1.0)
+    vms(W("c0"), CB)
+    vms(X("tab", 4096, TW), 0.0, 16)
+    vms(X("bits", 4096, TW), 0.0, 16)
+    iota(W("cg8"), [[1, 8]], 0, 0, 8, True)
+    vts(W("gk"), W("cg8"), G_, 16.0, AL.is_equal, AL.mult)
+    iota(W("tie"), [[0, 8], [1, 16]], 0, 0, 128, True)
+    iota(W("rsc"), [[0, 8], [1, 16]], 0, 0, 128, True)
+    iota(W("rs0c"), [[0, 16], [1, 8]], 0, 0, 128, True)
+    for a, b in (("rs", "rsc"), ("rs0", "rs0c")):
+        vts(W(b), W(b), 0.0, BIG - 1, AL.is_equal, AL.mult)
+        vts(W(a), W(b), -BIG, None, AL.add)
+    vts(W("dm"), W("cr"), I_, BIG + 8192, AL.is_gt, AL.mult, 272)
+    vts(W("dm"), W("dm"), -BIG, None, AL.add, None, 272)
+    vcp(W("thf"), W("thi"))
+    vts(W("nbw"), W("nbi"), 2.0, 1.0, AL.mult, AL.add, 2048)
+    for t in range(RO):
+        if t < 2:
+            vms(X("xa%d" % t, 1408, 1536), -1.0)
+        vcp(W("va%d" % t), X("sti", 8 * t, 8 * t + 8))
+        vcp(W("vb%d" % t), X("stin", 8 * t, 8 * t + 8))
+        vts(X("aw%d" % t, 0, 8), X("sti", 8 * t, 8 * t + 8), 2.0, 1.0, AL.mult, AL.add)
+    cbcol = X("c0", 0, 1)
+
+    def lessened(c):
+        vts(X("e1", c * 512, c * 512 + 512), X("tab", c * 512, c * 512 + 512), 0.5, 0.75, AL.add, AL.mult, 512)
+
+    def prep(t):
+        xa, xb = X("xa%d" % t, 0, 128), X("xb%d" % t, 0, 128)
+        va, vb = "va%d" % t, "vb%d" % t
+        for o, w, l, s in ((W("na"), "nbw", va, "mlo"), (W("nb2"), "nbw", vb, "mhi"), (W("xma"), "win2", va, "mlo"), (W("xmb"), "win2", vb, "mhi")):
+            act(o, IX(w, 0, 2048, l, 0, 8), AF.Copy, 128, 1.6, scale=W(s))
+        act(xa, IX("win2", 0, 2048, va, 0, 8), AF.Copy, 128, 1.6)
+        act(xb, IX("win2", 0, 2048, vb, 0, 8), AF.Copy, 128, 1.6)
+        nm = W("nm%d" % t)
+        vtt(nm, W("na"), W("nb2"), AL.add)
+        vtt(W("xm"), W("xma"), W("xmb"), AL.add)
+        act(W("cm"), W("xm"), AF.Identity, scale=296.0, bias=cbcol)
+        vtt(W("tp"), nm, W("xm"), AL.mult)
+        vtt(W("zpi"), W("tp"), W("cm"), AL.add)
+        vts(W("hpi"), W("zpi"), 4, 4095, AL.arith_shift_right, AL.bitwise_and)
+        vcp(W("h0%d" % t), W("hpi"))
+        for o, l in (("qm", "qmix"), ("qb", "qpar")):
+            for c in range(4):
+                act(X("%s%d" % (o, t), c * 512, c * 512 + 512), IX("qw%d" % t, 0, 256, l, c * 32, c * 32 + 32), AF.Copy, 512, 1.5)
+        vtt(W("pnp%d" % t), nm, W("xm"), AL.is_equal)
+        un = W("unp%d" % t)
+        act(un, W("pnp%d" % t), AF.Identity, scale=-1.0, bias=1.0)
+        d = X("pb7", 0, 128)
+        for x, xx, m in (("a", xa, "indnl"), ("b", xb, "indnh")):
+            mm([(d, W("idf"), xx, True, False), (d, W(m), un, False, True)], 640)
+            act(W("rp%s%d" % (x, t)), d, AF.Relu)
+
+    def records(x, hl, qx):
+        for c in SCHUNKS + tuple(c for c in range(4) if c not in SCHUNKS):
+            q = X(qx, c * 512, c * 512 + 512)
+            i = IX("tab", 0, TW, hl, c * 32, c * 32 + 32)
+            if c in SCHUNKS:
+                o = X("pb6", 0, 512)
+                act(W("xs" + x), i, AF.Copy, 512, 1.5)
+                mm([(o, W("ibf"), W("xs" + x), True, False), (o, W("negib"), q, False, True)], 1024)
+            else:
+                o = X("dif" + x, c * 512, c * 512 + 512)
+                vtt(o, i, q, AL.subtract, 512, 1.5)
+            act(X("ad" + x, c * 512, c * 512 + 512), o, AF.Abs, 512)
+
+    def choose(x, key, rs, ls, nn):
+        ks, r = W("ks" + x), W("r" + x)
+        act(ks, key, AF.Copy)
+        vscan(r, W(rs), ks, -1.0, AL.max, AL.min)
+        vtt(W("mk" + x), IX("r" + x, 0, 128, ls, 0, 8), ks, AL.is_equal, 128, 1.6)
+        m1 = X("pb%d" % (4 + "ab".index(x)), 0, 128)
+        mm([(m1, W("mk" + x), W("ibf"), True, True)], 128)
+        vtt(W("w" + x), m1, nn, AL.mult, 128, 1)
+
+    def after(x, src, t, a, indB, rv, ind6):
+        i = "ab".index(x)
+        bb, w = X("pb%d" % (2 + i), 0, 128), W("w" + src)
+        mm([(bb, W("idf"), rv, True, False)], 512)
+        mm([(bb, W(indB), w, False, True)], 512)
+        vscan(W("sc" + x), X("dm", 0, 128), bb, 0.0, AL.add, AL.max)
+        last = X("sc" + x, 15, 128, 16)
+        if a < 4:
+            cc = X("pb%d" % (4 + i), 128, 256)
+            mm([(cc, X("c0", 0, 128, 1, (0, 1)), X("onef", 0, 128, 1, (0, 1)), True, False), (cc, W("id6"), rv, False, False),
+                (cc, W(ind6), w, False, True)], 1536)
+            vts(W("vl" + x), last, W("corrn"), 0.5, AL.subtract, AL.mult)
+        act(X("aw%d" % t, (a + 1) * 8, (a + 2) * 8) if x == "a" else X("bo%d" % t, a * 8, (a + 1) * 8), last, AF.Identity, bias=W("corrw"))
+        if x == "a" or a < 4:
+            act(X("x%s%d" % (x, t), (a + 1) * 128, (a + 2) * 128), bb, AF.Copy)
+
+    def keys(x, key, un):
+        n = key[1][0][0]
+        mm([(key, X("oneb", 0, 128, 1, (0, 1)), X("tie", 0, 128, 1, (0, 1)), True, False)], 128)
+        mm([((T[n][:, k:128:16], key[1]), X("ad" + x, k, 2048, 16), W("gk"), False, False) for k in range(16)], 1024)
+        mm([(key, un, W("penr"), False, True)], 128)
+
+    def first(t):
+        records("a", "h0%d" % t, "qm%d" % t)
+        key = X("pb0", 0, 128)
+        keys("a", key, W("unp%d" % t))
+        choose("a", key, "rs0", "ls0", W("nm%d" % t))
+        after("b", "a", t, 0, "indh", W("rpb%d" % t), "ind6h")
+        after("a", "a", t, 0, "indl", W("rpa%d" % t), "ind6l")
+
+    def step(x, t, a):
+        i = "ab".index(x)
+        pm, pd = "pb%d" % (2 + i), "pb%d" % (4 + i)
+        xh, v, nn = "x%s%d" % (x, t), "vl" + x, W("nn" + x)
+        vtt(W("t1" + x), IX("nbw", 0, 2048, v, 0, 8), X(xh, (a - 1) * 128, a * 128), AL.mult, 128, 1.6)
+        act(nn, IX("nbw", 0, 2048, v, 0, 8), AF.Copy, 128, 1.6)
+        vtt(W("zi" + x), W("t1" + x), X(pd, 128, 256), AL.add, 128, 1)
+        vts(W("hi" + x), W("zi" + x), 4, 4095, AL.arith_shift_right, AL.bitwise_and)
+        vcp(W("hl" + x), W("hi" + x))
+        records(x, "hl" + x, "qa" if x == "a" else "qb%d" % t)
+        n = min(a + 1, 4)
+        mm([(X(pd, m * 128, m * 128 + 128), W("idf"), nn, True, True) for m in range(n)], 512 * n)
+        vtt(X("pn" + x, 0, n * 128), X(xh, 0, n * 128), X(pd, 0, n * 128), AL.is_equal, n * 128, 1)
+        if a == 4:
+            d = X("pb7", 384, 512)
+            mm([(d, W("idf"), nn, True, True)], 512)
+            vtt(X("pn" + x, 512, 640), X(xh, 512, 640), d, AL.is_equal, 128, 1)
+        sg = X(pm, 128, 256)
+        mm([(sg, W("ibf"), X("pn" + x, m * 128, m * 128 + 128), m == 0, m == a) for m in range(a + 1)], 128 * (a + 1))
+        un = W("unb" + x)
+        act(un, sg, AF.Relu, scale=-1.0, bias=1.0)
+        rs = X(pm, 256, 384)
+        mm([(rs, W("idf"), X(xh, a * 128, a * 128 + 128), True, False), (rs, W("indn"), un, False, True)], 640)
+        rv = W("rv" + x)
+        act(rv, rs, AF.Relu)
+        key = X("pb%d" % i, 0, 128)
+        keys(x, key, un)
+        choose(x, key, "rs", "ls", nn)
+        after(x, x, t, a, "indf", rv, "ind6")
+        if x == "b" and a == 4:
+            s = add("G", lambda: sendb(t), [W("bo%d" % t)], [], 1.0)
+            add("R", None, [], [X("aw%d" % t, 48, 88)], 3.0, mdep=[s], sem="rb%d" % t, cnt=4)
+
+    def tolist(name, w):
+        vscan(X("lsc", 0, w), X("dm", 0, w), X("lr", 0, w), 0.0, AL.add, AL.max, w)
+        vts(X(name, 0, w // 16), X("lsc", 15, w, 16), W("corrw"), None, AL.add)
+
+    def late_constants():
+        def blk(i):
+            return i * 8
+
+        def bb(j):
+            return 0 if j == 0 else 48 + (j - 1) * 8
+        for name, f, tail in (("LP", lambda i, j: blk(i - 1), [(200, 8, bb(1)), (208, 8, 0), (216, 24, 48), (240, 32, 0)]),
+                              ("LV", lambda i, j: blk(i), [(200, 8, 0), (208, 32, 48), (240, 32, 8)]),
+                              ("LN", lambda i, j: bb(j - 1), [(200, 8, 8), (208, 32, 56), (240, 32, 16)]),
+                              ("LB", lambda i, j: bb(j), [(200, 8, 0)])):
+            iota(X("lr", 0, 200, 25), [[1, 8]], 0, 0, 8, True)
+            for e in range(1, 25):
+                ix = 25 - e
+                iota(X("lr", e, 200, 25), [[1, 8]], f(ix // 5 + 1, ix % 5 + 1), 0, 8, True)
+            for c, n, b in tail:
+                iota(X("lr", c, c + n), [[1, n]], b, 0, n, True)
+            tolist(name, 208 if name == "LB" else 272)
+        for k in range(10):
+            iota(X("lr", k * 8, k * 8 + 8), [[1, 8]], 8 if 1 <= k <= 4 else 0, 0, 8, True)
+            iota(X("thr", k * 8, k * 8 + 8), [[0, 8]], k if 1 <= k <= 4 else 5 * (k - 4) if 5 <= k <= 8 else 1, 0, 8, True)
+        tolist("LM", 80)
+        iota(X("pack", 0, 200, 25), [[0, 8]], 0, 0, 8)
+        for e in range(1, 25):
+            ix = 25 - e
+            iota(X("pack", e, 200, 25), [[0, 8]], (ix * 8 + ix % 5) << 12, 0, 8)
+        f, fI, fJ, fT, fU, fV = [W(n) for n in ("ft", "fI", "fJ", "fT", "fU", "fV")]
+        iota(f, [[1, 32]], 0, 0, 32, True)
+        vts(W("fii"), f, 0.2, -0.4, AL.mult, AL.add)
+        vcp(fI, W("fii"))
+        vts(fJ, fI, -4.0, None, AL.mult)
+        vtt(fJ, fJ, f, AL.add)
+        vts(fT, fJ, I_, -1.0, AL.subtract, AL.is_ge)
+        vts(fU, fJ, I_, -4.0, AL.subtract, AL.add)
+        vtt(fU, fU, fT, AL.mult)
+        vts(fU, fU, 11.0, None, AL.add)
+        vts(fT, fI, I_, -1.0, AL.subtract, AL.is_ge)
+        vts(fV, fU, I_, -1.0, AL.subtract, AL.mult)
+        vtt(fV, fV, fT, AL.mult)
+        vtt(fV, fV, fU, AL.add)
+        vts(W("tw"), fV, 128.0, None, AL.mult)
+        vms(X("tw", 0, 1), 1408.0)
+        vms(W("sel"), 1.0, 2048)
+        keep(W("sel"), [[0, 16], [1, 128]], -1, 2048)
+        keep(W("sel"), [[1, 16], [0, 8], [-1, 16]], 0, 2048)
+        vts(W("m6"), I_, 6.0, None, AL.is_ge)
+        vts(W("p0"), W("m6"), -6.0, None, AL.mult)
+        vtt(W("p0"), W("p0"), I_, AL.add)
+        vcp(W("wi"), W("p0"))
+        vts(W("b0"), W("wi"), 1, None, AL.bitwise_and)
+        vts(W("b1"), W("wi"), 1, 1, AL.arith_shift_right, AL.bitwise_and)
+        vts(W("b2"), W("wi"), 2, 1, AL.arith_shift_right, AL.bitwise_and)
+        vts(W("p0"), W("b0"), -0.5, 1.0, AL.mult, AL.add)
+        vts(W("p1"), W("b1"), -0.75, 1.0, AL.mult, AL.add)
+        vts(W("p2"), W("b2"), -0.9375, 1.0, AL.mult, AL.add)
+        vtt(W("p0"), W("p0"), W("p1"), AL.mult)
+        vtt(W("pw"), W("p0"), W("p2"), AL.mult)
+        vts(W("m12"), I_, 12.0, None, AL.is_lt)
+        iota(W("eg"), [[1, 8], [0, 64]], 0, 0, 512, True)
+        iota(W("ex"), [[0, 8], [1, 64]], 0, 0, 512, True)
+        vts(W("ei"), W("ex"), W("pw"), -0.5 + 2.0 ** -8, AL.mult, AL.add, 512)
+        vts(W("ei"), W("ei"), 1, None, AL.bitwise_and, None, 512)
+        vts(W("ea"), W("ei"), 2.0, -1.0, AL.mult, AL.add, 512)
+        vts(W("eb"), W("eg"), G_, None, AL.is_equal, None, 512)
+        vtt(W("ea"), W("ea"), W("eb"), AL.mult, 512)
+        vts(W("p1"), W("m6"), -1.0, 1.0, AL.mult, AL.add)
+        vtt(W("p2"), W("m6"), W("m12"), AL.mult)
+        vts(W("ehi"), W("ea"), W("p1"), None, AL.mult, None, 512)
+        vts(W("elo"), W("ea"), W("p2"), None, AL.mult, None, 512)
+        for o, e in ((X("pb7", 0, 128, 1, (0, 64)), "ehi"), (X("pb7", 0, 128, 1, (64, 128)), "elo")):
+            mm([(o, X(e, q * 64, q * 64 + 64), W("ibf"), q == 0, q == 7) for q in range(8)], 1024)
+        act(W("lt"), X("pb7", 0, 128), AF.Copy)
+        vms(W("rh"), 1.0, 2048)
+        vms(W("rl"), 1.0, 2048)
+        keep(W("rh"), [[1, 64], [0, 64]], -1, 4096)
+        keep(W("rl"), [[0, 64], [1, 64]], -1, 4096, 64)
+        for c in range(8):
+            mm([(X("pb7", 0, 512), W("lt"), X(r, c * 512, c * 512 + 512), r == "rh", r == "rl") for r in ("rh", "rl")], 1024)
+            act(X("bits", c * 512, c * 512 + 512), X("pb7", 0, 512), AF.Copy, 512)
+        iota(W("wc"), [[1, 240]], -112, 0, 240, True)
+        vts(W("wi"), W("pi"), 2, None, AL.arith_shift_right)
+        vcp(W("wh"), W("wi"))
+        vts(W("wi2"), W("pi"), 3, None, AL.bitwise_and)
+        for b in range(4):
+            vts(X("wbm", b, b + 1), W("wi2"), float(b), None, AL.is_equal)
+            vts(X("wid", b * 240, b * 240 + 240), W("wc"), W("wh"), X("wbm", b, b + 1), AL.is_equal, AL.mult, 240)
+        vms(W("la"), -256.0, 1024)
+        keep(W("la"), [[1, 16], [16, 8], [0, 16]], -1, 2048)
+
+    def join(t):
+        aw = "aw%d" % t
+        vts(W("nlb"), X(aw, 48, 88), 0.5, -0.5, AL.mult, AL.add)
+        act(W("bj"), IX(aw, 0, 88, "LB", 0, 13), AF.Copy, 208, 1.6)
+        act(W("narr"), IX(aw, 0, 88, "LN", 0, 17), AF.Copy, 272, 1.6)
+        act(W("varr"), IX(aw, 0, 88, "LV", 0, 17), AF.Identity, 272, 1.6, scale=296.0, bias=cbcol)
+        vtt(W("eq"), IX(aw, 0, 88, "LV", 0, 13), W("bj"), AL.is_equal, 208, 1.6)
+        act(W("neq"), W("eq"), AF.Identity, 208, scale=-1.0, bias=1.0)
+        vtt(W("tj"), IX(aw, 0, 88, "LP", 0, 17), W("narr"), AL.mult, 272, 1.6)
+        vtt(W("hji"), W("tj"), W("varr"), AL.add, 272)
+        vts(W("hji"), W("hji"), 4, 4095, AL.arith_shift_right, AL.bitwise_and, 272)
+        vtt(X("hp", 0, 200), X("hji", 0, 200), X("pack", 0, 200), AL.add, 200)
+        vtt(X("ek", 0, 200), X("eq", 0, 200), X("hp", 0, 200), AL.mult, 200)
+        vscan(X("scj", 0, 200), X("neq", 0, 200), X("ek", 0, 200), 0.0, AL.mult, AL.add, 200)
+        vcp(W("j8"), X("scj", 24, 200, 25))
+        vts(X("win24", 0, 8), W("j8"), 15, None, AL.arith_shift_right)
+        vts(X("win24", 8, 16), W("j8"), 12, 7, AL.arith_shift_right, AL.bitwise_and)
+        vts(W("hj"), W("j8"), 4095, None, AL.bitwise_and)
+        vts(X("hr", 0, 72), X("hji", 200, 272), -4096.0, None, AL.add)
+        vts(X("hr", 72, 80), W("hj"), -4096.0, None, AL.add)
+        vcp(W("fl"), X("win24", 0, 8))
+        vtt(W("mk"), IX("win24", 0, 16, "LM", 0, 5), W("thr"), AL.is_ge, 80, 1.6)
+        vtt(W("off"), W("hr"), W("mk"), AL.mult, 80)
+        vts(W("off80"), W("off"), 4096.0, None, AL.add)
+
+    def lessen(t):
+        act(X("xr", 0, 640), IX("tab", 0, TW, "off80", 0, 40), AF.Copy, 640, 1.5)
+        vcp(X("xr", 640, 1280), IX("tab", 0, TW, "off80", 40, 80), 640, 1.5)
+        tot, cnt = X("pb5", 0, 128), X("pb5", 128, 136)
+        mm([(tot, W("ibf"), X("xr", k * 128, k * 128 + 128), k == 0, k == 9) for k in range(10)], 1280)
+        vts(W("ge"), tot, W("thf"), None, AL.is_ge)
+        mm([(cnt, W("ge"), W("gk"), True, True)], 64)
+        vts(W("nhc"), cnt, 139.0, -5.0, AL.subtract, AL.min)
+        act(X("hb", 0, 640), IX("bits", 0, TW, "off80", 0, 40), AF.Copy, 640, 1.5)
+        vcp(X("hb", 640, 1280), IX("bits", 0, TW, "off80", 40, 80), 640, 1.5)
+        rot = [0]
+        bk = ("pb2", "pb3", "pb4", "pb7", "pb0", "pb1", "pb6")
+
+        def chunk(w):
+            rot[0] += 1
+            return X(bk[rot[0] % len(bk)], 0, w)
+
+        def onehot(o, e, q, h, b):
+            c = chunk(320)
+            n = c[1][0][0]
+            mm([(X(n, j * 64, j * 64 + 64), X("hb", (h * 5 + j) * 128, (h * 5 + j) * 128 + 128), X(e, q * 64, q * 64 + 64), True, True)
+                for j in range(5)], 320)
+            r = X(o, (q * 10 + h * 5) * 64, (q * 10 + h * 5 + 5) * 64)
+            if rot[0] % 2:
+                act(r, c, AF.Relu, 320, bias=b)
+            else:
+                vts(r, c, b, 0.0, AL.add, AL.max, 320)
+        for h in range(2):
+            for q in range(8):
+                onehot("ohh", "ehi", q, h, -5.0)
+        for q in range(8):
+            for h in range(2):
+                onehot("ohl", "elo", q, h, X("nhc", q, q + 1))
+            mm([(X("pb5", q * 64, q * 64 + 64, 1, (0, 64)), X("ohh", (q * 10 + k) * 64, (q * 10 + k) * 64 + 64),
+                 X("ohl", (q * 10 + k) * 64, (q * 10 + k) * 64 + 64), k == 0, k == 9) for k in range(10)], 640)
+        vts(X("flg", 0, 512, 1, (0, 64)), X("pb5", 0, 512, 1, (0, 64)), 0.0, None, AL.is_gt, None, 512)
+        for b in range(4):
+            o = X("pb2", b * 64, b * 64 + 64)
+            mm([(o, X("wid", b * 240 + 112 - 16 * q, b * 240 + 240 - 16 * q, 1, (0, 64)), X("flg", q * 64, q * 64 + 64, 1, (0, 64)), q == 0, q == 7)
+                for q in range(8)], 512)
+        act(W("fx"), X("pb2", 0, 256), AF.Copy, 256)
+        for k in range(8):
+            c = chunk(512)
+            l = []
+            for h in range(2):
+                o = X(c[1][0][0], h * 256, h * 256 + 256)
+                l += [(o, W("ibf"), X("tab", k * 512 + h * 256, k * 512 + h * 256 + 256), True, False),
+                      (o, X("la", (2 * k + h) * 128, (2 * k + h) * 128 + 128), W("fx"), False, True)]
+            mm(l, 1024)
+            vtt(X("tab", k * 512, k * 512 + 512), X("e1", k * 512, k * 512 + 512), c, AL.max, 512, 1)
+            if t == RO - 1 and k % 2:
+                dma((T.ye[:, (k - 1) * 512:(k + 1) * 512], []), X("tab", (k - 1) * 512, (k + 1) * 512))
+
+    def rings(t):
+        xa = "xa%d" % t
+        act(X(xa, 768, 1408), IX("win2", 0, 2048, "nlb", 0, 40), AF.Copy, 640, 1.6)
+        vtt(W("of"), IX("tw", 0, 32, "fl", 0, 8), W("cf"), AL.add, 128, 1.6)
+        vcp(W("ofu"), W("of"))
+        for c in range(4):
+            act(X("gy", c * 512, c * 512 + 512), IX(xa, 0, 1536, "ofu", c * 32, c * 32 + 32), AF.Identity, 512, 1.6, scale=0.5, bias=-0.5)
+        y = X("pb7", 0, 128)
+        for c in range(4):
+            mm([(y, X("sel", m * 128, m * 128 + 128), X("gy", m, 2048, 16), m == 0, m == 15) for m in range(c * 4, c * 4 + 4)], 2048)
+        act(W("yo"), y, AF.Copy)
+        dma((T.yr[:, t * 128:t * 128 + 128], []), W("yo"))
+
+    act(W("qa"), IX("qw0", 0, 256, "qown", 0, 128), AF.Copy, 2048, 1.5)
+    prep(0)
+    for t in range(RO):
+        first(t)
+        for a in range(1, 5):
+            step("b", t, a)
+            step("a", t, a)
+            if a == 1:
+                for c in range(8):
+                    lessened(c)
+                if t == 0:
+                    late_constants()
+            if a == 2 and t + 1 < RO:
+                prep(t + 1)
+        join(t)
+        lessen(t)
+        rings(t)
+
+    n = len(ops)
+    pred = [[] for _ in range(n)]
+    seen, banks = {}, {}
+    for i, o in enumerate(ops):
+        e = o["e"]
+        d = {}
+        for rw, regs in ((0, o["r"]), (1, o["w"])):
+            for nm, lo, hi in regs:
+                for j, l2, h2, w2 in seen.get(nm, ()):
+                    if l2 < hi and lo < h2 and (rw or w2) and j != i:
+                        d[j] = d.get(j, False) or ops[j]["e"] != e or e != "P"
+        for nm in set(x[0] for x in o["r"] + o["w"] if x[0][:2] == "pb"):
+            p = banks.get(nm)
+            if p is not None:
+                d[p] = d.get(p, False) or ops[p]["e"] != e
+            banks[nm] = i
+        for rw, regs in ((0, o["r"]), (1, o["w"])):
+            for nm, lo, hi in regs:
+                l = seen.setdefault(nm, [])
+                if rw:
+                    l[:] = [x for x in l if not (lo <= x[1] and x[2] <= hi)]
+                l.append((i, lo, hi, rw))
+        pred[i] = sorted(d.items())
+
+    order = CACHE.get("order")
+    if order is None:
+        succ = [[] for _ in range(n)]
+        npd = [0] * n
+        for i, o in enumerate(ops):
+            for j in [p[0] for p in pred[i]] + list(o.get("mdep", ())):
+                succ[j].append(i)
+                npd[i] += 1
+        pr = [0.0] * n
+        for i in range(n - 1, -1, -1):
+            pr[i] = ops[i]["c"] + ops[i].get("lat", 0) + max([pr[j] + .08 for j in succ[i]] or [0])
+        ready = [0.0] * n
+        cand = {e: [] for e in ("V", "S", "P", "G", "Y", "R")}
+        free = {e: 0.0 for e in cand}
+        for i in range(n):
+            if npd[i] == 0:
+                cand[ops[i]["e"]].append(i)
+        order = []
+        while len(order) < n:
+            s, e = min((min(ready[i] for i in l) if e == "R" else max(free[e], min(ready[i] for i in l)), e) for e, l in cand.items() if l)
+            i = max((x for x in cand[e] if ready[x] <= s), key=lambda x: (pr[x], -x))
+            cand[e].remove(i)
+            order.append(i)
+            free[e] = s + ops[i]["c"]
+            fin = s + ops[i]["c"] + ops[i].get("lat", 0)
+            for j in succ[i]:
+                npd[j] -= 1
+                ready[j] = max(ready[j], fin + .08)
+                if npd[j] == 0:
+                    cand[ops[j]["e"]].append(j)
+        CACHE["order"] = order
+
+    qs = {"V": g.vector, "S": g.scalar, "P": g.tensor, "G": g, "Y": g.sync}
+    known = {e: {} for e in qs}
+    cnt = {e: 0 for e in "VSPG"}
+    done = {}
+    for i in order:
+        o = ops[i]
+        e = o["e"]
+        if e == "R":
+            done[i] = (o["sem"], o["cnt"], {o["sem"]: o["cnt"]})
+            continue
+        kn = known[e]
+        for j, need in sorted(pred[i], reverse=True):
+            if not need:
+                continue
+            sm, c, snap = done[j]
+            if c > kn.get(sm, 0):
+                qs[e].wait_ge(T.sem[sm], c)
+                for a, b in snap.items():
+                    if b > kn.get(a, 0):
+                        kn[a] = b
+        ins = o["fn"]()
+        if e == "Y":
+            ins[0].then_inc(T.sem[o["sem"]], 16)
+            sm, c = o["sem"], 16
+        else:
+            sm = "s" + e
+            for x in ins:
+                x.then_inc(T.sem[sm], 1)
+            cnt[e] += len(ins)
+            c = cnt[e]
+        snap = dict(kn)
+        snap[sm] = c
+        done[i] = (sm, c, snap)
+    for e in "VSPG":
+        g.wait_ge(T.sem["s" + e], cnt[e])
+    for i in range(dn[0]):
+        g.wait_ge(T.sem["d%d" % i], 16)
+    for t in range(RO):
+        g.wait_ge(T.sem["rq%d" % t], NE)
+        g.wait_ge(T.sem["rs%d" % t], NE)
+        g.wait_ge(T.sem["rb%d" % t], 4)
+    g.wait_ge(T.sem.ls, lsn)
+
+
+def rank_program(g, core, T, topo):
+    if T.rank_of(core) is not None:
+        program(g, core, T, topo)

@@ -5,10 +5,10 @@ from concourse.mybir import dt, AluOpType, AxisListType, ActivationFunctionType
 AL = AluOpType
 AF = ActivationFunctionType
 RO, ST, N = 3, 5, 8
-TW = 4112
-F, B, I32, U16 = "float32", "bfloat16", "int32", "uint16"
-PHYS = {F: "vf", B: "vb", I32: "vi", U16: "vu"}
-SIZE = {F: 0, B: 0, I32: 0, U16: 0}
+TW = 4144
+F, B, H, I32, U16 = "float32", "bfloat16", "float16", "int32", "uint16"
+PHYS = {F: "vf", B: "vb", H: "vh", I32: "vi", U16: "vu"}
+SIZE = {F: 0, B: 0, H: 0, I32: 0, U16: 0}
 VB = {}
 
 
@@ -18,71 +18,64 @@ def _sb(dtype, **kw):
         SIZE[dtype] += (n + 31) // 32 * 32
 
 
-def _over(k, base, n):
-    VB[k] = (VB[base][0], VB[base][1], n)
-
-
-_sb(B, tab=TW, bits=TW, qa=2048, difa=2048, difb=2048, ada=2048, adb=2048, ibf=128, gk=8, penr=128, xsa=512, xsb=512,
-    tie=128, oneb=128, indn=128, indnl=128, indnh=128, xr=1280, hb=1280, ehi=512, elo=512,
-    ge=128, ohl=5120, flg=512, fx=256, la=2048, wid=960, negib=128, lt=128, rl=4096)
-_sb(F, nbw=2048, win2=2048, idf=128, indf=128, indl=128, indh=128, ind6=128, ind6l=128, ind6h=128, id6=128,
-    c0=128, onef=128, rs=128, rs0=128, dm=272, corrn=1, corrw=1, mlo=1, mhi=1, mhi8=1, mhi128=1, pf=1, gf=1, fi=1, cf=128, cg=128, cr=272,
-    cg8=8, rsc=128, rs0c=128, sel=2048, thf=1, nhc=8,
-    pw=1, p0=1, p1=1, p2=1, m6=1, m12=1, wh=1, wbm=4, lr=272, lsc=272, thr=80,
-    ft=32, fI=32, fJ=32, fT=32, fU=32, fV=32, tw=32, gy=2048, yo=128, narr=272, varr=272, bj=208, tj=272, eq=208, neq=208,
-    hp=208, ek=208, scj=208, hr=80, mk=80, off=80, of=128, na=128, nb2=128, xma=128, xmb=128, xm=128, cm=128, tp=128)
-_sb(F, eg=512, ex=512, ea=512, eb=512, wc=240)
-_sb(I32, e1=4096, sti=24, pi=1, gi=1, ii=1, b0=1, b1=1, b2=1, ei=512, wi=1, wi2=1, fii=32, pack=208, hji=272,
-    j8=8, hj=8, win24=32, c128=128, c8=8, stin=24, zpi=128, hpi=128, thi=1)
-_over("nbi", "e1", 2048)
-_over("ohh", "difa", 5120)
-_over("rh", "ohl", 4096)
-_sb(U16, qown=128, qpar=128, qmix=128, LP=18, LV=18, LN=18, LB=14, LM=6, off80=80, fl=8, ofu=128, nlb=40, ls=8, ls0=8)
+_sb(B, tab=TW, qa=2048, qm=2048, qb0=2048, qb1=2048, qw=512, cf=128, cg=128, cr=128, c8=128, ibf=128, negib=128, bigi=128, ind=128, indl=128,
+    indh=128, ind6=128, ind6l=128, ind6h=128, dlo=128, dhi=128, gk=8, ngk=8, oneb=128, crow=128, selc=2048, nsb=2048, dw=1024, tg=1024,
+    i8k=128, fl2=1280, xr=1280, nd1=1280, nd=1280, lr=1088, ge=128)
+_sb(H, i594=128, da=128, db=128, rep=80, gy=2048)
+_sb(F, win=2048, xa=1536, pf=1, gf=1, fi=1, mlo=1, mhi=1, ncorr=1, c1=1, i7=1, de=1, do=1, thf=1, rs=128, rs0=128, dm=128,
+    s8a=8, s8b=8, src8=8, tgt8=8, l6=8, pack=200, thr=80, fI=64, fL=64, t1w=64, t2w=64, t3w=64, tw=64,
+    pm=128, cm=128, tp=128, aw=104, narr=288, varr=288, bj=208, tj=288, hp=200, eq=208, neq=208, ek=200, scj=200,
+    t8=8, aa=80, bb=80, hm=80, u8=8, of=128, yo=128)
+_sb(I32, nbi=2048, sti=64, stin0=64, stin1=64, stin2=64, pi=1, gi=1, thi=1, zpi=128, hpi=128, hji=288, zj=288, z8=8, w16=16, c8i=8)
+_sb(U16, LL=68, LH=6, LM=6, off=80, offs=80, fl=8, ofu=128)
 for _x in "ab":
-    _sb(F, **{"t1" + _x: 128, "nn" + _x: 128, "rv" + _x: 128, "r" + _x: 128, "ks" + _x: 128, "w" + _x: 128, "sc" + _x: 128})
+    _sb(F, **{"t1" + _x: 128, "r" + _x: 128, "rr" + _x: 128, "sc" + _x: 128})
     _sb(I32, **{"zi" + _x: 128, "hi" + _x: 128})
-    _sb(U16, **{"vl" + _x: 8, "hl" + _x: 128})
-    _sb(B, **{"pn" + _x: 640, "unb" + _x: 128, "mk" + _x: 128})
+    _sb(U16, **{"hl" + _x: 128})
+    _sb(B, **{"pn" + _x: 640, "mk" + _x: 128, "dif" + _x: 2048, "ad" + _x: 2048, "xs" + _x: 2048})
+    _sb(H, **{"dn" + _x: 128, "w" + _x: 128})
 for _t in range(RO):
-    if _t < 2:
-        _sb(B, **{"qm%d" % _t: 2048, "qb%d" % _t: 2048})
-        _sb(F, **{"xa%d" % _t: 1536})
-    _sb(B, **{"qw%d" % _t: 256, "unp%d" % _t: 128, "pnp%d" % _t: 128})
-    _sb(F, **{"xb%d" % _t: 640, "aw%d" % _t: 88, "bo%d" % _t: 40, "nm%d" % _t: 128, "rpa%d" % _t: 128, "rpb%d" % _t: 128})
-    _sb(U16, **{"h0%d" % _t: 128, "va%d" % _t: 8, "vb%d" % _t: 8})
-_over("qm2", "qm0", 2048)
-_over("qb2", "qb0", 2048)
-_over("xa2", "xa0", 1536)
+    _sb(B, **{"pn0%d" % _t: 128})
+    _sb(H, **{"xa%d" % _t: 640, "xb%d" % _t: 640, "dn0%d" % _t: 128})
+    _sb(F, **{"pa%d" % _t: 512, "pb_%d" % _t: 512})
+    _sb(U16, **{"h0%d" % _t: 128, "la%d" % _t: 104, "lb%d" % _t: 48})
 SCRATCH = {PHYS[d]: ("sbuf", [128, SIZE[d]], d) for d in PHYS}
 for _i in range(8):
     SCRATCH["pb%d" % _i] = ("psum", [128, 512], F)
     VB["pb%d" % _i] = ("pb%d" % _i, 0, 512)
-NDMA = 24
+NDMA = 12
 SEMAPHORES = ["sV", "sS", "sP", "sG", "ls"] + ["d%d" % i for i in range(NDMA)] + ["rq%d" % i for i in range(RO)] + \
     ["rs%d" % i for i in range(RO)] + ["rb%d" % i for i in range(RO)]
 CACHE = {}
 BIG = 16777216.0
+TOP = 100000.0
 CB = -296.0 - 8388608.0
-SCHUNKS = (3,)
+NONE = 63 * 16384.0 + 8192.0
+OPT = dict(nv=768, nc=768, nv0=896, nc0=768, nvl=1024, ncl=768, gat=1.56, lam=.08, xv=640)
 
 
 def program(g, core, T, topo):
     rank = T.rank_of(core)
     ops = []
     dn = [0]
+    GAT = OPT["gat"]
 
     def X(n, a, b, s=1, p=None):
         ph, o, _ = VB[n]
         ps = slice(None) if p is None else slice(p[0], p[1])
         cs = slice(o + a, o + b, s) if s > 1 else slice(o + a, o + b)
-        return (T[ph][ps, cs], [(ph, o + a, o + b)])
+        return (T[ph][ps, cs], [(ph, o + a, o + b, s)], len(range(a, b, s)))
 
     def W(n):
         return X(n, 0, VB[n][2])
 
+    def REV(n):
+        ph, o, w = VB[n]
+        return (T[ph][:, slice(o + w - 1, o - 1, -1)], [(ph, o, o + w, 1)], w)
+
     def IX(n, a, b, o, c, d):
         w, l = X(n, a, b), X(o, c, d)
-        return (w[0].indirect(l[0]), w[1] + l[1])
+        return (w[0].indirect(l[0]), w[1] + l[1], 16 * (d - c), "ix")
 
     def add(e, fn, r, w, c, **kw):
         ops.append(dict(e=e, fn=fn, r=[y for x in r for y in x[1]], w=[y for x in w for y in x[1]], c=c, **kw))
@@ -91,28 +84,38 @@ def program(g, core, T, topo):
     def sc(s):
         return (s[0], [s]) if isinstance(s, tuple) else (s, [])
 
-    def vts(o, a, s1, s2, o0, o1=None, n=128, k=1.0):
+    def cost(o, ins, k=None):
+        if len(o) > 3:
+            k = 3.8
+        elif len(ins) and len(ins[0]) > 3:
+            k = GAT
+        elif k is None:
+            k = .5 if all(x[1][0][0] in ("vb", "vh", "vu") for x in [o] + ins) else 1.0
+        return max(64, o[2] * k) * .83e-3
+
+    def vts(o, a, s1, s2, o0, o1=None):
         (v1, r1), (v2, r2) = sc(s1), sc(s2)
         if o1 is None:
             f = lambda: [g.vector.tensor_scalar(out=o[0], in0=a[0], scalar1=v1, scalar2=None, op0=o0)]
         else:
             f = lambda: [g.vector.tensor_scalar(out=o[0], in0=a[0], scalar1=v1, scalar2=v2, op0=o0, op1=o1)]
-        add("V", f, [a] + r1 + r2, [o], .05 + max(64, n * k) * .83e-3)
+        add("V", f, [a] + r1 + r2, [o], .05 + cost(o, [a]))
 
-    def vtt(o, a, b, op, n=128, k=2.0):
-        add("V", lambda: [g.vector.tensor_tensor(out=o[0], in0=a[0], in1=b[0], op=op)], [a, b], [o], .05 + max(64, n * k) * .83e-3)
+    def vtt(o, a, b, op):
+        k = 1.0 if "pb" in (a[1][0][0][:2], b[1][0][0][:2]) else 2.0
+        add("V", lambda: [g.vector.tensor_tensor(out=o[0], in0=a[0], in1=b[0], op=op)], [a, b], [o], .05 + cost(o, [a, b], k))
 
-    def vcp(o, a, n=128, k=1.0):
-        add("V", lambda: [g.vector.tensor_copy(out=o[0], in_=a[0])], [a], [o], .05 + max(64, n * k) * .83e-3)
+    def vcp(o, a):
+        add("V", lambda: [g.vector.tensor_copy(out=o[0], in_=a[0])], [a], [o], .05 + cost(o, [a]))
 
-    def vms(o, v, n=128):
-        add("V", lambda: [g.vector.memset(o[0], v)], [], [o], .05 + max(64, n) * .83e-3)
+    def vms(o, v):
+        add("V", lambda: [g.vector.memset(o[0], v)], [], [o], .05 + cost(o, []))
 
-    def vscan(o, d0, d1, ini, o0, o1, n=128):
+    def vscan(o, d0, d1, ini, o0, o1):
         add("V", lambda: [g.vector.tensor_tensor_scan(out=o[0], data0=d0[0], data1=d1[0], initial=ini, op0=o0, op1=o1)],
-            [d0, d1], [o], .05 + max(64, n) * .83e-3)
+            [d0, d1], [o], .05 + cost(o, [d0, d1]))
 
-    def act(o, a, fn, n=128, k=1.0, bias=None, scale=None):
+    def act(o, a, fn, bias=None, scale=None):
         kw, r = {}, []
         if bias is not None:
             kw["bias"], rr = sc(bias)
@@ -120,19 +123,21 @@ def program(g, core, T, topo):
         if scale is not None:
             kw["scale"], rr = sc(scale)
             r = r + rr
-        add("S", lambda: [g.scalar.activation(out=o[0], in_=a[0], func=fn, **kw)], [a] + r, [o], .065 + max(64, n * k) * .83e-3)
+        add("S", lambda: [g.scalar.activation(out=o[0], in_=a[0], func=fn, **kw)], [a] + r, [o], .065 + cost(o, [a], 1.0))
 
-    def mm(l, c):
+    def mm(l):
+        c = sum(max(min(64, a[2]), b[2]) for o, a, b, s, p in l)
         add("P", lambda: [g.tensor.matmul(out=o[0], lhsT=a[0], rhs=b[0], start=s, stop=p) for o, a, b, s, p in l],
-            [x for m in l for x in m[1:3]], [m[0] for m in l], c * .45e-3 + .03)
+            [x for m in l for x in m[1:3]], [m[0] for m in l], c * .42e-3)
 
-    def iota(o, pat, base, cm, n=64, small=False):
-        kw = {"allow_small_or_imprecise_dtypes": True} if small else {}
-        add("G", lambda: [g.iota(o[0], pattern=pat, base=base, channel_multiplier=cm, **kw)], [], [o], .13 + 2 * n * .83e-3)
+    def iota(o, pat, base, cm=0):
+        kw = {} if o[1][0][0] == "vi" else {"allow_small_or_imprecise_dtypes": True}
+        add("G", lambda: [g.iota(o[0], pattern=pat, base=base, channel_multiplier=cm, **kw)], [], [o], .13 + 2 * o[2] * .83e-3)
 
-    def keep(o, pat, cm, n, base=0):
-        add("G", lambda: [g.affine_select(out=o[0], in_=o[0], pattern=pat, compare_op=AL.is_equal, fill=0.0, base=base, channel_multiplier=cm)],
-            [o], [o], .17 + 2 * n * .83e-3)
+    def keep(o, a, pat, cm, op=None, fill=0.0):
+        op = AL.is_equal if op is None else op
+        add("G", lambda: [g.affine_select(out=o[0], in_=a[0], pattern=pat, compare_op=op, fill=fill, base=0, channel_multiplier=cm)],
+            [a], [o], .17 + 2 * o[2] * .83e-3)
 
     def dma(o, a, lat=2.5):
         i = dn[0]
@@ -140,426 +145,378 @@ def program(g, core, T, topo):
         add("Y", lambda: [g.sync.dma_start(out=o[0], in_=a[0])], [a], [o], .1, lat=lat, sem="d%d" % i)
 
     def ext(n):
-        return (T[n][:], [])
+        return (T[n][:], [], 0)
 
     outq = [T.cores[(rank + 1 + t % (N - 1)) % N] for t in range(RO)]
     back = [T.cores[(rank - 1 - t % (N - 1)) % N] for t in range(RO)]
-    NE = 2
+    NE = (2, 1, 1)
+    NB = 4
 
     def engs(dst, first, n):
         m = 0
-        for e in topo.engines(core, dst)[first:first + n]:
+        for e in topo.engines(core, dst)[::2][first:first + n]:
             m |= 1 << e
         return m
 
-    def exchange(kind):
+    def exchange(ts):
         tr = []
-        for t in range(RO):
+        for t in ts:
             a = topo.addr(outq[t])
-            src = X("qw%d" % t, 0, 128)[0] if kind == "q" else X("sti", 8 * t, 8 * t + 8)[0]
-            dst = X("qw%d" % t, 128, 256)[0] if kind == "q" else X("stin", 8 * t, 8 * t + 8)[0]
-            tr.append(RemoteDMATransfer(dst_ids=[DstId(rid=a[0], pnc=a[1])], dma_engine_mask=engs(outq[t], NE * t, NE),
-                                        remote_sem=T.sem["r%s%d" % (kind, t)], src=src, dst=dst))
+            for kind, src, dst in (("s", W("sti"), W("stin%d" % t)), ("q", X("qw", 0, 128), X("qw", 128 * t + 128, 128 * t + 256))):
+                tr.append(RemoteDMATransfer(dst_ids=[DstId(rid=a[0], pnc=a[1])], dma_engine_mask=engs(outq[t], NE[t] * len(tr), NE[t]),
+                                            remote_sem=T.sem["r%s%d" % (kind, t)], src=src[0], dst=dst[0]))
         g.remote_dma_fused(tr, local_sem=T.sem.ls)
         return []
 
     def sendb(t):
         a = topo.addr(back[t])
-        g.remote_dma(out_ap=X("aw%d" % t, 48, 88)[0], in_ap=X("bo%d" % t, 0, 40)[0], remote_sem=T.sem["rb%d" % t], local_sem=T.sem.ls,
-                     pid=a[1], routing_id=a[0], dma_engine_mask=engs(back[t], 0, 4))
+        g.remote_dma(out_ap=X("la%d" % t, 8, 48)[0], in_ap=X("lb%d" % t, 8, 48)[0], remote_sem=T.sem["rb%d" % t], local_sem=T.sem.ls,
+                     pid=a[1], routing_id=a[0], dma_engine_mask=engs(back[t], 0, NB))
         return []
 
-    lsn = NE * RO * 2 + 4 * RO
+    lsn = 2 * sum(NE) + NB * RO
 
-    dma(W("sti"), ext("st"))
-    for t in range(RO):
-        dma(X("qw%d" % t, 0, 128), ext("q"))
-    dma(W("nbi"), ext("nb"), 5.0)
-    dma(X("tab", 0, 4096), ext("ang"), 6.0)
-    dma(W("thi"), ext("th"))
-    s1 = add("G", lambda: exchange("s"), [W("sti")], [], 1.0)
-    s2 = add("G", lambda: exchange("q"), [X("qw%d" % t, 0, 128) for t in range(RO)], [], 1.0)
-    for t in range(RO):
-        add("R", None, [], [X("stin", 8 * t, 8 * t + 8)], 3.0, mdep=[s1], sem="rs%d" % t, cnt=NE)
-        add("R", None, [], [X("qw%d" % t, 128, 256)], 3.0, mdep=[s2], sem="rq%d" % t, cnt=NE)
+    dma(X("sti", 0, 24), ext("st"), 2.0)
+    dma(X("qw", 0, 128), ext("q"), 2.0)
+    dma(W("nbi"), ext("nb"), 6.0)
+    dma(X("tab", 0, 4096), ext("ang"), 9.0)
+    dma(W("thi"), ext("th"), 9.0)
+    vms(X("sti", 24, 64), 0)
+    for ts in ((0,), (1, 2)):
+        s = add("G", lambda ts=ts: exchange(ts), [W("sti"), X("qw", 0, 128)], [], 1.0)
+        for t in ts:
+            add("R", None, [], [W("stin%d" % t)], 4.0, mdep=[s], sem="rs%d" % t, cnt=NE[t])
+            add("R", None, [], [X("qw", 128 * t + 128, 128 * t + 256)], 4.0, mdep=[s], sem="rq%d" % t, cnt=NE[t])
 
     iota(W("pi"), [[0, 1]], 0, 1)
-    iota(W("cf"), [[1, 128]], 0, 0, 128, True)
-    iota(W("cg"), [[1, 8], [0, 16]], 0, 0, 128, True)
-    iota(W("cr"), [[0, 17], [1, 16]], 0, 0, 272, True)
-    iota(W("win2"), [[2, 2048]], 1, 0, 2048, True)
-    iota(W("c128"), [[1, 128]], 0, 0, 128)
-    vts(W("gi"), W("pi"), 4, None, AL.arith_shift_right)
-    vts(W("ii"), W("pi"), 15, None, AL.bitwise_and)
-    vcp(W("pf"), W("pi"))
-    vcp(W("gf"), W("gi"))
-    vcp(W("fi"), W("ii"))
+    iota(W("pf"), [[0, 1]], 0, 1)
+    iota(W("cf"), [[1, 128]], 0)
+    iota(W("cg"), [[1, 8], [0, 16]], 0)
+    iota(W("cr"), [[0, 8], [1, 16]], 0)
+    iota(W("c8"), [[0, 16], [1, 8]], 0)
+    for c in range(4):
+        iota(X("win", c * 512, c * 512 + 512), [[1, 512]], c * 512)
     P_, G_, I_ = W("pf"), W("gf"), W("fi")
+    vts(W("gi"), W("pi"), 4, None, AL.arith_shift_right)
+    vcp(G_, W("gi"))
+    vts(I_, G_, -16.0, P_, AL.mult, AL.add)
     vts(W("mhi"), I_, 8.0, None, AL.is_ge)
     vts(W("mlo"), I_, 8.0, None, AL.is_lt)
-    vts(W("mhi128"), W("mhi"), 128.0, None, AL.mult)
-    vts(W("mhi8"), W("mhi"), 8.0, -8.0, AL.mult, AL.add)
-    vts(W("corrw"), I_, 8192.0, -122880.0, AL.mult, AL.add)
-    vts(W("corrn"), W("corrw"), -1.0, 1.0, AL.mult, AL.add)
-    vcp(W("qown"), W("c128"))
-    vts(W("qpar"), W("c128"), 128.0, None, AL.add)
-    vts(W("qmix"), W("c128"), W("mhi128"), None, AL.add)
-    iota(W("c8"), [[16, 8]], 15, 0, 8)
-    vcp(W("ls"), W("c8"))
-    vts(W("ls0"), W("c8"), W("mhi8"), None, AL.add)
-    vts(W("ibf"), W("cf"), P_, None, AL.is_equal)
-    vts(W("negib"), W("cf"), P_, -1.0, AL.is_equal, AL.mult)
-    vts(W("idf"), W("cf"), P_, None, AL.is_equal)
-    vts(W("id6"), W("cf"), P_, 296.0, AL.is_equal, AL.mult)
-    vts(W("penr"), W("cf"), P_, -131072.0, AL.is_equal, AL.mult)
-    vts(W("indf"), W("cg"), G_, None, AL.is_equal)
-    vts(W("indl"), W("cg"), G_, W("mlo"), AL.is_equal, AL.mult)
-    vts(W("indh"), W("cg"), G_, W("mhi"), AL.is_equal, AL.mult)
-    vts(W("ind6"), W("cg"), G_, 296.0, AL.is_equal, AL.mult)
-    vts(W("ind6l"), W("indl"), 296.0, None, AL.mult)
-    vts(W("ind6h"), W("indh"), 296.0, None, AL.mult)
-    vts(W("indn"), W("cg"), G_, -4096.0, AL.is_equal, AL.mult)
-    vts(W("indnl"), W("indl"), -4096.0, None, AL.mult)
-    vts(W("indnh"), W("indh"), -4096.0, None, AL.mult)
+    vts(W("ncorr"), I_, 8192.0, -122880.0, AL.mult, AL.add)
+    vts(W("c1"), I_, 8192.0, -122879.5, AL.mult, AL.add)
+    for n, v in (("ibf", 1.0), ("negib", -1.0), ("bigi", 131072.0), ("i594", 594.0), ("dlo", W("mlo")), ("dhi", W("mhi")), ("i8k", 8192.0)):
+        vts(W(n), W("cf"), P_, v, AL.is_equal, AL.mult)
+    for n, v in (("ind", 1.0), ("indl", W("mlo")), ("indh", W("mhi")), ("ind6", 592.0)):
+        vts(W(n), W("cg"), G_, v, AL.is_equal, AL.mult)
+    vts(W("ind6l"), W("indl"), 592.0, None, AL.mult)
+    vts(W("ind6h"), W("indh"), 592.0, None, AL.mult)
+    vts(W("gk"), X("cg", 0, 128, 16), G_, 16.0, AL.is_equal, AL.mult)
+    vts(W("ngk"), X("cg", 0, 128, 16), G_, -16.0, AL.is_equal, AL.mult)
     vms(W("oneb"), 1.0)
-    vms(W("onef"), 1.0)
-    vms(W("c0"), CB)
-    vms(X("tab", 4096, TW), 0.0, 16)
-    vms(X("bits", 4096, TW), 0.0, 16)
-    iota(W("cg8"), [[1, 8]], 0, 0, 8, True)
-    vts(W("gk"), W("cg8"), G_, 16.0, AL.is_equal, AL.mult)
-    iota(W("tie"), [[0, 8], [1, 16]], 0, 0, 128, True)
-    iota(W("rsc"), [[0, 8], [1, 16]], 0, 0, 128, True)
-    iota(W("rs0c"), [[0, 16], [1, 8]], 0, 0, 128, True)
-    for a, b in (("rs", "rsc"), ("rs0", "rs0c")):
-        vts(W(b), W(b), 0.0, BIG - 1, AL.is_equal, AL.mult)
-        vts(W(a), W(b), -BIG, None, AL.add)
-    vts(W("dm"), W("cr"), I_, BIG + 8192, AL.is_gt, AL.mult, 272)
-    vts(W("dm"), W("dm"), -BIG, None, AL.add, None, 272)
+    vms(W("crow"), 1.0)
+    vms(X("crow", 0, 128, 1, (0, 1)), -8388608.0)
+    vms(X("tab", 4096, TW), 0.0)
+    vts(W("rs"), W("cr"), 0.0, TOP, AL.is_equal, AL.mult)
+    vts(W("rs0"), W("c8"), 0.0, TOP, AL.is_equal, AL.mult)
+    vts(W("dm"), W("cr"), I_, BIG + 8192, AL.is_gt, AL.mult)
+    vts(W("dm"), W("dm"), -BIG, None, AL.add)
     vcp(W("thf"), W("thi"))
-    vts(W("nbw"), W("nbi"), 2.0, 1.0, AL.mult, AL.add, 2048)
     for t in range(RO):
-        if t < 2:
-            vms(X("xa%d" % t, 1408, 1536), -1.0)
-        vcp(W("va%d" % t), X("sti", 8 * t, 8 * t + 8))
-        vcp(W("vb%d" % t), X("stin", 8 * t, 8 * t + 8))
-        vts(X("aw%d" % t, 0, 8), X("sti", 8 * t, 8 * t + 8), 2.0, 1.0, AL.mult, AL.add)
-    cbcol = X("c0", 0, 1)
+        la = "la%d" % t
+        vcp(X(la, 0, 8), X("sti", 8 * t, 8 * t + 8))
+        vms(X(la, 48, 56), 0)
+        vcp(X(la, 56, 64), X("sti", 8 * t, 8 * t + 8))
+        vcp(X("lb%d" % t, 0, 8), X("stin%d" % t, 8 * t, 8 * t + 8))
+    one1 = X("oneb", 0, 128, 1, (0, 1))
 
-    def lessened(c):
-        vts(X("e1", c * 512, c * 512 + 512), X("tab", c * 512, c * 512 + 512), 0.5, 0.75, AL.add, AL.mult, 512)
+    def spread(e, dst, src, ks):
+        for k in ks:
+            o, a = X(dst, k, 2048, 16), X("qw", 128 * src, 128 * src + 128)
+            if e == "G":
+                keep(o, a, [[0, 128]], 0)
+            elif e == "V":
+                vcp(o, a)
+            else:
+                act(o, a, AF.Copy)
 
     def prep(t):
+        la, lb = IX("win", 0, 2048, "la%d" % t, 56, 64), IX("win", 0, 2048, "lb%d" % t, 0, 8)
         xa, xb = X("xa%d" % t, 0, 128), X("xb%d" % t, 0, 128)
-        va, vb = "va%d" % t, "vb%d" % t
-        for o, w, l, s in ((W("na"), "nbw", va, "mlo"), (W("nb2"), "nbw", vb, "mhi"), (W("xma"), "win2", va, "mlo"), (W("xmb"), "win2", vb, "mhi")):
-            act(o, IX(w, 0, 2048, l, 0, 8), AF.Copy, 128, 1.6, scale=W(s))
-        act(xa, IX("win2", 0, 2048, va, 0, 8), AF.Copy, 128, 1.6)
-        act(xb, IX("win2", 0, 2048, vb, 0, 8), AF.Copy, 128, 1.6)
-        nm = W("nm%d" % t)
-        vtt(nm, W("na"), W("nb2"), AL.add)
-        vtt(W("xm"), W("xma"), W("xmb"), AL.add)
-        act(W("cm"), W("xm"), AF.Identity, scale=296.0, bias=cbcol)
-        vtt(W("tp"), nm, W("xm"), AL.mult)
+        act(xa, la, AF.Copy)
+        act(xb, lb, AF.Copy)
+        act(X("pa%d" % t, 0, 128), la, AF.Identity, scale=4.0, bias=2.0)
+        act(X("pb_%d" % t, 0, 128), lb, AF.Identity, scale=4.0, bias=2.0)
+        vtt(W("da"), IX("nbi", 0, 2048, "la%d" % t, 56, 64), xa, AL.subtract)
+        vtt(W("db"), IX("nbi", 0, 2048, "lb%d" % t, 0, 8), xb, AL.subtract)
+        xm, d, nm = X("pb5", 0, 128), X("pb5", 128, 256), X("pb4", 0, 128)
+        lx, ld = [(W("dlo"), xa), (W("dhi"), xb)], [(W("dlo"), W("da")), (W("dhi"), W("db"))]
+        for o, l in ((xm, lx), (nm, lx + ld), (d, ld)):
+            mm([(o, a, b, i == 0, i == len(l) - 1) for i, (a, b) in enumerate(l)])
+            if o is xm:
+                act(W("pm"), xm, AF.Identity, scale=4.0, bias=2.0)
+                act(W("cm"), xm, AF.Identity, scale=594.0, bias=-8388607.0)
+        act(W("dn0%d" % t), d, AF.Copy)
+        vtt(W("tp"), W("pm"), nm, AL.mult)
         vtt(W("zpi"), W("tp"), W("cm"), AL.add)
         vts(W("hpi"), W("zpi"), 4, 4095, AL.arith_shift_right, AL.bitwise_and)
         vcp(W("h0%d" % t), W("hpi"))
-        for o, l in (("qm", "qmix"), ("qb", "qpar")):
-            for c in range(4):
-                act(X("%s%d" % (o, t), c * 512, c * 512 + 512), IX("qw%d" % t, 0, 256, l, c * 32, c * 32 + 32), AF.Copy, 512, 1.5)
-        vtt(W("pnp%d" % t), nm, W("xm"), AL.is_equal)
-        un = W("unp%d" % t)
-        act(un, W("pnp%d" % t), AF.Identity, scale=-1.0, bias=1.0)
-        d = X("pb7", 0, 128)
-        for x, xx, m in (("a", xa, "indnl"), ("b", xb, "indnh")):
-            mm([(d, W("idf"), xx, True, False), (d, W(m), un, False, True)], 640)
-            act(W("rp%s%d" % (x, t)), d, AF.Relu)
+        vts(W("pn0%d" % t), W("dn0%d" % t), 0.0, None, AL.is_equal)
 
-    def records(x, hl, qx):
-        for c in SCHUNKS + tuple(c for c in range(4) if c not in SCHUNKS):
-            q = X(qx, c * 512, c * 512 + 512)
-            i = IX("tab", 0, TW, hl, c * 32, c * 32 + 32)
-            if c in SCHUNKS:
-                o = X("pb6", 0, 512)
-                act(W("xs" + x), i, AF.Copy, 512, 1.5)
-                mm([(o, W("ibf"), W("xs" + x), True, False), (o, W("negib"), q, False, True)], 1024)
-            else:
-                o = X("dif" + x, c * 512, c * 512 + 512)
-                vtt(o, i, q, AL.subtract, 512, 1.5)
-            act(X("ad" + x, c * 512, c * 512 + 512), o, AF.Abs, 512)
+    rot = [0]
 
-    def choose(x, key, rs, ls, nn):
-        ks, r = W("ks" + x), W("r" + x)
-        act(ks, key, AF.Copy)
-        vscan(r, W(rs), ks, -1.0, AL.max, AL.min)
-        vtt(W("mk" + x), IX("r" + x, 0, 128, ls, 0, 8), ks, AL.is_equal, 128, 1.6)
+    def records(x, hl, qx, nv, nc):
+        ch = [(a, min(a + 512, 2048)) for a in range(nv, 2048, 512)]
+        for a, b in ch:
+            act(X("xs" + x, a, b), IX("tab", 0, TW, hl, a // 16, b // 16), AF.Copy)
+        vtt(X("dif" + x, 0, nv), IX("tab", 0, TW, hl, 0, nv // 16), X(qx, 0, nv), AL.subtract)
+        if nc:
+            vts(X("ad" + x, 0, nc), X("dif" + x, 0, nc), 0.0, 2.0, AL.max, AL.mult)
+        if nv > nc:
+            act(X("ad" + x, nc, nv), X("dif" + x, nc, nv), AF.Abs)
+        for a, b in ch:
+            rot[0] += 1
+            o = X("pb%d" % (6 + rot[0] % 2), 0, b - a)
+            mm([(o, W("negib"), X(qx, a, b), True, False)])
+            mm([(o, W("ibf"), X("xs" + x, a, b), False, True)])
+            act(X("ad" + x, a, b), o, AF.Abs)
+
+    def keys(x, kb, pn, nc):
+        key = X(kb, 0, 128)
+        mm([(key, one1, X("cr", 0, 128, 1, (0, 1)), True, False)] + [(key, p, W("bigi"), False, False) for p in pn])
+        if nc:
+            mm([(X(kb, k, 128, 16, (0, nc // 16)), X("dif" + x, k, nc, 16), W("ngk"), False, False) for k in range(16)])
+        mm([(X(kb, k, 128, 16), X("ad" + x, k, 2048, 16), W("gk"), False, k == 15) for k in range(16)])
+        return key
+
+    def choose(x, key, rs, d):
+        vscan(W("r" + x), W(rs), key, TOP, AL.max, AL.min)
+        vscan(REV("rr" + x), W(rs), REV("r" + x), TOP, AL.max, AL.min)
+        vtt(W("mk" + x), W("rr" + x), key, AL.is_equal)
         m1 = X("pb%d" % (4 + "ab".index(x)), 0, 128)
-        mm([(m1, W("mk" + x), W("ibf"), True, True)], 128)
-        vtt(W("w" + x), m1, nn, AL.mult, 128, 1)
+        mm([(m1, W("mk" + x), W("ibf"), True, True)])
+        vtt(W("w" + x), m1, d, AL.mult)
 
-    def after(x, src, t, a, indB, rv, ind6):
+    def after(x, src, t, a, ind, ind6):
         i = "ab".index(x)
-        bb, w = X("pb%d" % (2 + i), 0, 128), W("w" + src)
-        mm([(bb, W("idf"), rv, True, False)], 512)
-        mm([(bb, W(indB), w, False, True)], 512)
-        vscan(W("sc" + x), X("dm", 0, 128), bb, 0.0, AL.add, AL.max)
-        last = X("sc" + x, 15, 128, 16)
+        bb, w, xo = X("pb%d" % (2 + i), 0, 128), W("w" + src), X("x%s%d" % (x, t), a * 128, a * 128 + 128)
+        mm([(bb, W("ibf"), xo, True, False)])
+        mm([(bb, W(ind), w, False, True)])
         if a < 4:
-            cc = X("pb%d" % (4 + i), 128, 256)
-            mm([(cc, X("c0", 0, 128, 1, (0, 1)), X("onef", 0, 128, 1, (0, 1)), True, False), (cc, W("id6"), rv, False, False),
-                (cc, W(ind6), w, False, True)], 1536)
-            vts(W("vl" + x), last, W("corrn"), 0.5, AL.subtract, AL.mult)
-        act(X("aw%d" % t, (a + 1) * 8, (a + 2) * 8) if x == "a" else X("bo%d" % t, a * 8, (a + 1) * 8), last, AF.Identity, bias=W("corrw"))
-        if x == "a" or a < 4:
+            cc = X("pb%d" % i, 128, 256)
+            mm([(cc, X("crow", 0, 128, 1, (0, 2)), X("oneb", 0, 128, 1, (0, 2)), True, False), (cc, W("i594"), xo, False, False)])
+            mm([(cc, W(ind6), w, False, True)])
+        vscan(W("sc" + x), W("dm"), bb, 0.0, AL.add, AL.max)
+        last = X("sc" + x, 15, 128, 16)
+        if x == "a" and a == 4:
+            vts(X("aw", 96, 104), last, W("c1"), 2.0, AL.add, AL.mult)
+        c = 64 + 8 * a if x == "a" else 8 + 8 * a
+        vts(X("l%s%d" % (x, t), c, c + 8), last, W("ncorr"), None, AL.add)
+        if a < 4:
             act(X("x%s%d" % (x, t), (a + 1) * 128, (a + 2) * 128), bb, AF.Copy)
-
-    def keys(x, key, un):
-        n = key[1][0][0]
-        mm([(key, X("oneb", 0, 128, 1, (0, 1)), X("tie", 0, 128, 1, (0, 1)), True, False)], 128)
-        mm([((T[n][:, k:128:16], key[1]), X("ad" + x, k, 2048, 16), W("gk"), False, False) for k in range(16)], 1024)
-        mm([(key, un, W("penr"), False, True)], 128)
+        if a < 3:
+            act(X(("pa%d" if x == "a" else "pb_%d") % t, (a + 1) * 128, (a + 2) * 128), bb, AF.Identity, scale=4.0, bias=2.0)
 
     def first(t):
-        records("a", "h0%d" % t, "qm%d" % t)
-        key = X("pb0", 0, 128)
-        keys("a", key, W("unp%d" % t))
-        choose("a", key, "rs0", "ls0", W("nm%d" % t))
-        after("b", "a", t, 0, "indh", W("rpb%d" % t), "ind6h")
-        after("a", "a", t, 0, "indl", W("rpa%d" % t), "ind6l")
+        records("a", "h0%d" % t, "qm", OPT["nv0"], OPT["nc0"])
+        key = keys("a", "pb0", [W("pn0%d" % t)], OPT["nc0"])
+        choose("a", key, "rs0", W("dn0%d" % t))
+        after("b", "a", t, 0, "indh", "ind6h")
+        after("a", "a", t, 0, "indl", "ind6l")
 
     def step(x, t, a):
         i = "ab".index(x)
-        pm, pd = "pb%d" % (2 + i), "pb%d" % (4 + i)
-        xh, v, nn = "x%s%d" % (x, t), "vl" + x, W("nn" + x)
-        vtt(W("t1" + x), IX("nbw", 0, 2048, v, 0, 8), X(xh, (a - 1) * 128, a * 128), AL.mult, 128, 1.6)
-        act(nn, IX("nbw", 0, 2048, v, 0, 8), AF.Copy, 128, 1.6)
-        vtt(W("zi" + x), W("t1" + x), X(pd, 128, 256), AL.add, 128, 1)
+        xh, c = "x%s%d" % (x, t), (56 if x == "a" else 0) + 8 * a
+        nb = IX("nbi", 0, 2048, "l%s%d" % (x, t), c, c + 8)
+        xo, d = X(xh, a * 128, a * 128 + 128), W("dn" + x)
+        vtt(W("t1" + x), nb, X(("pa%d" if x == "a" else "pb_%d") % t, (a - 1) * 128, a * 128), AL.mult)
+        vtt(W("zi" + x), W("t1" + x), X("pb%d" % i, 128, 256), AL.add)
         vts(W("hi" + x), W("zi" + x), 4, 4095, AL.arith_shift_right, AL.bitwise_and)
         vcp(W("hl" + x), W("hi" + x))
-        records(x, "hl" + x, "qa" if x == "a" else "qb%d" % t)
-        n = min(a + 1, 4)
-        mm([(X(pd, m * 128, m * 128 + 128), W("idf"), nn, True, True) for m in range(n)], 512 * n)
-        vtt(X("pn" + x, 0, n * 128), X(xh, 0, n * 128), X(pd, 0, n * 128), AL.is_equal, n * 128, 1)
+        nv, nc = (OPT["nvl"], OPT["ncl"]) if (x, a) == ("a", 4) else (OPT["nv"], OPT["nc"])
+        records(x, "hl" + x, "qa" if x == "a" else "qb%d" % (t % 2), nv, nc)
+        vtt(d, nb, xo, AL.subtract)
+        n, pd = min(a + 1, 4), "pb%d" % (4 + i)
+        for m in range(n):
+            o = X(pd, m * 128, m * 128 + 128)
+            mm([(o, W("ibf"), xo, True, False), (o, W("ibf"), d, False, True)])
+        vtt(X("pn" + x, 0, n * 128), X(xh, 0, n * 128), X(pd, 0, n * 128), AL.is_equal)
         if a == 4:
-            d = X("pb7", 384, 512)
-            mm([(d, W("idf"), nn, True, True)], 512)
-            vtt(X("pn" + x, 512, 640), X(xh, 512, 640), d, AL.is_equal, 128, 1)
-        sg = X(pm, 128, 256)
-        mm([(sg, W("ibf"), X("pn" + x, m * 128, m * 128 + 128), m == 0, m == a) for m in range(a + 1)], 128 * (a + 1))
-        un = W("unb" + x)
-        act(un, sg, AF.Relu, scale=-1.0, bias=1.0)
-        rs = X(pm, 256, 384)
-        mm([(rs, W("idf"), X(xh, a * 128, a * 128 + 128), True, False), (rs, W("indn"), un, False, True)], 640)
-        rv = W("rv" + x)
-        act(rv, rs, AF.Relu)
-        key = X("pb%d" % i, 0, 128)
-        keys(x, key, un)
-        choose(x, key, "rs", "ls", nn)
-        after(x, x, t, a, "indf", rv, "ind6")
+            vts(X("pn" + x, 512, 640), d, 0.0, None, AL.is_equal)
+        key = keys(x, "pb%d" % i, [X("pn" + x, m * 128, m * 128 + 128) for m in range(a + 1)], nc)
+        choose(x, key, "rs", d)
+        after(x, x, t, a, "ind", "ind6")
         if x == "b" and a == 4:
-            s = add("G", lambda: sendb(t), [W("bo%d" % t)], [], 1.0)
-            add("R", None, [], [X("aw%d" % t, 48, 88)], 3.0, mdep=[s], sem="rb%d" % t, cnt=4)
+            s = add("G", lambda: sendb(t), [X("lb%d" % t, 8, 48)], [], 1.0)
+            add("R", None, [], [X("la%d" % t, 8, 48)], 3.0, mdep=[s], sem="rb%d" % t, cnt=NB)
 
-    def tolist(name, w):
-        vscan(X("lsc", 0, w), X("dm", 0, w), X("lr", 0, w), 0.0, AL.add, AL.max, w)
-        vts(X(name, 0, w // 16), X("lsc", 15, w, 16), W("corrw"), None, AL.add)
+    LP, LV, LN, LA = 0, 18, 36, 54
 
     def late_constants():
-        def blk(i):
-            return i * 8
-
-        def bb(j):
-            return 0 if j == 0 else 48 + (j - 1) * 8
-        for name, f, tail in (("LP", lambda i, j: blk(i - 1), [(200, 8, bb(1)), (208, 8, 0), (216, 24, 48), (240, 32, 0)]),
-                              ("LV", lambda i, j: blk(i), [(200, 8, 0), (208, 32, 48), (240, 32, 8)]),
-                              ("LN", lambda i, j: bb(j - 1), [(200, 8, 8), (208, 32, 56), (240, 32, 16)]),
-                              ("LB", lambda i, j: bb(j), [(200, 8, 0)])):
-            iota(X("lr", 0, 200, 25), [[1, 8]], 0, 0, 8, True)
-            for e in range(1, 25):
-                ix = 25 - e
-                iota(X("lr", e, 200, 25), [[1, 8]], f(ix // 5 + 1, ix % 5 + 1), 0, 8, True)
+        iota(W("selc"), [[0, 2048]], 0)
+        for i in range(16):
+            keep(X("selc", 129 * i, 129 * i + 113, 16), X("ind", 0, 128, 16), [[0, 8]], 0)
+        iota(W("nsb"), [[0, 2048]], -1)
+        keep(W("nsb"), W("nsb"), [[-1, 16], [-16, 8], [0, 16]], 1)
+        iota(W("lr"), [[0, 1088]], 48)
+        byi, byj = [[1, 8], [-8, 5], [0, 5]], [[1, 8], [0, 5], [-8, 5]]
+        for l, pat, base, tail in ((LP, byi, 88, ((0, 8, 8), (16, 32, 56), (48, 32, 0))), (LV, byj, 40, ((0, 8, 56), (16, 32, 64), (48, 32, 8))),
+                                   (LN, byj, 32, ((0, 8, 64), (16, 24, 72), (48, 32, 16))), (LA, byi, 96, ())):
+            iota(X("lr", 16 * l, 16 * l + 200), pat, base)
+            iota(X("lr", 16 * l + 24, 16 * l + 200, 25), [[0, 8]], 48)
             for c, n, b in tail:
-                iota(X("lr", c, c + n), [[1, n]], b, 0, n, True)
-            tolist(name, 208 if name == "LB" else 272)
-        for k in range(10):
-            iota(X("lr", k * 8, k * 8 + 8), [[1, 8]], 8 if 1 <= k <= 4 else 0, 0, 8, True)
-            iota(X("thr", k * 8, k * 8 + 8), [[0, 8]], k if 1 <= k <= 4 else 5 * (k - 4) if 5 <= k <= 8 else 1, 0, 8, True)
-        tolist("LM", 80)
-        iota(X("pack", 0, 200, 25), [[0, 8]], 0, 0, 8)
-        for e in range(1, 25):
-            ix = 25 - e
-            iota(X("pack", e, 200, 25), [[0, 8]], (ix * 8 + ix % 5) << 12, 0, 8)
-        f, fI, fJ, fT, fU, fV = [W(n) for n in ("ft", "fI", "fJ", "fT", "fU", "fV")]
-        iota(f, [[1, 32]], 0, 0, 32, True)
-        vts(W("fii"), f, 0.2, -0.4, AL.mult, AL.add)
-        vcp(fI, W("fii"))
-        vts(fJ, fI, -4.0, None, AL.mult)
-        vtt(fJ, fJ, f, AL.add)
-        vts(fT, fJ, I_, -1.0, AL.subtract, AL.is_ge)
-        vts(fU, fJ, I_, -4.0, AL.subtract, AL.add)
-        vtt(fU, fU, fT, AL.mult)
-        vts(fU, fU, 11.0, None, AL.add)
-        vts(fT, fI, I_, -1.0, AL.subtract, AL.is_ge)
-        vts(fV, fU, I_, -1.0, AL.subtract, AL.mult)
-        vtt(fV, fV, fT, AL.mult)
-        vtt(fV, fV, fU, AL.add)
-        vts(W("tw"), fV, 128.0, None, AL.mult)
-        vms(X("tw", 0, 1), 1408.0)
-        vms(W("sel"), 1.0, 2048)
-        keep(W("sel"), [[0, 16], [1, 128]], -1, 2048)
-        keep(W("sel"), [[1, 16], [0, 8], [-1, 16]], 0, 2048)
-        vts(W("m6"), I_, 6.0, None, AL.is_ge)
-        vts(W("p0"), W("m6"), -6.0, None, AL.mult)
-        vtt(W("p0"), W("p0"), I_, AL.add)
-        vcp(W("wi"), W("p0"))
-        vts(W("b0"), W("wi"), 1, None, AL.bitwise_and)
-        vts(W("b1"), W("wi"), 1, 1, AL.arith_shift_right, AL.bitwise_and)
-        vts(W("b2"), W("wi"), 2, 1, AL.arith_shift_right, AL.bitwise_and)
-        vts(W("p0"), W("b0"), -0.5, 1.0, AL.mult, AL.add)
-        vts(W("p1"), W("b1"), -0.75, 1.0, AL.mult, AL.add)
-        vts(W("p2"), W("b2"), -0.9375, 1.0, AL.mult, AL.add)
-        vtt(W("p0"), W("p0"), W("p1"), AL.mult)
-        vtt(W("pw"), W("p0"), W("p2"), AL.mult)
-        vts(W("m12"), I_, 12.0, None, AL.is_lt)
-        iota(W("eg"), [[1, 8], [0, 64]], 0, 0, 512, True)
-        iota(W("ex"), [[0, 8], [1, 64]], 0, 0, 512, True)
-        vts(W("ei"), W("ex"), W("pw"), -0.5 + 2.0 ** -8, AL.mult, AL.add, 512)
-        vts(W("ei"), W("ei"), 1, None, AL.bitwise_and, None, 512)
-        vts(W("ea"), W("ei"), 2.0, -1.0, AL.mult, AL.add, 512)
-        vts(W("eb"), W("eg"), G_, None, AL.is_equal, None, 512)
-        vtt(W("ea"), W("ea"), W("eb"), AL.mult, 512)
-        vts(W("p1"), W("m6"), -1.0, 1.0, AL.mult, AL.add)
-        vtt(W("p2"), W("m6"), W("m12"), AL.mult)
-        vts(W("ehi"), W("ea"), W("p1"), None, AL.mult, None, 512)
-        vts(W("elo"), W("ea"), W("p2"), None, AL.mult, None, 512)
-        for o, e in ((X("pb7", 0, 128, 1, (0, 64)), "ehi"), (X("pb7", 0, 128, 1, (64, 128)), "elo")):
-            mm([(o, X(e, q * 64, q * 64 + 64), W("ibf"), q == 0, q == 7) for q in range(8)], 1024)
-        act(W("lt"), X("pb7", 0, 128), AF.Copy)
-        vms(W("rh"), 1.0, 2048)
-        vms(W("rl"), 1.0, 2048)
-        keep(W("rh"), [[1, 64], [0, 64]], -1, 4096)
-        keep(W("rl"), [[0, 64], [1, 64]], -1, 4096, 64)
-        for c in range(8):
-            mm([(X("pb7", 0, 512), W("lt"), X(r, c * 512, c * 512 + 512), r == "rh", r == "rl") for r in ("rh", "rl")], 1024)
-            act(X("bits", c * 512, c * 512 + 512), X("pb7", 0, 512), AF.Copy, 512)
-        iota(W("wc"), [[1, 240]], -112, 0, 240, True)
-        vts(W("wi"), W("pi"), 2, None, AL.arith_shift_right)
-        vcp(W("wh"), W("wi"))
-        vts(W("wi2"), W("pi"), 3, None, AL.bitwise_and)
-        for b in range(4):
-            vts(X("wbm", b, b + 1), W("wi2"), float(b), None, AL.is_equal)
-            vts(X("wid", b * 240, b * 240 + 240), W("wc"), W("wh"), X("wbm", b, b + 1), AL.is_equal, AL.mult, 240)
-        vms(W("la"), -256.0, 1024)
-        keep(W("la"), [[1, 16], [16, 8], [0, 16]], -1, 2048)
+                iota(X("lr", 16 * l + 200 + c, 16 * l + 200 + c + n), [[1, n]], b)
+        iota(W("pack"), [[0, 8], [8, 5], [1, 5]], 0)
+        iota(X("pack", 24, 200, 25), [[0, 8]], 63)
+        vts(W("pack"), W("pack"), 16384.0, 8192.0, AL.mult, AL.add)
+        iota(X("thr", 0, 16), [[0, 16]], 7 << 17)
+        for m in range(1, 5):
+            iota(X("thr", 8 + 8 * m, 16 + 8 * m), [[0, 8]], (5 - m) << 17)
+        iota(X("thr", 48, 80), [[-16384, 4], [0, 8]], 4 << 14)
+        vts(W("i7"), W("mhi"), -8.0, I_, AL.mult, AL.add)
+        vts(W("LH"), X("cf", 0, 6), 0.0, W("i7"), AL.mult, AL.add)
+        vts(X("l6", 0, 6), X("cf", 0, 6), 3.0, 8.0, AL.is_ge, AL.mult)
+        vts(W("LM"), X("l6", 0, 6), W("i7"), None, AL.add)
+        vts(W("de"), I_, 4112.0, None, AL.add)
+        vts(W("do"), I_, 4128.0, None, AL.add)
+        dd = X("cf", 1, 9)
+        vts(W("s8a"), dd, I_, 16.0, AL.is_gt, AL.mult)
+        vtt(W("s8b"), W("s8a"), dd, AL.subtract)
+        vts(W("src8"), W("s8b"), P_, None, AL.add)
+        vts(W("s8a"), dd, I_, 15.0, AL.add, AL.is_le)
+        vtt(W("s8b"), W("s8a"), dd, AL.mult)
+        vts(W("tgt8"), W("s8b"), P_, None, AL.add)
+        for d in range(8):
+            vts(X("dw", d * 128, d * 128 + 128), W("cf"), X("src8", d, d + 1), -1.0, AL.is_equal, AL.mult)
+            vts(X("tg", d * 128, d * 128 + 128), W("cf"), X("tgt8", d, d + 1), 8192.0, AL.is_equal, AL.mult)
+        keep(W("dw"), W("dw"), [[0, 8], [-1, 128]], 1, AL.not_equal, 1.0)
+        fI, fL, t1, t2, t3 = [W(n) for n in ("fI", "fL", "t1w", "t2w", "t3w")]
+        iota(fI, [[-1, 8], [0, 8]], 5)
+        iota(fL, [[-1, 8], [-1, 8]], 10)
+        vts(t1, fL, I_, -6.0, AL.subtract, AL.add)
+        vts(t2, fL, I_, None, AL.is_gt)
+        vtt(t1, t1, t2, AL.mult)
+        vts(t2, t1, -1.0, I_, AL.mult, AL.add)
+        vts(t2, t2, 1.0, None, AL.add)
+        vts(t3, fI, I_, None, AL.is_ge)
+        vtt(t2, t2, t3, AL.mult)
+        vtt(t1, t1, t2, AL.add)
+        vts(W("tw"), t1, 5.0, 128.0, AL.add, AL.mult)
+        vms(X("xa", 640, 768), -1.0)
+
+    def tolist():
+        o = X("pb5", 0, 68)
+        mm([(o, X("selc", 128 * i, 128 * i + 128), X("lr", i, 1088, 16), i == 0, i == 15) for i in range(16)])
+        vts(W("LL"), o, 0.0625, None, AL.mult)
+
+    def join_early(t):
+        vts(X("aw", 0, 96), X("la%d" % t, 0, 96), 2.0, 1.0, AL.mult, AL.add)
+        act(W("narr"), IX("aw", 0, 96, "LL", LN, LN + 18), AF.Copy)
+        act(W("varr"), IX("aw", 0, 96, "LL", LV, LV + 18), AF.Identity, scale=296.0, bias=CB)
+        act(W("bj"), IX("aw", 0, 96, "LL", LV, LV + 13), AF.Copy)
+        vtt(W("tj"), IX("aw", 0, 96, "LL", LP, LP + 18), W("narr"), AL.mult)
+        vtt(X("zj", 0, 280), X("tj", 0, 280), X("varr", 0, 280), AL.add)
+        vts(X("hji", 0, 280), X("zj", 0, 280), 4, 4095, AL.arith_shift_right, AL.bitwise_and)
+        vtt(W("hp"), X("hji", 0, 200), W("pack"), AL.add)
 
     def join(t):
-        aw = "aw%d" % t
-        vts(W("nlb"), X(aw, 48, 88), 0.5, -0.5, AL.mult, AL.add)
-        act(W("bj"), IX(aw, 0, 88, "LB", 0, 13), AF.Copy, 208, 1.6)
-        act(W("narr"), IX(aw, 0, 88, "LN", 0, 17), AF.Copy, 272, 1.6)
-        act(W("varr"), IX(aw, 0, 88, "LV", 0, 17), AF.Identity, 272, 1.6, scale=296.0, bias=cbcol)
-        vtt(W("eq"), IX(aw, 0, 88, "LV", 0, 13), W("bj"), AL.is_equal, 208, 1.6)
-        act(W("neq"), W("eq"), AF.Identity, 208, scale=-1.0, bias=1.0)
-        vtt(W("tj"), IX(aw, 0, 88, "LP", 0, 17), W("narr"), AL.mult, 272, 1.6)
-        vtt(W("hji"), W("tj"), W("varr"), AL.add, 272)
-        vts(W("hji"), W("hji"), 4, 4095, AL.arith_shift_right, AL.bitwise_and, 272)
-        vtt(X("hp", 0, 200), X("hji", 0, 200), X("pack", 0, 200), AL.add, 200)
-        vtt(X("ek", 0, 200), X("eq", 0, 200), X("hp", 0, 200), AL.mult, 200)
-        vscan(X("scj", 0, 200), X("neq", 0, 200), X("ek", 0, 200), 0.0, AL.mult, AL.add, 200)
-        vcp(W("j8"), X("scj", 24, 200, 25))
-        vts(X("win24", 0, 8), W("j8"), 15, None, AL.arith_shift_right)
-        vts(X("win24", 8, 16), W("j8"), 12, 7, AL.arith_shift_right, AL.bitwise_and)
-        vts(W("hj"), W("j8"), 4095, None, AL.bitwise_and)
-        vts(X("hr", 0, 72), X("hji", 200, 272), -4096.0, None, AL.add)
-        vts(X("hr", 72, 80), W("hj"), -4096.0, None, AL.add)
-        vcp(W("fl"), X("win24", 0, 8))
-        vtt(W("mk"), IX("win24", 0, 16, "LM", 0, 5), W("thr"), AL.is_ge, 80, 1.6)
-        vtt(W("off"), W("hr"), W("mk"), AL.mult, 80)
-        vts(W("off80"), W("off"), 4096.0, None, AL.add)
+        vtt(W("eq"), IX("aw", 0, 104, "LL", LA, LA + 13), W("bj"), AL.is_equal)
+        act(X("neq", 0, 200), X("eq", 0, 200), AF.Identity, scale=-1.0, bias=1.0)
+        vtt(W("ek"), X("eq", 0, 200), W("hp"), AL.mult)
+        vtt(W("t8"), X("aw", 96, 104), X("aw", 80, 88), AL.mult)
+        vtt(W("z8"), W("t8"), X("varr", 240, 248), AL.add)
+        vts(X("hji", 240, 248), W("z8"), 4, 4095, AL.arith_shift_right, AL.bitwise_and)
+        vscan(W("scj"), X("neq", 0, 200), W("ek"), NONE, AL.mult, AL.add)
+        vcp(X("w16", 0, 8), X("scj", 23, 200, 25))
+        vts(X("w16", 8, 16), X("w16", 0, 8), (1 << 17) - 1, None, AL.bitwise_and)
+        vts(X("hji", 208, 216), X("w16", 0, 8), 4095, None, AL.bitwise_and)
+        vtt(W("aa"), IX("w16", 0, 16, "LM", 0, 5), W("thr"), AL.subtract)
+        vtt(W("bb"), W("aa"), X("hji", 200, 280), AL.max)
+        vts(W("off"), W("bb"), 4096.0, None, AL.min)
+        vts(W("hm"), W("bb"), 4160.0, -2048.0, AL.min, AL.add)
 
     def lessen(t):
-        act(X("xr", 0, 640), IX("tab", 0, TW, "off80", 0, 40), AF.Copy, 640, 1.5)
-        vcp(X("xr", 640, 1280), IX("tab", 0, TW, "off80", 40, 80), 640, 1.5)
-        tot, cnt = X("pb5", 0, 128), X("pb5", 128, 136)
-        mm([(tot, W("ibf"), X("xr", k * 128, k * 128 + 128), k == 0, k == 9) for k in range(10)], 1280)
+        xv = OPT["xv"]
+        act(X("xr", xv, 1280), IX("tab", 0, TW, "off", xv // 16, 80), AF.Copy)
+        vcp(X("xr", 0, xv), IX("tab", 0, TW, "off", 0, xv // 16))
+        tot, cnt = X("pb0", 0, 128), X("pb1", 0, 8)
+        for k in range(10):
+            mm([(tot, W("ibf"), X("xr", k * 128, k * 128 + 128), k == 0, k == 9)])
         vts(W("ge"), tot, W("thf"), None, AL.is_ge)
-        mm([(cnt, W("ge"), W("gk"), True, True)], 64)
-        vts(W("nhc"), cnt, 139.0, -5.0, AL.subtract, AL.min)
-        act(X("hb", 0, 640), IX("bits", 0, TW, "off80", 0, 40), AF.Copy, 640, 1.5)
-        vcp(X("hb", 640, 1280), IX("bits", 0, TW, "off80", 40, 80), 640, 1.5)
-        rot = [0]
-        bk = ("pb2", "pb3", "pb4", "pb7", "pb0", "pb1", "pb6")
-
-        def chunk(w):
-            rot[0] += 1
-            return X(bk[rot[0] % len(bk)], 0, w)
-
-        def onehot(o, e, q, h, b):
-            c = chunk(320)
-            n = c[1][0][0]
-            mm([(X(n, j * 64, j * 64 + 64), X("hb", (h * 5 + j) * 128, (h * 5 + j) * 128 + 128), X(e, q * 64, q * 64 + 64), True, True)
-                for j in range(5)], 320)
-            r = X(o, (q * 10 + h * 5) * 64, (q * 10 + h * 5 + 5) * 64)
-            if rot[0] % 2:
-                act(r, c, AF.Relu, 320, bias=b)
-            else:
-                vts(r, c, b, 0.0, AL.add, AL.max, 320)
-        for h in range(2):
-            for q in range(8):
-                onehot("ohh", "ehi", q, h, -5.0)
-        for q in range(8):
-            for h in range(2):
-                onehot("ohl", "elo", q, h, X("nhc", q, q + 1))
-            mm([(X("pb5", q * 64, q * 64 + 64, 1, (0, 64)), X("ohh", (q * 10 + k) * 64, (q * 10 + k) * 64 + 64),
-                 X("ohl", (q * 10 + k) * 64, (q * 10 + k) * 64 + 64), k == 0, k == 9) for k in range(10)], 640)
-        vts(X("flg", 0, 512, 1, (0, 64)), X("pb5", 0, 512, 1, (0, 64)), 0.0, None, AL.is_gt, None, 512)
-        for b in range(4):
-            o = X("pb2", b * 64, b * 64 + 64)
-            mm([(o, X("wid", b * 240 + 112 - 16 * q, b * 240 + 240 - 16 * q, 1, (0, 64)), X("flg", q * 64, q * 64 + 64, 1, (0, 64)), q == 0, q == 7)
-                for q in range(8)], 512)
-        act(W("fx"), X("pb2", 0, 256), AF.Copy, 256)
-        for k in range(8):
-            c = chunk(512)
-            l = []
-            for h in range(2):
-                o = X(c[1][0][0], h * 256, h * 256 + 256)
-                l += [(o, W("ibf"), X("tab", k * 512 + h * 256, k * 512 + h * 256 + 256), True, False),
-                      (o, X("la", (2 * k + h) * 128, (2 * k + h) * 128 + 128), W("fx"), False, True)]
-            mm(l, 1024)
-            vtt(X("tab", k * 512, k * 512 + 512), X("e1", k * 512, k * 512 + 512), c, AL.max, 512, 1)
-            if t == RO - 1 and k % 2:
-                dma((T.ye[:, (k - 1) * 512:(k + 1) * 512], []), X("tab", (k - 1) * 512, (k + 1) * 512))
+        mm([(cnt, X("selc", 128 * i, 128 * i + 128), X("ge", i, 128, 16), i == 0, i == 15) for i in range(16)])
+        vts(W("u8"), cnt, -8.5, -4200.0, AL.add, AL.mult)
+        vtt(W("rep"), IX("u8", 0, 8, "LH", 0, 5), W("hm"), AL.max)
+        for c in range(0, 1280, 320):
+            act(X("nd1", c, c + 320), X("xr", c, c + 320), AF.Identity, scale=-0.25, bias=-191.625)
+            act(X("nd", c, c + 320), X("nd1", c, c + 320), AF.Identity, bias=192.0)
+        rep, re_, ro = W("rep"), X("rep", 0, 80, 2), X("rep", 1, 80, 2)
+        z = X("pb5", 0, 80)
+        mm([(z, W("ibf"), rep, True, False)])
+        c0 = 0
+        for bk, within, cross in (("pb6", range(6), ()), ("pb7", range(6, 8), range(8)), ("pb4", (), range(8, 16))):
+            l, s, c = [], [], 0
+            for d in within:
+                l.append((X(bk, c, c + 80), X("dw", d * 128, d * 128 + 128), rep, True, True))
+                s.append((z, X("tg", d * 128, d * 128 + 128), X("fl2", c0 + c, c0 + c + 80), False, False))
+                c += 80
+            for i in cross:
+                l += [(X(bk, c, c + 40), W("ibf"), ro, True, False), (X(bk, c, c + 40), X("nsb", i * 128, i * 128 + 128), re_, False, True)]
+                s.append((X("pb5", 1, 80, 2), W("i8k"), X("fl2", c0 + c, c0 + c + 40), False, i == 15))
+                c += 40
+            mm(l)
+            vts(X("fl2", c0, c0 + c), X(bk, 0, c), 0.0, None, AL.is_equal)
+            mm(s)
+            c0 += c
+        vts(X("offs", 0, 80, 2), X("pb5", 0, 80, 2), 2048.0, W("de"), AL.add, AL.min)
+        vts(X("offs", 1, 80, 2), X("pb5", 1, 80, 2), 2048.0, W("do"), AL.add, AL.min)
+        for u in range(40):
+            o = IX("tab", 0, TW, "offs", 2 * u, 2 * u + 2)
+            a, b, l = X("xr", 32 * u, 32 * u + 32), X("nd", 32 * u, 32 * u + 32), X("offs", 2 * u, 2 * u + 2)
+            add("V", lambda o=o, a=a, b=b: [g.vector.tensor_tensor(out=o[0], in0=a[0], in1=b[0], op=AL.add)], [a, b, l], [X("tab", 0, TW)], .15)
+        if t == RO - 1:
+            dma((T.ye[:], [], 0), X("tab", 0, 4096), 6.0)
 
     def rings(t):
-        xa = "xa%d" % t
-        act(X(xa, 768, 1408), IX("win2", 0, 2048, "nlb", 0, 40), AF.Copy, 640, 1.6)
-        vtt(W("of"), IX("tw", 0, 32, "fl", 0, 8), W("cf"), AL.add, 128, 1.6)
+        la = "la%d" % t
+        act(X("xa", 0, 640), IX("win", 0, 2048, la, 8, 48), AF.Copy)
+        act(X("xa", 768, 1536), IX("win", 0, 2048, la, 56, 104), AF.Copy)
+        vts(W("c8i"), X("w16", 0, 8), 14, None, AL.arith_shift_right)
+        vcp(W("fl"), W("c8i"))
+        vtt(W("of"), IX("tw", 0, 64, "fl", 0, 8), W("cf"), AL.add)
         vcp(W("ofu"), W("of"))
         for c in range(4):
-            act(X("gy", c * 512, c * 512 + 512), IX(xa, 0, 1536, "ofu", c * 32, c * 32 + 32), AF.Identity, 512, 1.6, scale=0.5, bias=-0.5)
-        y = X("pb7", 0, 128)
+            act(X("gy", c * 512, c * 512 + 512), IX("xa", 0, 1536, "ofu", c * 32, c * 32 + 32), AF.Copy)
+        y = X("pb3", 0, 128)
         for c in range(4):
-            mm([(y, X("sel", m * 128, m * 128 + 128), X("gy", m, 2048, 16), m == 0, m == 15) for m in range(c * 4, c * 4 + 4)], 2048)
-        act(W("yo"), y, AF.Copy)
-        dma((T.yr[:, t * 128:t * 128 + 128], []), W("yo"))
+            mm([(y, X("selc", m * 128, m * 128 + 128), X("gy", m, 2048, 16), m == 0, m == 15) for m in range(c * 4, c * 4 + 4)])
+        act(W("yo"), y, AF.Copy, scale=0.0625)
+        dma((T.yr[:, t * 128:t * 128 + 128], [], 0), W("yo"))
 
-    act(W("qa"), IX("qw0", 0, 256, "qown", 0, 128), AF.Copy, 2048, 1.5)
-    prep(0)
+    spread("V", "qm", 0, range(8))
+    spread("S", "qa", 0, range(16))
+    spread("V", "qm", 1, range(8, 16))
+    spread("G", "qb0", 1, range(16))
+    for t in range(RO):
+        prep(t)
+    late_constants()
     for t in range(RO):
         first(t)
+        if t + 1 < RO:
+            spread("G", "qm", t + 2, range(8, 16))
+            spread("G", "qb%d" % ((t + 1) % 2), t + 2, range(16))
         for a in range(1, 5):
             step("b", t, a)
-            step("a", t, a)
-            if a == 1:
-                for c in range(8):
-                    lessened(c)
+            if a == 4:
                 if t == 0:
-                    late_constants()
-            if a == 2 and t + 1 < RO:
-                prep(t + 1)
+                    tolist()
+                join_early(t)
+            step("a", t, a)
         join(t)
         lessen(t)
         rings(t)
+
+    def meets(x, y):
+        (lo, hi, s), (l2, h2, s2) = x, y
+        return l2 < hi and lo < h2 and (s != s2 or (lo - l2) % s == 0)
 
     n = len(ops)
     pred = [[] for _ in range(n)]
@@ -568,34 +525,35 @@ def program(g, core, T, topo):
         e = o["e"]
         d = {}
         for rw, regs in ((0, o["r"]), (1, o["w"])):
-            for nm, lo, hi in regs:
-                for j, l2, h2, w2 in seen.get(nm, ()):
-                    if l2 < hi and lo < h2 and (rw or w2) and j != i:
-                        d[j] = d.get(j, False) or ops[j]["e"] != e or e != "P"
+            for nm, lo, hi, s in regs:
+                for j, r2, w2 in seen.get(nm, ()):
+                    if (rw or w2) and j != i and meets((lo, hi, s), r2):
+                        d[j] = d.get(j, False) or ops[j]["e"] != e or (e != "P" and bool(w2))
         for nm in set(x[0] for x in o["r"] + o["w"] if x[0][:2] == "pb"):
             p = banks.get(nm)
             if p is not None:
                 d[p] = d.get(p, False) or ops[p]["e"] != e
             banks[nm] = i
         for rw, regs in ((0, o["r"]), (1, o["w"])):
-            for nm, lo, hi in regs:
+            for nm, lo, hi, s in regs:
                 l = seen.setdefault(nm, [])
-                if rw:
-                    l[:] = [x for x in l if not (lo <= x[1] and x[2] <= hi)]
-                l.append((i, lo, hi, rw))
+                if rw and s == 1:
+                    l[:] = [x for x in l if not (lo <= x[1][0] and x[1][1] <= hi)]
+                l.append((i, (lo, hi, s), rw))
         pred[i] = sorted(d.items())
 
     order = CACHE.get("order")
     if order is None:
+        lam = OPT["lam"]
         succ = [[] for _ in range(n)]
         npd = [0] * n
         for i, o in enumerate(ops):
-            for j in [p[0] for p in pred[i]] + list(o.get("mdep", ())):
-                succ[j].append(i)
+            for j, need in pred[i] + [(j, True) for j in o.get("mdep", ())]:
+                succ[j].append((i, lam if need else 0.0))
                 npd[i] += 1
         pr = [0.0] * n
         for i in range(n - 1, -1, -1):
-            pr[i] = ops[i]["c"] + ops[i].get("lat", 0) + max([pr[j] + .08 for j in succ[i]] or [0])
+            pr[i] = ops[i]["c"] + ops[i].get("lat", 0) + max([pr[j] + w for j, w in succ[i]] or [0])
         ready = [0.0] * n
         cand = {e: [] for e in ("V", "S", "P", "G", "Y", "R")}
         free = {e: 0.0 for e in cand}
@@ -610,9 +568,9 @@ def program(g, core, T, topo):
             order.append(i)
             free[e] = s + ops[i]["c"]
             fin = s + ops[i]["c"] + ops[i].get("lat", 0)
-            for j in succ[i]:
+            for j, w in succ[i]:
                 npd[j] -= 1
-                ready[j] = max(ready[j], fin + .08)
+                ready[j] = max(ready[j], fin + w)
                 if npd[j] == 0:
                     cand[ops[j]["e"]].append(j)
         CACHE["order"] = order
@@ -655,9 +613,9 @@ def program(g, core, T, topo):
     for i in range(dn[0]):
         g.wait_ge(T.sem["d%d" % i], 16)
     for t in range(RO):
-        g.wait_ge(T.sem["rq%d" % t], NE)
-        g.wait_ge(T.sem["rs%d" % t], NE)
-        g.wait_ge(T.sem["rb%d" % t], 4)
+        g.wait_ge(T.sem["rq%d" % t], NE[t])
+        g.wait_ge(T.sem["rs%d" % t], NE[t])
+        g.wait_ge(T.sem["rb%d" % t], NB)
     g.wait_ge(T.sem.ls, lsn)
 
 

@@ -1,11 +1,11 @@
-import numpy as np
+import math
 from concourse.bass import DstId, RemoteDMATransfer
 from concourse.mybir import dt, AluOpType, AxisListType, ActivationFunctionType
 
 AL = AluOpType
 AF = ActivationFunctionType
 RO, ST, N = 3, 5, 8
-TW = 4144
+TW = 4176
 F, B, H, I32, U16 = "float32", "bfloat16", "float16", "int32", "uint16"
 PHYS = {F: "vf", B: "vb", H: "vh", I32: "vi", U16: "vu"}
 SIZE = {F: 0, B: 0, H: 0, I32: 0, U16: 0}
@@ -18,16 +18,18 @@ def _sb(dtype, **kw):
         SIZE[dtype] += (n + 31) // 32 * 32
 
 
-_sb(B, tab=TW, qa=2048, qm=2048, qb0=2048, qb1=2048, qw=512, cf=128, cg=128, cr=128, c8=128, ibf=128, negib=128, bigi=128, ind=128, indl=128,
-    indh=128, ind6=128, ind6l=128, ind6h=128, dlo=128, dhi=128, gk=8, ngk=8, oneb=128, crow=128, selc=2048, nsb=2048, dw=1024, tg=1024,
-    i8k=128, fl2=1280, xr=1280, nd1=1280, nd=1280, lr=1088, ge=128)
-_sb(H, i594=128, da=128, db=128, rep=80, gy=2048)
-_sb(F, win=2048, xa=1536, pf=1, gf=1, fi=1, mlo=1, mhi=1, ncorr=1, c1=1, i7=1, de=1, do=1, thf=1, rs=128, rs0=128, dm=128,
+NL = 114
+_sb(B, tab=TW, qa=2048, qb0=2048, qb1=2048, qw=512, cfx=144, cg=128, cr=128, c8=128, ibf=128, negib=128, bigi=128, ind=128, indl=128,
+    indh=128, ind6=128, ind6l=128, ind6h=128, dl=144, dh=144, gk=8, ngk=8, oneb=128, crow=128, selc=2048, nsb=2048, dw=1024, tg=1024,
+    i8k=128, fl2=2560, ab2=2560, xr=1280, nd1=1280, nd=1280, lr=16 * NL, ge=128)
+VB["cf"] = (VB["cfx"][0], VB["cfx"][1] + 8, 128)
+_sb(H, i594=128, da=128, db=128, rep=320, gy=2048)
+_sb(F, win=2048, xa=1536, pf=1, gf=1, fi=1, mlo=1, mhi=1, ncorr=1, c1=1, i7=1, du=4, thf=1, rs=128, rs0=128, dm=128,
     s8a=8, s8b=8, src8=8, tgt8=8, l6=8, pack=200, thr=80, fI=64, fL=64, t1w=64, t2w=64, t3w=64, tw=64,
-    pm=128, cm=128, tp=128, aw=104, narr=288, varr=288, bj=208, tj=288, hp=200, eq=208, neq=208, ek=200, scj=200,
-    t8=8, aa=80, bb=80, hm=80, u8=8, of=128, yo=128)
-_sb(I32, nbi=2048, sti=64, stin0=64, stin1=64, stin2=64, pi=1, gi=1, thi=1, zpi=128, hpi=128, hji=288, zj=288, z8=8, w16=16, c8i=8)
-_sb(U16, LL=68, LH=6, LM=6, off=80, offs=80, fl=8, ofu=128)
+    pm=128, cm=128, tp=128, aw=104, narr=320, varr=320, bj=208, tj=320, hp=200, eq=208, neq=208, ek=200, scj=200,
+    t8=8, aa=80, bb=80, hm=320, u8=8, of=128, yo=128)
+_sb(I32, nbi=2048, sti=64, stin0=64, stin1=64, stin2=64, pi=1, gi=1, thi=1, zpi=128, hpi=128, hji=320, zj=320, z8=8, w16=16, c8i=8)
+_sb(U16, LL=NL, LM=6, off=80, offs=80, fl=8, ofu=128)
 for _x in "ab":
     _sb(F, **{"t1" + _x: 128, "r" + _x: 128, "rr" + _x: 128, "sc" + _x: 128})
     _sb(I32, **{"zi" + _x: 128, "hi" + _x: 128})
@@ -51,7 +53,7 @@ BIG = 16777216.0
 TOP = 100000.0
 CB = -296.0 - 8388608.0
 NONE = 63 * 16384.0 + 8192.0
-OPT = dict(nv=768, nc=768, nv0=896, nc0=768, nvl=1024, ncl=768, gat=1.56, lam=.08, xv=640)
+OPT = dict(nv=640, nc=640, nv0=512, nc0=512, nvl=1024, ncl=1024, gat=1.56, lam=.15, xv=640, ns=1, vs=3, ksp=0, look=.05, rl=3.0, rsp=1, bw=512, line=1, pp=1)
 
 
 def program(g, core, T, topo):
@@ -69,9 +71,9 @@ def program(g, core, T, topo):
     def W(n):
         return X(n, 0, VB[n][2])
 
-    def REV(n):
+    def REV(n, m):
         ph, o, w = VB[n]
-        return (T[ph][:, slice(o + w - 1, o - 1, -1)], [(ph, o, o + w, 1)], w)
+        return (T[ph][0:m, slice(o + w - 1, o - 1, -1)], [(ph, o, o + w, 1)], w)
 
     def IX(n, a, b, o, c, d):
         w, l = X(n, a, b), X(o, c, d)
@@ -181,21 +183,27 @@ def program(g, core, T, topo):
     dma(W("nbi"), ext("nb"), 6.0)
     dma(X("tab", 0, 4096), ext("ang"), 9.0)
     dma(W("thi"), ext("th"), 9.0)
+    for i in range(1, 5):
+        ops[i]["mdep"] = [i - 1]
     vms(X("sti", 24, 64), 0)
+    sent = []
     for ts in ((0,), (1, 2)):
-        s = add("G", lambda ts=ts: exchange(ts), [W("sti"), X("qw", 0, 128)], [], 1.0)
+        sent.append(len(ops))
+        s = add("G", lambda ts=ts: exchange(ts), [W("sti"), X("qw", 0, 128)], [], 1.0 if ts[0] else 3.0)
         for t in ts:
-            add("R", None, [], [W("stin%d" % t)], 4.0, mdep=[s], sem="rs%d" % t, cnt=NE[t])
-            add("R", None, [], [X("qw", 128 * t + 128, 128 * t + 256)], 4.0, mdep=[s], sem="rq%d" % t, cnt=NE[t])
+            lat = 14.0 if t else 4.0
+            add("R", None, [], [W("stin%d" % t)], lat, mdep=[s], sem="rs%d" % t, cnt=NE[t])
+            add("R", None, [], [X("qw", 128 * t + 128, 128 * t + 256)], lat, mdep=[s], sem="rq%d" % t, cnt=NE[t])
 
     iota(W("pi"), [[0, 1]], 0, 1)
     iota(W("pf"), [[0, 1]], 0, 1)
-    iota(W("cf"), [[1, 128]], 0)
+    iota(W("cfx"), [[1, 144]], -8)
     iota(W("cg"), [[1, 8], [0, 16]], 0)
     iota(W("cr"), [[0, 8], [1, 16]], 0)
     iota(W("c8"), [[0, 16], [1, 8]], 0)
-    for c in range(4):
-        iota(X("win", c * 512, c * 512 + 512), [[1, 512]], c * 512)
+    act(X("win", 0, 128), W("cf"), AF.Copy)
+    for c in (128, 256, 512, 1024):
+        act(X("win", c, 2 * c), X("win", 0, c), AF.Identity, bias=float(c))
     P_, G_, I_ = W("pf"), W("gf"), W("fi")
     vts(W("gi"), W("pi"), 4, None, AL.arith_shift_right)
     vcp(G_, W("gi"))
@@ -204,8 +212,10 @@ def program(g, core, T, topo):
     vts(W("mlo"), I_, 8.0, None, AL.is_lt)
     vts(W("ncorr"), I_, 8192.0, -122880.0, AL.mult, AL.add)
     vts(W("c1"), I_, 8192.0, -122879.5, AL.mult, AL.add)
-    for n, v in (("ibf", 1.0), ("negib", -1.0), ("bigi", 131072.0), ("i594", 594.0), ("dlo", W("mlo")), ("dhi", W("mhi")), ("i8k", 8192.0)):
+    for n, v in (("ibf", 1.0), ("negib", -1.0), ("bigi", 131072.0), ("i594", 594.0), ("i8k", 8192.0)):
         vts(W(n), W("cf"), P_, v, AL.is_equal, AL.mult)
+    for n, v in (("dl", W("mlo")), ("dh", W("mhi"))):
+        vts(W(n), W("cfx"), P_, v, AL.is_equal, AL.mult)
     for n, v in (("ind", 1.0), ("indl", W("mlo")), ("indh", W("mhi")), ("ind6", 592.0)):
         vts(W(n), W("cg"), G_, v, AL.is_equal, AL.mult)
     vts(W("ind6l"), W("indl"), 592.0, None, AL.mult)
@@ -249,9 +259,12 @@ def program(g, core, T, topo):
         vtt(W("da"), IX("nbi", 0, 2048, "la%d" % t, 56, 64), xa, AL.subtract)
         vtt(W("db"), IX("nbi", 0, 2048, "lb%d" % t, 0, 8), xb, AL.subtract)
         xm, d, nm = X("pb5", 0, 128), X("pb5", 128, 256), X("pb4", 0, 128)
-        lx, ld = [(W("dlo"), xa), (W("dhi"), xb)], [(W("dlo"), W("da")), (W("dhi"), W("db"))]
+        lo, up, hi, dw_ = X("dl", 8, 136), X("dl", 0, 128), X("dh", 8, 136), X("dh", 16, 144)
+        lx = [(0, lo, "xa%d" % t, 0), (0, hi, "xa%d" % t, 1), (64, lo, "xb%d" % t, 0), (64, hi, "xb%d" % t, 1)]
+        ld = [(0, lo, "da", 0), (0, up, "da", 1), (64, dw_, "db", 0), (64, hi, "db", 1)]
         for o, l in ((xm, lx), (nm, lx + ld), (d, ld)):
-            mm([(o, a, b, i == 0, i == len(l) - 1) for i, (a, b) in enumerate(l)])
+            bk, c0 = o[1][0][0], o[1][0][1]
+            mm([(X(bk, c0 + c, c0 + c + 64), a, X(b, par, 128, 2), i == 0, i == len(l) - 1) for i, (c, a, b, par) in enumerate(l)])
             if o is xm:
                 act(W("pm"), xm, AF.Identity, scale=4.0, bias=2.0)
                 act(W("cm"), xm, AF.Identity, scale=594.0, bias=-8388607.0)
@@ -262,49 +275,72 @@ def program(g, core, T, topo):
         vcp(W("h0%d" % t), W("hpi"))
         vts(W("pn0%d" % t), W("dn0%d" % t), 0.0, None, AL.is_equal)
 
-    rot = [0]
+    rot, line = [0], []
 
-    def records(x, hl, qx, nv, nc):
-        ch = [(a, min(a + 512, 2048)) for a in range(nv, 2048, 512)]
+    def inline(tot):
+        if tot == 2048 and OPT["line"]:
+            ops[-1]["mdep"] = line[-1:]
+            line.append(len(ops) - 1)
+
+    def records(x, hl, h0, qx, tot, nv, nc):
+        st = 2048 // tot
+        ch = [(max(b - 512, nv), b) for b in range(tot, nv, -512)][::-1]
         for a, b in ch:
-            act(X("xs" + x, a, b), IX("tab", 0, TW, hl, a // 16, b // 16), AF.Copy)
-        vtt(X("dif" + x, 0, nv), IX("tab", 0, TW, hl, 0, nv // 16), X(qx, 0, nv), AL.subtract)
-        if nc:
-            vts(X("ad" + x, 0, nc), X("dif" + x, 0, nc), 0.0, 2.0, AL.max, AL.mult)
+            act(X("xs" + x, a, b), IX("tab", 0, TW, hl, h0 + a // 16, h0 + b // 16), AF.Copy)
+            inline(tot)
+        vs = OPT["vs"] if tot == 2048 else 1
+        cut = [nv * j // vs // 32 * 32 for j in range(vs)] + [nv]
+        for a, b in zip(cut, cut[1:]):
+            vtt(X("dif" + x, a, b), IX("tab", 0, TW, hl, h0 + a // 16, h0 + b // 16), X(qx, a * st, b * st, st), AL.subtract)
+        rs_ = OPT["rsp"] if tot == 2048 else 1
+        for j in range(rs_ if nc else 0):
+            a, b = nc * j // rs_, nc * (j + 1) // rs_
+            vts(X("ad" + x, a, b), X("dif" + x, a, b), 0.0, 2.0, AL.max, AL.mult)
         if nv > nc:
             act(X("ad" + x, nc, nv), X("dif" + x, nc, nv), AF.Abs)
         for a, b in ch:
             rot[0] += 1
-            o = X("pb%d" % (6 + rot[0] % 2), 0, b - a)
-            mm([(o, W("negib"), X(qx, a, b), True, False)])
+            o = X("pb%d" % (5 + rot[0] % 3), 0, b - a)
+            mm([(o, W("negib"), X(qx, a * st, b * st, st), True, False)])
             mm([(o, W("ibf"), X("xs" + x, a, b), False, True)])
             act(X("ad" + x, a, b), o, AF.Abs)
+            inline(tot)
 
-    def keys(x, kb, pn, nc):
-        key = X(kb, 0, 128)
-        mm([(key, one1, X("cr", 0, 128, 1, (0, 1)), True, False)] + [(key, p, W("bigi"), False, False) for p in pn])
+    def keys(x, kb, pn, tot, nc):
+        m = tot // 16
+        key = X(kb, 0, 128, 1, (0, m))
+        mm([(key, X("oneb", 0, m, 1, (0, 1)), X("cr", 0, 128, 1, (0, 1)), True, False)] + [(key, p, W("bigi"), False, False) for p in pn])
         if nc:
             mm([(X(kb, k, 128, 16, (0, nc // 16)), X("dif" + x, k, nc, 16), W("ngk"), False, False) for k in range(16)])
-        mm([(X(kb, k, 128, 16), X("ad" + x, k, 2048, 16), W("gk"), False, k == 15) for k in range(16)])
+        cut = (0, 96, 128) if m == 128 and OPT["ksp"] else (0, m)
+        for a, b in zip(cut, cut[1:]):
+            mm([(X(kb, k, 128, 16, (a, b)), X("ad" + x, 16 * a + k, 16 * b, 16), W("gk"), False, k == 15 and b == m) for k in range(16)])
         return key
 
-    def choose(x, key, rs, d):
-        vscan(W("r" + x), W(rs), key, TOP, AL.max, AL.min)
-        vscan(REV("rr" + x), W(rs), REV("r" + x), TOP, AL.max, AL.min)
-        vtt(W("mk" + x), W("rr" + x), key, AL.is_equal)
-        m1 = X("pb%d" % (4 + "ab".index(x)), 0, 128)
-        mm([(m1, W("mk" + x), W("ibf"), True, True)])
-        vtt(W("w" + x), m1, d, AL.mult)
+    def choose(x, key, rs, d, m):
+        r, mk = X("r" + x, 0, 128, 1, (0, m)), X("mk" + x, 0, 128, 1, (0, m))
+        vscan(r, X(rs, 0, 128, 1, (0, m)), key, TOP, AL.max, AL.min)
+        vscan(REV("rr" + x, m), X(rs, 0, 128, 1, (0, m)), REV("r" + x, m), TOP, AL.max, AL.min)
+        vtt(mk, X("rr" + x, 0, 128, 1, (0, m)), key, AL.is_equal)
+        m1 = X("pb%d" % "ab".index(x), 256, 256 + m)
+        mm([(m1, mk, X("ibf", 0, m, 1, (0, m)), True, True)])
+        vtt(X("w" + x, 0, m), m1, d, AL.mult)
 
-    def after(x, src, t, a, ind, ind6):
+    def after(x, t, a):
         i = "ab".index(x)
-        bb, w, xo = X("pb%d" % (2 + i), 0, 128), W("w" + src), X("x%s%d" % (x, t), a * 128, a * 128 + 128)
+        bb, xo = X("pb%d" % (2 + i), 0, 128), X("x%s%d" % (x, t), a * 128, a * 128 + 128)
+
+        def sums(bk, c, ind):
+            if a:
+                mm([(X(bk, c, c + 128), W(ind), W("w" + x), False, True)])
+            else:
+                mm([(X(bk, c + par, c + 128, 2), W(ind + "lh"[par]), X("w" + x, 0, 64), False, par == 1) for par in range(2)])
         mm([(bb, W("ibf"), xo, True, False)])
-        mm([(bb, W(ind), w, False, True)])
+        sums("pb%d" % (2 + i), 0, "ind")
         if a < 4:
             cc = X("pb%d" % i, 128, 256)
             mm([(cc, X("crow", 0, 128, 1, (0, 2)), X("oneb", 0, 128, 1, (0, 2)), True, False), (cc, W("i594"), xo, False, False)])
-            mm([(cc, W(ind6), w, False, True)])
+            sums("pb%d" % i, 128, "ind6")
         vscan(W("sc" + x), W("dm"), bb, 0.0, AL.add, AL.max)
         last = X("sc" + x, 15, 128, 16)
         if x == "a" and a == 4:
@@ -316,12 +352,12 @@ def program(g, core, T, topo):
         if a < 3:
             act(X(("pa%d" if x == "a" else "pb_%d") % t, (a + 1) * 128, (a + 2) * 128), bb, AF.Identity, scale=4.0, bias=2.0)
 
-    def first(t):
-        records("a", "h0%d" % t, "qm", OPT["nv0"], OPT["nc0"])
-        key = keys("a", "pb0", [W("pn0%d" % t)], OPT["nc0"])
-        choose("a", key, "rs0", W("dn0%d" % t))
-        after("b", "a", t, 0, "indh", "ind6h")
-        after("a", "a", t, 0, "indl", "ind6l")
+    def first(x, t):
+        i = "ab".index(x)
+        records(x, "h0%d" % t, 64 * i, "qa" if x == "a" else "qb%d" % (t % 2), 1024, OPT["nv0"], OPT["nc0"])
+        key = keys(x, "pb%d" % i, [X("pn0%d" % t, 64 * i, 64 * i + 64)], 1024, OPT["nc0"])
+        choose(x, key, "rs0", X("dn0%d" % t, 64 * i, 64 * i + 64), 64)
+        after(x, t, 0)
 
     def step(x, t, a):
         i = "ab".index(x)
@@ -333,23 +369,25 @@ def program(g, core, T, topo):
         vts(W("hi" + x), W("zi" + x), 4, 4095, AL.arith_shift_right, AL.bitwise_and)
         vcp(W("hl" + x), W("hi" + x))
         nv, nc = (OPT["nvl"], OPT["ncl"]) if (x, a) == ("a", 4) else (OPT["nv"], OPT["nc"])
-        records(x, "hl" + x, "qa" if x == "a" else "qb%d" % (t % 2), nv, nc)
+        records(x, "hl" + x, 0, "qa" if x == "a" else "qb%d" % (t % 2), 2048, nv, nc)
         vtt(d, nb, xo, AL.subtract)
-        n, pd = min(a + 1, 4), "pb%d" % (4 + i)
+        n, pd = min(a + 1, 4), "pb4"
         for m in range(n):
             o = X(pd, m * 128, m * 128 + 128)
             mm([(o, W("ibf"), xo, True, False), (o, W("ibf"), d, False, True)])
-        vtt(X("pn" + x, 0, n * 128), X(xh, 0, n * 128), X(pd, 0, n * 128), AL.is_equal)
+        for c0 in range(0, n * 128, OPT["bw"]):
+            c1 = min(c0 + OPT["bw"], n * 128)
+            vtt(X("pn" + x, c0, c1), X(xh, c0, c1), X(pd, c0, c1), AL.is_equal)
         if a == 4:
             vts(X("pn" + x, 512, 640), d, 0.0, None, AL.is_equal)
-        key = keys(x, "pb%d" % i, [X("pn" + x, m * 128, m * 128 + 128) for m in range(a + 1)], nc)
-        choose(x, key, "rs", d)
-        after(x, x, t, a, "ind", "ind6")
+        key = keys(x, "pb%d" % i, [X("pn" + x, m * 128, m * 128 + 128) for m in range(a + 1)], 2048, nc)
+        choose(x, key, "rs", d, 128)
+        after(x, t, a)
         if x == "b" and a == 4:
             s = add("G", lambda: sendb(t), [X("lb%d" % t, 8, 48)], [], 1.0)
-            add("R", None, [], [X("la%d" % t, 8, 48)], 3.0, mdep=[s], sem="rb%d" % t, cnt=NB)
+            add("R", None, [], [X("la%d" % t, 8, 48)], OPT["rl"], mdep=[s], sem="rb%d" % t, cnt=NB)
 
-    LP, LV, LN, LA = 0, 18, 36, 54
+    LP, LV, LN, LA, LX, LH = 0, 20, 40, 60, 74, 94
 
     def late_constants():
         iota(W("selc"), [[0, 2048]], 0)
@@ -357,14 +395,19 @@ def program(g, core, T, topo):
             keep(X("selc", 129 * i, 129 * i + 113, 16), X("ind", 0, 128, 16), [[0, 8]], 0)
         iota(W("nsb"), [[0, 2048]], -1)
         keep(W("nsb"), W("nsb"), [[-1, 16], [-16, 8], [0, 16]], 1)
-        iota(W("lr"), [[0, 1088]], 48)
+        iota(X("lr", 0, 16 * LX), [[0, 16 * LX]], 48)
+        c = 0
+        for p0, n in ((0, 4), (1, 3), (2, 2), (3, 1), (0, 3), (0, 2), (0, 1)):
+            iota(X("lr", 16 * LX + c, 16 * LX + c + 20 * n), [[1, n], [4, 20]], p0)
+            iota(X("lr", 16 * LH + c, 16 * LH + c + 20 * n), [[1, n], [0, 10], [4, 2]], p0)
+            c += 20 * n
         byi, byj = [[1, 8], [-8, 5], [0, 5]], [[1, 8], [0, 5], [-8, 5]]
         for l, pat, base, tail in ((LP, byi, 88, ((0, 8, 8), (16, 32, 56), (48, 32, 0))), (LV, byj, 40, ((0, 8, 56), (16, 32, 64), (48, 32, 8))),
                                    (LN, byj, 32, ((0, 8, 64), (16, 24, 72), (48, 32, 16))), (LA, byi, 96, ())):
             iota(X("lr", 16 * l, 16 * l + 200), pat, base)
             iota(X("lr", 16 * l + 24, 16 * l + 200, 25), [[0, 8]], 48)
             for c, n, b in tail:
-                iota(X("lr", 16 * l + 200 + c, 16 * l + 200 + c + n), [[1, n]], b)
+                iota(X("lr", 16 * l + 224 + c, 16 * l + 224 + c + n), [[1, n]], b)
         iota(W("pack"), [[0, 8], [8, 5], [1, 5]], 0)
         iota(X("pack", 24, 200, 25), [[0, 8]], 63)
         vts(W("pack"), W("pack"), 16384.0, 8192.0, AL.mult, AL.add)
@@ -373,11 +416,10 @@ def program(g, core, T, topo):
             iota(X("thr", 8 + 8 * m, 16 + 8 * m), [[0, 8]], (5 - m) << 17)
         iota(X("thr", 48, 80), [[-16384, 4], [0, 8]], 4 << 14)
         vts(W("i7"), W("mhi"), -8.0, I_, AL.mult, AL.add)
-        vts(W("LH"), X("cf", 0, 6), 0.0, W("i7"), AL.mult, AL.add)
         vts(X("l6", 0, 6), X("cf", 0, 6), 3.0, 8.0, AL.is_ge, AL.mult)
         vts(W("LM"), X("l6", 0, 6), W("i7"), None, AL.add)
-        vts(W("de"), I_, 4112.0, None, AL.add)
-        vts(W("do"), I_, 4128.0, None, AL.add)
+        vts(X("l6", 0, 4), X("cf", 0, 4), 16.0, 4112.0, AL.mult, AL.add)
+        vts(W("du"), X("l6", 0, 4), I_, None, AL.add)
         dd = X("cf", 1, 9)
         vts(W("s8a"), dd, I_, 16.0, AL.is_gt, AL.mult)
         vtt(W("s8b"), W("s8a"), dd, AL.subtract)
@@ -404,81 +446,100 @@ def program(g, core, T, topo):
         vms(X("xa", 640, 768), -1.0)
 
     def tolist():
-        o = X("pb5", 0, 68)
-        mm([(o, X("selc", 128 * i, 128 * i + 128), X("lr", i, 1088, 16), i == 0, i == 15) for i in range(16)])
+        o = X("pb5", 0, NL)
+        mm([(o, X("selc", 128 * i, 128 * i + 128), X("lr", i, 16 * NL, 16), i == 0, i == 15) for i in range(16)])
         vts(W("LL"), o, 0.0625, None, AL.mult)
 
     def join_early(t):
         vts(X("aw", 0, 96), X("la%d" % t, 0, 96), 2.0, 1.0, AL.mult, AL.add)
-        act(W("narr"), IX("aw", 0, 96, "LL", LN, LN + 18), AF.Copy)
-        act(W("varr"), IX("aw", 0, 96, "LL", LV, LV + 18), AF.Identity, scale=296.0, bias=CB)
-        act(W("bj"), IX("aw", 0, 96, "LL", LV, LV + 13), AF.Copy)
-        vtt(W("tj"), IX("aw", 0, 96, "LL", LP, LP + 18), W("narr"), AL.mult)
-        vtt(X("zj", 0, 280), X("tj", 0, 280), X("varr", 0, 280), AL.add)
-        vts(X("hji", 0, 280), X("zj", 0, 280), 4, 4095, AL.arith_shift_right, AL.bitwise_and)
-        vtt(W("hp"), X("hji", 0, 200), W("pack"), AL.add)
+        for a, b, n in ((0, 13, 200), (14, 19, 80)):
+            c, d = 16 * a, 16 * b
+            act(X("narr", c, d), IX("aw", 0, 96, "LL", LN + a, LN + b), AF.Copy)
+            act(X("varr", c, d), IX("aw", 0, 96, "LL", LV + a, LV + b), AF.Identity, scale=296.0, bias=CB)
+            vtt(X("tj", c, d), IX("aw", 0, 96, "LL", LP + a, LP + b), X("narr", c, d), AL.mult)
+            vtt(X("zj", c, c + n), X("tj", c, c + n), X("varr", c, c + n), AL.add)
+            vts(X("hji", c, c + n), X("zj", c, c + n), 4, 4095, AL.arith_shift_right, AL.bitwise_and)
+            if a == 0:
+                act(W("bj"), IX("aw", 0, 96, "LL", LV, LV + 13), AF.Copy)
+                vtt(W("hp"), X("hji", 0, 200), W("pack"), AL.add)
 
     def join(t):
         vtt(W("eq"), IX("aw", 0, 104, "LL", LA, LA + 13), W("bj"), AL.is_equal)
         act(X("neq", 0, 200), X("eq", 0, 200), AF.Identity, scale=-1.0, bias=1.0)
         vtt(W("ek"), X("eq", 0, 200), W("hp"), AL.mult)
         vtt(W("t8"), X("aw", 96, 104), X("aw", 80, 88), AL.mult)
-        vtt(W("z8"), W("t8"), X("varr", 240, 248), AL.add)
-        vts(X("hji", 240, 248), W("z8"), 4, 4095, AL.arith_shift_right, AL.bitwise_and)
+        vtt(W("z8"), W("t8"), X("varr", 264, 272), AL.add)
+        vts(X("hji", 264, 272), W("z8"), 4, 4095, AL.arith_shift_right, AL.bitwise_and)
         vscan(W("scj"), X("neq", 0, 200), W("ek"), NONE, AL.mult, AL.add)
         vcp(X("w16", 0, 8), X("scj", 23, 200, 25))
         vts(X("w16", 8, 16), X("w16", 0, 8), (1 << 17) - 1, None, AL.bitwise_and)
-        vts(X("hji", 208, 216), X("w16", 0, 8), 4095, None, AL.bitwise_and)
+        vts(X("hji", 232, 240), X("w16", 0, 8), 4095, None, AL.bitwise_and)
         vtt(W("aa"), IX("w16", 0, 16, "LM", 0, 5), W("thr"), AL.subtract)
-        vtt(W("bb"), W("aa"), X("hji", 200, 280), AL.max)
+        vtt(W("bb"), W("aa"), X("hji", 224, 304), AL.max)
         vts(W("off"), W("bb"), 4096.0, None, AL.min)
-        vts(W("hm"), W("bb"), 4160.0, -2048.0, AL.min, AL.add)
+        vts(W("hm"), IX("bb", 0, 80, "LL", LX, LX + 20), 4192.0, -2048.0, AL.min, AL.add)
 
     def lessen(t):
         xv = OPT["xv"]
         act(X("xr", xv, 1280), IX("tab", 0, TW, "off", xv // 16, 80), AF.Copy)
+        mark.append(len(ops) - 1)
         vcp(X("xr", 0, xv), IX("tab", 0, TW, "off", 0, xv // 16))
         tot, cnt = X("pb0", 0, 128), X("pb1", 0, 8)
         for k in range(10):
             mm([(tot, W("ibf"), X("xr", k * 128, k * 128 + 128), k == 0, k == 9)])
         vts(W("ge"), tot, W("thf"), None, AL.is_ge)
         mm([(cnt, X("selc", 128 * i, 128 * i + 128), X("ge", i, 128, 16), i == 0, i == 15) for i in range(16)])
-        vts(W("u8"), cnt, -8.5, -4200.0, AL.add, AL.mult)
-        vtt(W("rep"), IX("u8", 0, 8, "LH", 0, 5), W("hm"), AL.max)
-        for c in range(0, 1280, 320):
-            act(X("nd1", c, c + 320), X("xr", c, c + 320), AF.Identity, scale=-0.25, bias=-191.625)
-            act(X("nd", c, c + 320), X("nd1", c, c + 320), AF.Identity, bias=192.0)
-        rep, re_, ro = W("rep"), X("rep", 0, 80, 2), X("rep", 1, 80, 2)
-        z = X("pb5", 0, 80)
-        mm([(z, W("ibf"), rep, True, False)])
+        vts(W("u8"), cnt, -8.5, -4400.0, AL.add, AL.mult)
+        vtt(W("rep"), IX("u8", 0, 8, "LL", LH, LH + 20), W("hm"), AL.max)
+        for c in range(0, 1280, 128):
+            vts(X("nd1", c, c + 128), X("xr", c, c + 128), -0.25, -191.625, AL.mult, AL.add)
+            vts(X("nd", c, c + 128), X("nd1", c, c + 128), 192.0, None, AL.add)
+        rep = X("rep", 0, 80)
+        mm([(X("pb5", 0, 80), W("ibf"), rep, True, False)])
         c0 = 0
-        for bk, within, cross in (("pb6", range(6), ()), ("pb7", range(6, 8), range(8)), ("pb4", (), range(8, 16))):
+        parts = (("pb6", range(6), ()), ("pb7", (), range(4)), ("pb4", (), range(4, 8)), ("pb2", (), range(8, 12)), ("pb0", (), range(12, 16)),
+                 ("pb1", range(6, 8), ()))
+        for j, (bk, within, cross) in enumerate(parts):
             l, s, c = [], [], 0
             for d in within:
                 l.append((X(bk, c, c + 80), X("dw", d * 128, d * 128 + 128), rep, True, True))
-                s.append((z, X("tg", d * 128, d * 128 + 128), X("fl2", c0 + c, c0 + c + 80), False, False))
+                s.append((X("pb5", 0, 80), X("tg", d * 128, d * 128 + 128), X("fl2", c0 + c, c0 + c + 80), False, d == 7))
                 c += 80
             for i in cross:
-                l += [(X(bk, c, c + 40), W("ibf"), ro, True, False), (X(bk, c, c + 40), X("nsb", i * 128, i * 128 + 128), re_, False, True)]
-                s.append((X("pb5", 1, 80, 2), W("i8k"), X("fl2", c0 + c, c0 + c + 40), False, i == 15))
-                c += 40
+                o = X(bk, c, c + 120)
+                l += [(o, W("ibf"), X("rep", 80, 200), True, False), (o, X("nsb", i * 128, i * 128 + 128), X("rep", 200, 320), False, True)]
+                s += [(X("pb5", a, 80), W("i8k"), X("fl2", c0 + c + b, c0 + c + b + 80 - a), False, False) for a, b in ((20, 0), (40, 60), (60, 100))]
+                c += 120
             mm(l)
-            vts(X("fl2", c0, c0 + c), X(bk, 0, c), 0.0, None, AL.is_equal)
-            mm(s)
+            if j < OPT["ns"]:
+                act(X("ab2", c0, c0 + c), X(bk, 0, c), AF.Abs)
+                act(X("fl2", c0, c0 + c), X("ab2", c0, c0 + c), AF.Relu, scale=-1.0, bias=1.0)
+            else:
+                vts(X("fl2", c0, c0 + c), X(bk, 0, c), 0.0, None, AL.is_equal)
+            late.append(s)
+            if j >= OPT["ns"]:
+                mm(late.pop())
             c0 += c
-        vts(X("offs", 0, 80, 2), X("pb5", 0, 80, 2), 2048.0, W("de"), AL.add, AL.min)
-        vts(X("offs", 1, 80, 2), X("pb5", 1, 80, 2), 2048.0, W("do"), AL.add, AL.min)
-        for u in range(40):
-            o = IX("tab", 0, TW, "offs", 2 * u, 2 * u + 2)
-            a, b, l = X("xr", 32 * u, 32 * u + 32), X("nd", 32 * u, 32 * u + 32), X("offs", 2 * u, 2 * u + 2)
-            add("V", lambda o=o, a=a, b=b: [g.vector.tensor_tensor(out=o[0], in0=a[0], in1=b[0], op=AL.add)], [a, b, l], [X("tab", 0, TW)], .15)
+            if j == 4:
+                while late:
+                    mm(late.pop())
+        for c in range(4):
+            vts(X("offs", c, 80, 4), X("pb5", 20 * c, 20 * c + 20), 2048.0, X("du", c, c + 1), AL.add, AL.min)
+        for u in range(20):
+            o = IX("tab", 0, TW, "offs", 4 * u, 4 * u + 4)
+            a, b, l = X("xr", 64 * u, 64 * u + 64), X("nd", 64 * u, 64 * u + 64), X("offs", 4 * u, 4 * u + 4)
+            add("V", lambda o=o, a=a, b=b: [g.vector.tensor_tensor(out=o[0], in0=a[0], in1=b[0], op=AL.add)], [a, b, l], [X("tab", 0, TW)], .25)
         if t == RO - 1:
             dma((T.ye[:], [], 0), X("tab", 0, 4096), 6.0)
+
+    mark, late = [], []
 
     def rings(t):
         la = "la%d" % t
         act(X("xa", 0, 640), IX("win", 0, 2048, la, 8, 48), AF.Copy)
+        ops[-1]["mdep"] = [mark[-1]]
         act(X("xa", 768, 1536), IX("win", 0, 2048, la, 56, 104), AF.Copy)
+        ops[-1]["mdep"] = [mark[-1]]
         vts(W("c8i"), X("w16", 0, 8), 14, None, AL.arith_shift_right)
         vcp(W("fl"), W("c8i"))
         vtt(W("of"), IX("tw", 0, 64, "fl", 0, 8), W("cf"), AL.add)
@@ -491,17 +552,21 @@ def program(g, core, T, topo):
         act(W("yo"), y, AF.Copy, scale=0.0625)
         dma((T.yr[:, t * 128:t * 128 + 128], [], 0), W("yo"))
 
-    spread("V", "qm", 0, range(8))
     spread("S", "qa", 0, range(16))
-    spread("V", "qm", 1, range(8, 16))
-    spread("G", "qb0", 1, range(16))
-    for t in range(RO):
-        prep(t)
+    spread("V", "qb0", 1, range(0, 16, 2))
+    spread("G", "qb0", 1, range(1, 16, 2))
+    prep(0)
+    i0 = len(ops)
     late_constants()
+    for o in ops[i0:]:
+        if o["e"] == "G":
+            o["mdep"] = sent[-1:]
     for t in range(RO):
-        first(t)
+        first("b", t)
+        first("a", t)
         if t + 1 < RO:
-            spread("G", "qm", t + 2, range(8, 16))
+            if OPT["pp"] == 0:
+                prep(t + 1)
             spread("G", "qb%d" % ((t + 1) % 2), t + 2, range(16))
         for a in range(1, 5):
             step("b", t, a)
@@ -510,13 +575,15 @@ def program(g, core, T, topo):
                     tolist()
                 join_early(t)
             step("a", t, a)
+        if OPT["pp"] == 1 and t + 1 < RO:
+            prep(t + 1)
         join(t)
         lessen(t)
         rings(t)
 
     def meets(x, y):
         (lo, hi, s), (l2, h2, s2) = x, y
-        return l2 < hi and lo < h2 and (s != s2 or (lo - l2) % s == 0)
+        return l2 < hi and lo < h2 and (lo - l2) % math.gcd(s, s2) == 0
 
     n = len(ops)
     pred = [[] for _ in range(n)]
@@ -548,7 +615,7 @@ def program(g, core, T, topo):
         succ = [[] for _ in range(n)]
         npd = [0] * n
         for i, o in enumerate(ops):
-            for j, need in pred[i] + [(j, True) for j in o.get("mdep", ())]:
+            for j, need in pred[i] + [(j, ops[j]["e"] != o["e"]) for j in o.get("mdep", ())]:
                 succ[j].append((i, lam if need else 0.0))
                 npd[i] += 1
         pr = [0.0] * n
@@ -561,11 +628,43 @@ def program(g, core, T, topo):
             if npd[i] == 0:
                 cand[ops[i]["e"]].append(i)
         order = []
+
+        def soon(e, s):
+            out = [(ready[x], x) for x in cand[e] if ready[x] > s]
+            front = [(max(free[q], ready[x], s) + ops[x]["c"] + ops[x].get("lat", 0), x) for q in cand if q != e for x in cand[q]]
+            for _ in range(2):
+                nxt = []
+                for fin, x in front:
+                    for j, w in succ[x]:
+                        if npd[j] == 1 and fin < s + 1.5:
+                            r = max(ready[j], fin + w)
+                            if ops[j]["e"] == e:
+                                out.append((r, j))
+                            else:
+                                nxt.append((max(r, free[ops[j]["e"]]) + ops[j]["c"], j))
+                front = nxt
+            return out
+
         while len(order) < n:
             s, e = min((min(ready[i] for i in l) if e == "R" else max(free[e], min(ready[i] for i in l)), e) for e, l in cand.items() if l)
-            i = max((x for x in cand[e] if ready[x] <= s), key=lambda x: (pr[x], -x))
+            s += 1e-6
+            now = sorted((x for x in cand[e] if ready[x] <= s), key=lambda x: (-pr[x], x))
+            i = now[0]
+            if OPT["look"] and e in "VSP":
+                nx = [(r, j) for r, j in soon(e, s) if pr[j] > pr[i]]
+
+                def late_by(x, t0):
+                    t1 = t0 + ops[x]["c"]
+                    return max([t0 + pr[x]] + [t1 + pr[j] for j in now[:2] if j != x] + [max(r, t1) + pr[j] for r, j in nx if j != x])
+                if nx:
+                    i = min(now[:6], key=lambda x: (round(late_by(x, s) / OPT["look"]), -pr[x]))
+                    r, j = min(nx, key=lambda y: late_by(y[1], y[0]))
+                    if late_by(j, r) + OPT["look"] < late_by(i, s):
+                        free[e] = min(r, s + .03)
+                        continue
             cand[e].remove(i)
             order.append(i)
+            CACHE.setdefault("log", []).append((s, e, ops[i]["c"], pr[i], i))
             free[e] = s + ops[i]["c"]
             fin = s + ops[i]["c"] + ops[i].get("lat", 0)
             for j, w in succ[i]:

@@ -18,7 +18,7 @@ def _sb(dtype, **kw):
         SIZE[dtype] += (n + 31) // 32 * 32
 
 
-NL = 114
+NL = 128
 _sb(B, tab=TW, qa=2048, qb0=2048, qb1=2048, qw=512, cfx=144, cg=128, cr=128, c8=128, ibf=128, negib=128, bigi=128, ind=128, indl=128,
     indh=128, ind6=128, ind6l=128, ind6h=128, dl=144, dh=144, gk=8, ngk=8, oneb=128, crow=128, selc=2048, nsb=2048, dw=1024, tg=1024,
     i8k=128, fl2=2560, ab2=2560, xr=1280, nd1=1280, nd=1280, lr=16 * NL, ge=128)
@@ -27,7 +27,7 @@ _sb(H, i594=128, da=128, db=128, rep=320, gy=2048)
 _sb(F, win=2048, xa=1536, pf=1, gf=1, fi=1, mlo=1, mhi=1, ncorr=1, c1=1, i7=1, du=4, thf=1, rs=128, rs0=128, dm=128,
     s8a=8, s8b=8, src8=8, tgt8=8, l6=8, pack=200, thr=80, fI=64, fL=64, t1w=64, t2w=64, t3w=64, tw=64,
     pm=128, cm=128, tp=128, aw=104, narr=320, varr=320, bj=208, tj=320, hp=200, eq=208, neq=208, ek=200, scj=200,
-    t8=8, aa=80, bb=80, hm=320, u8=8, of=128, yo=128)
+    t8=8, t9=8, i5=1, aa=80, bb=80, hm=320, u8=8, of=128, yo=128)
 _sb(I32, nbi=2048, sti=64, stin0=64, stin1=64, stin2=64, pi=1, gi=1, thi=1, zpi=128, hpi=128, hji=320, zj=320, z8=8, w16=16, c8i=8)
 _sb(U16, LL=NL, LM=6, off=80, offs=80, fl=8, ofu=128)
 for _x in "ab":
@@ -39,7 +39,7 @@ for _x in "ab":
 for _t in range(RO):
     _sb(B, **{"pn0%d" % _t: 128})
     _sb(H, **{"xa%d" % _t: 640, "xb%d" % _t: 640, "dn0%d" % _t: 128})
-    _sb(F, **{"pa%d" % _t: 512, "pb_%d" % _t: 512})
+    _sb(F, **{"pa%d" % _t: 512, "pb_%d" % _t: 512, "aw%d" % _t: 104, "b5%d" % _t: 8})
     _sb(U16, **{"h0%d" % _t: 128, "la%d" % _t: 104, "lb%d" % _t: 48})
 SCRATCH = {PHYS[d]: ("sbuf", [128, SIZE[d]], d) for d in PHYS}
 for _i in range(8):
@@ -47,13 +47,15 @@ for _i in range(8):
     VB["pb%d" % _i] = ("pb%d" % _i, 0, 512)
 NDMA = 12
 SEMAPHORES = ["sV", "sS", "sP", "sG", "ls"] + ["d%d" % i for i in range(NDMA)] + ["rq%d" % i for i in range(RO)] + \
-    ["rs%d" % i for i in range(RO)] + ["rb%d" % i for i in range(RO)]
+    ["rs%d" % i for i in range(RO)] + ["rb%d" % i for i in range(RO)] + ["rc%d" % i for i in range(RO)]
 CACHE = {}
 BIG = 16777216.0
 TOP = 100000.0
 CB = -296.0 - 8388608.0
 NONE = 63 * 16384.0 + 8192.0
-OPT = dict(nv=640, nc=640, nv0=512, nc0=512, nvl=1024, ncl=1024, gat=1.56, lam=.15, xv=640, ns=1, vs=3, ksp=0, look=.05, rl=3.0, rsp=1, bw=512, line=1, pp=1)
+OPT = dict(nv=640, nc=640, nv0=(512, 640), nvl=1024, ncl=1024, gat=1.56, lam=.15, ns=(0, 3), vs=3, ksp=0, look=.08, rl=4.0, rsp=1, bw=512, line=1, pp=2, ps=2.0,
+           passes=1, mix=.3, cut=(96, 96, 256, 96, 96), cutl=(96, 96, 256, 128, 192), halves=9, penl=0,
+           weave="xdn ymin xg0 yback xg1 yeq xg2 yw xb0 ysc xg3 yvl xg4 zt1 xr0 zzi xr1 zhi zhl")
 
 
 def program(g, core, T, topo):
@@ -170,13 +172,13 @@ def program(g, core, T, topo):
         g.remote_dma_fused(tr, local_sem=T.sem.ls)
         return []
 
-    def sendb(t):
+    def sendb(t, dst, src, sem):
         a = topo.addr(back[t])
-        g.remote_dma(out_ap=X("la%d" % t, 8, 48)[0], in_ap=X("lb%d" % t, 8, 48)[0], remote_sem=T.sem["rb%d" % t], local_sem=T.sem.ls,
+        g.remote_dma(out_ap=dst[0], in_ap=src[0], remote_sem=T.sem[sem], local_sem=T.sem.ls,
                      pid=a[1], routing_id=a[0], dma_engine_mask=engs(back[t], 0, NB))
         return []
 
-    lsn = 2 * sum(NE) + NB * RO
+    lsn = 2 * sum(NE) + 2 * NB * RO
 
     dma(X("sti", 0, 24), ext("st"), 2.0)
     dma(X("qw", 0, 128), ext("q"), 2.0)
@@ -234,8 +236,8 @@ def program(g, core, T, topo):
     for t in range(RO):
         la = "la%d" % t
         vcp(X(la, 0, 8), X("sti", 8 * t, 8 * t + 8))
-        vms(X(la, 48, 56), 0)
-        vcp(X(la, 56, 64), X("sti", 8 * t, 8 * t + 8))
+        vms(X(la, 40, 96), 0)
+        vcp(X(la, 48, 56), X("sti", 8 * t, 8 * t + 8))
         vcp(X("lb%d" % t, 0, 8), X("stin%d" % t, 8 * t, 8 * t + 8))
     one1 = X("oneb", 0, 128, 1, (0, 1))
 
@@ -250,13 +252,13 @@ def program(g, core, T, topo):
                 act(o, a, AF.Copy)
 
     def prep(t):
-        la, lb = IX("win", 0, 2048, "la%d" % t, 56, 64), IX("win", 0, 2048, "lb%d" % t, 0, 8)
+        la, lb = IX("win", 0, 2048, "la%d" % t, 48, 56), IX("win", 0, 2048, "lb%d" % t, 0, 8)
         xa, xb = X("xa%d" % t, 0, 128), X("xb%d" % t, 0, 128)
         act(xa, la, AF.Copy)
         act(xb, lb, AF.Copy)
         act(X("pa%d" % t, 0, 128), la, AF.Identity, scale=4.0, bias=2.0)
         act(X("pb_%d" % t, 0, 128), lb, AF.Identity, scale=4.0, bias=2.0)
-        vtt(W("da"), IX("nbi", 0, 2048, "la%d" % t, 56, 64), xa, AL.subtract)
+        vtt(W("da"), IX("nbi", 0, 2048, "la%d" % t, 48, 56), xa, AL.subtract)
         vtt(W("db"), IX("nbi", 0, 2048, "lb%d" % t, 0, 8), xb, AL.subtract)
         xm, d, nm = X("pb5", 0, 128), X("pb5", 128, 256), X("pb4", 0, 128)
         lo, up, hi, dw_ = X("dl", 8, 136), X("dl", 0, 128), X("dh", 8, 136), X("dh", 16, 144)
@@ -275,11 +277,14 @@ def program(g, core, T, topo):
         vcp(W("h0%d" % t), W("hpi"))
         vts(W("pn0%d" % t), W("dn0%d" % t), 0.0, None, AL.is_equal)
 
-    rot, line = [0], []
+    rot, line, tags, at = [0], [], {}, [None]
+
+    def tag(name):
+        tags[at[0] + (name,)] = len(ops) - 1
 
     def inline(tot):
-        if tot == 2048 and OPT["line"]:
-            ops[-1]["mdep"] = line[-1:]
+        ops[-1]["mdep"] = line[-1:]
+        if tot == 2048:
             line.append(len(ops) - 1)
 
     def records(x, hl, h0, qx, tot, nv, nc):
@@ -288,14 +293,16 @@ def program(g, core, T, topo):
         for a, b in ch:
             act(X("xs" + x, a, b), IX("tab", 0, TW, hl, h0 + a // 16, h0 + b // 16), AF.Copy)
             inline(tot)
-        vs = OPT["vs"] if tot == 2048 else 1
-        cut = [nv * j // vs // 32 * 32 for j in range(vs)] + [nv]
-        for a, b in zip(cut, cut[1:]):
+        cut = [0]
+        for w in (OPT["cut"] if nv == sum(OPT["cut"]) and tot == 2048 else OPT["cutl"] if tot == 2048 else (nv,)):
+            cut.append(cut[-1] + w)
+        for j, (a, b) in enumerate(zip(cut, cut[1:])):
             vtt(X("dif" + x, a, b), IX("tab", 0, TW, hl, h0 + a // 16, h0 + b // 16), X(qx, a * st, b * st, st), AL.subtract)
-        rs_ = OPT["rsp"] if tot == 2048 else 1
-        for j in range(rs_ if nc else 0):
-            a, b = nc * j // rs_, nc * (j + 1) // rs_
+            tag("g%d" % j)
+        cut = (0, cut[len(cut) // 2], nc) if tot == 2048 else (0, nc)
+        for j, (a, b) in enumerate(zip(cut, cut[1:])):
             vts(X("ad" + x, a, b), X("dif" + x, a, b), 0.0, 2.0, AL.max, AL.mult)
+            tag("r%d" % j)
         if nv > nc:
             act(X("ad" + x, nc, nv), X("dif" + x, nc, nv), AF.Abs)
         for a, b in ch:
@@ -309,22 +316,31 @@ def program(g, core, T, topo):
     def keys(x, kb, pn, tot, nc):
         m = tot // 16
         key = X(kb, 0, 128, 1, (0, m))
-        mm([(key, X("oneb", 0, m, 1, (0, 1)), X("cr", 0, 128, 1, (0, 1)), True, False)] + [(key, p, W("bigi"), False, False) for p in pn])
+        mm([(key, X("oneb", 0, m, 1, (0, 1)), X("cr", 0, 128, 1, (0, 1)), True, False)])
+        e = len(pn) - (min(OPT["penl"], len(pn)) if m == 128 else 0)
+        if e:
+            mm([(key, p, W("bigi"), False, False) for p in pn[:e]])
         if nc:
             mm([(X(kb, k, 128, 16, (0, nc // 16)), X("dif" + x, k, nc, 16), W("ngk"), False, False) for k in range(16)])
         cut = (0, 96, 128) if m == 128 and OPT["ksp"] else (0, m)
         for a, b in zip(cut, cut[1:]):
-            mm([(X(kb, k, 128, 16, (a, b)), X("ad" + x, 16 * a + k, 16 * b, 16), W("gk"), False, k == 15 and b == m) for k in range(16)])
+            mm([(X(kb, k, 128, 16, (a, b)), X("ad" + x, 16 * a + k, 16 * b, 16), W("gk"), False, k == 15 and b == m and e == len(pn)) for k in range(16)])
+        for p in pn[e:]:
+            mm([(key, p, W("bigi"), False, p is pn[-1])])
         return key
 
     def choose(x, key, rs, d, m):
         r, mk = X("r" + x, 0, 128, 1, (0, m)), X("mk" + x, 0, 128, 1, (0, m))
         vscan(r, X(rs, 0, 128, 1, (0, m)), key, TOP, AL.max, AL.min)
+        tag("min")
         vscan(REV("rr" + x, m), X(rs, 0, 128, 1, (0, m)), REV("r" + x, m), TOP, AL.max, AL.min)
+        tag("back")
         vtt(mk, X("rr" + x, 0, 128, 1, (0, m)), key, AL.is_equal)
+        tag("eq")
         m1 = X("pb%d" % "ab".index(x), 256, 256 + m)
         mm([(m1, mk, X("ibf", 0, m, 1, (0, m)), True, True)])
         vtt(X("w" + x, 0, m), m1, d, AL.mult)
+        tag("w")
 
     def after(x, t, a):
         i = "ab".index(x)
@@ -342,11 +358,16 @@ def program(g, core, T, topo):
             mm([(cc, X("crow", 0, 128, 1, (0, 2)), X("oneb", 0, 128, 1, (0, 2)), True, False), (cc, W("i594"), xo, False, False)])
             sums("pb%d" % i, 128, "ind6")
         vscan(W("sc" + x), W("dm"), bb, 0.0, AL.add, AL.max)
+        tag("sc")
         last = X("sc" + x, 15, 128, 16)
         if x == "a" and a == 4:
             vts(X("aw", 96, 104), last, W("c1"), 2.0, AL.add, AL.mult)
-        c = 64 + 8 * a if x == "a" else 8 + 8 * a
-        vts(X("l%s%d" % (x, t), c, c + 8), last, W("ncorr"), None, AL.add)
+        c = 8 + 8 * a if x == "b" else 56 + 8 * a if a < 4 else 96
+        if (x, a) == ("b", 4):
+            vts(W("b5%d" % t), last, W("c1"), 2.0, AL.add, AL.mult)
+        else:
+            vts(X("l%s%d" % (x, t), c, c + 8), last, W("ncorr"), None, AL.add)
+        tag("vl")
         if a < 4:
             act(X("x%s%d" % (x, t), (a + 1) * 128, (a + 2) * 128), bb, AF.Copy)
         if a < 3:
@@ -354,23 +375,30 @@ def program(g, core, T, topo):
 
     def first(x, t):
         i = "ab".index(x)
-        records(x, "h0%d" % t, 64 * i, "qa" if x == "a" else "qb%d" % (t % 2), 1024, OPT["nv0"], OPT["nc0"])
-        key = keys(x, "pb%d" % i, [X("pn0%d" % t, 64 * i, 64 * i + 64)], 1024, OPT["nc0"])
+        at[0] = (x, t, 0)
+        records(x, "h0%d" % t, 64 * i, "qa" if x == "a" else "qb%d" % (t % 2), 1024, OPT["nv0"][i], OPT["nv0"][i])
+        key = keys(x, "pb%d" % i, [X("pn0%d" % t, 64 * i, 64 * i + 64)], 1024, OPT["nv0"][i])
         choose(x, key, "rs0", X("dn0%d" % t, 64 * i, 64 * i + 64), 64)
         after(x, t, 0)
 
     def step(x, t, a):
         i = "ab".index(x)
-        xh, c = "x%s%d" % (x, t), (56 if x == "a" else 0) + 8 * a
+        xh, c = "x%s%d" % (x, t), (48 if x == "a" else 0) + 8 * a
         nb = IX("nbi", 0, 2048, "l%s%d" % (x, t), c, c + 8)
         xo, d = X(xh, a * 128, a * 128 + 128), W("dn" + x)
+        at[0] = (x, t, a)
         vtt(W("t1" + x), nb, X(("pa%d" if x == "a" else "pb_%d") % t, (a - 1) * 128, a * 128), AL.mult)
+        tag("t1")
         vtt(W("zi" + x), W("t1" + x), X("pb%d" % i, 128, 256), AL.add)
+        tag("zi")
         vts(W("hi" + x), W("zi" + x), 4, 4095, AL.arith_shift_right, AL.bitwise_and)
+        tag("hi")
         vcp(W("hl" + x), W("hi" + x))
-        nv, nc = (OPT["nvl"], OPT["ncl"]) if (x, a) == ("a", 4) else (OPT["nv"], OPT["nc"])
+        tag("hl")
+        nv = nc = sum(OPT["cutl"] if (x, a) == ("a", 4) else OPT["cut"])
         records(x, "hl" + x, 0, "qa" if x == "a" else "qb%d" % (t % 2), 2048, nv, nc)
         vtt(d, nb, xo, AL.subtract)
+        tag("dn")
         n, pd = min(a + 1, 4), "pb4"
         for m in range(n):
             o = X(pd, m * 128, m * 128 + 128)
@@ -378,16 +406,19 @@ def program(g, core, T, topo):
         for c0 in range(0, n * 128, OPT["bw"]):
             c1 = min(c0 + OPT["bw"], n * 128)
             vtt(X("pn" + x, c0, c1), X(xh, c0, c1), X(pd, c0, c1), AL.is_equal)
+            tag("b%d" % (c0 // OPT["bw"]))
         if a == 4:
             vts(X("pn" + x, 512, 640), d, 0.0, None, AL.is_equal)
         key = keys(x, "pb%d" % i, [X("pn" + x, m * 128, m * 128 + 128) for m in range(a + 1)], 2048, nc)
         choose(x, key, "rs", d, 128)
         after(x, t, a)
-        if x == "b" and a == 4:
-            s = add("G", lambda: sendb(t), [X("lb%d" % t, 8, 48)], [], 1.0)
-            add("R", None, [], [X("la%d" % t, 8, 48)], OPT["rl"], mdep=[s], sem="rb%d" % t, cnt=NB)
+        if x == "b" and a >= 3:
+            dst, src, sem = (X("la%d" % t, 8, 40), X("lb%d" % t, 8, 40), "rb%d" % t) if a == 3 else \
+                (X("aw", 88, 96), W("b5%d" % t), "rc%d" % t)
+            s = add("G", lambda: sendb(t, dst, src, sem), [src], [], 1.0)
+            add("R", None, [], [dst], OPT["rl"], mdep=[s], sem=sem, cnt=NB)
 
-    LP, LV, LN, LA, LX, LH = 0, 20, 40, 60, 74, 94
+    LP, LV, LN, LA, LB, LX, LH = 0, 20, 40, 60, 74, 88, 108
 
     def late_constants():
         iota(W("selc"), [[0, 2048]], 0)
@@ -395,28 +426,35 @@ def program(g, core, T, topo):
             keep(X("selc", 129 * i, 129 * i + 113, 16), X("ind", 0, 128, 16), [[0, 8]], 0)
         iota(W("nsb"), [[0, 2048]], -1)
         keep(W("nsb"), W("nsb"), [[-1, 16], [-16, 8], [0, 16]], 1)
-        iota(X("lr", 0, 16 * LX), [[0, 16 * LX]], 48)
+        iota(X("lr", 0, 16 * LX), [[0, 16 * LX]], 40)
         c = 0
-        for p0, n in ((0, 4), (1, 3), (2, 2), (3, 1), (0, 3), (0, 2), (0, 1)):
-            iota(X("lr", 16 * LX + c, 16 * LX + c + 20 * n), [[1, n], [4, 20]], p0)
-            iota(X("lr", 16 * LH + c, 16 * LH + c + 20 * n), [[1, n], [0, 10], [4, 2]], p0)
-            c += 20 * n
+        for h in range(2):
+            for p0, n in ((0, 4), (1, 3), (2, 2), (3, 1), (0, 3), (0, 2), (0, 1)):
+                iota(X("lr", 16 * LX + c, 16 * LX + c + 10 * n), [[1, n], [4, 10]], p0 + 40 * h)
+                iota(X("lr", 16 * LH + c, 16 * LH + c + 10 * n), [[1, n], [0, 5], [4, 2]], p0)
+                c += 10 * n
         byi, byj = [[1, 8], [-8, 5], [0, 5]], [[1, 8], [0, 5], [-8, 5]]
-        for l, pat, base, tail in ((LP, byi, 88, ((0, 8, 8), (16, 32, 56), (48, 32, 0))), (LV, byj, 40, ((0, 8, 56), (16, 32, 64), (48, 32, 8))),
-                                   (LN, byj, 32, ((0, 8, 64), (16, 24, 72), (48, 32, 16))), (LA, byi, 96, ())):
+        for l, pat, base, tail in ((LP, byi, 80, ((0, 4, 0), (4, 2, 72), (6, 3, 48), (9, 1, 8))),
+                                   (LV, byj, 40, ((0, 4, 8), (4, 1, 80), (6, 3, 56), (9, 1, 48))),
+                                   (LN, byj, 32, ((0, 3, 16), (5, 1, 32), (6, 3, 64), (9, 1, 56))),
+                                   (LA, byi, 88, ()), (LB, byj, 40, ())):
             iota(X("lr", 16 * l, 16 * l + 200), pat, base)
-            iota(X("lr", 16 * l + 24, 16 * l + 200, 25), [[0, 8]], 48)
+            if l in (LV, LB):
+                iota(X("lr", 16 * l, 16 * l + 200, 5), [[1, 8], [-8 if l == LV else 0, 5]], 88)
+            for c in range(5 if l == LA else 0):
+                iota(X("lr", 16 * l + c, 16 * l + 200, 25), [[1, 8]], 96)
+            for c in (0, 24) if l < LA else (24,):
+                iota(X("lr", 16 * l + c, 16 * l + 200, 25), [[0, 8]], 40)
             for c, n, b in tail:
-                iota(X("lr", 16 * l + 224 + c, 16 * l + 224 + c + n), [[1, n]], b)
+                iota(X("lr", 16 * l + 224 + 8 * c, 16 * l + 224 + 8 * (c + n)), [[1, 8 * n]], b)
         iota(W("pack"), [[0, 8], [8, 5], [1, 5]], 0)
         iota(X("pack", 24, 200, 25), [[0, 8]], 63)
         vts(W("pack"), W("pack"), 16384.0, 8192.0, AL.mult, AL.add)
-        iota(X("thr", 0, 16), [[0, 16]], 7 << 17)
-        for m in range(1, 5):
-            iota(X("thr", 8 + 8 * m, 16 + 8 * m), [[0, 8]], (5 - m) << 17)
-        iota(X("thr", 48, 80), [[-16384, 4], [0, 8]], 4 << 14)
+        iota(X("thr", 0, 32), [[-16384, 4], [0, 8]], 4 << 14)
+        for k, v in enumerate((1, 7, 4, 3, 2, 7)):
+            iota(X("thr", 32 + 8 * k, 40 + 8 * k), [[0, 8]], v << 17)
         vts(W("i7"), W("mhi"), -8.0, I_, AL.mult, AL.add)
-        vts(X("l6", 0, 6), X("cf", 0, 6), 3.0, 8.0, AL.is_ge, AL.mult)
+        vts(X("l6", 0, 6), X("cf", 0, 6), 2.0, 8.0, AL.is_lt, AL.mult)
         vts(W("LM"), X("l6", 0, 6), W("i7"), None, AL.add)
         vts(X("l6", 0, 4), X("cf", 0, 4), 16.0, 4112.0, AL.mult, AL.add)
         vts(W("du"), X("l6", 0, 4), I_, None, AL.add)
@@ -434,16 +472,17 @@ def program(g, core, T, topo):
         fI, fL, t1, t2, t3 = [W(n) for n in ("fI", "fL", "t1w", "t2w", "t3w")]
         iota(fI, [[-1, 8], [0, 8]], 5)
         iota(fL, [[-1, 8], [-1, 8]], 10)
-        vts(t1, fL, I_, -6.0, AL.subtract, AL.add)
+        vts(t1, fL, I_, -5.0, AL.subtract, AL.add)
         vts(t2, fL, I_, None, AL.is_gt)
         vtt(t1, t1, t2, AL.mult)
+        vts(W("i5"), I_, 5.0, 1.0, AL.is_ge, AL.add)
         vts(t2, t1, -1.0, I_, AL.mult, AL.add)
-        vts(t2, t2, 1.0, None, AL.add)
+        vts(t2, t2, W("i5"), None, AL.add)
         vts(t3, fI, I_, None, AL.is_ge)
         vtt(t2, t2, t3, AL.mult)
         vtt(t1, t1, t2, AL.add)
-        vts(W("tw"), t1, 5.0, 128.0, AL.add, AL.mult)
-        vms(X("xa", 640, 768), -1.0)
+        vts(W("tw"), t1, 4.0, 128.0, AL.add, AL.mult)
+        vms(X("xa", 512, 640), -1.0)
 
     def tolist():
         o = X("pb5", 0, NL)
@@ -451,80 +490,91 @@ def program(g, core, T, topo):
         vts(W("LL"), o, 0.0625, None, AL.mult)
 
     def join_early(t):
-        vts(X("aw", 0, 96), X("la%d" % t, 0, 96), 2.0, 1.0, AL.mult, AL.add)
+        vts(X("aw", 0, 88), X("la%d" % t, 0, 88), 2.0, 1.0, AL.mult, AL.add)
         for a, b, n in ((0, 13, 200), (14, 19, 80)):
             c, d = 16 * a, 16 * b
-            act(X("narr", c, d), IX("aw", 0, 96, "LL", LN + a, LN + b), AF.Copy)
-            act(X("varr", c, d), IX("aw", 0, 96, "LL", LV + a, LV + b), AF.Identity, scale=296.0, bias=CB)
-            vtt(X("tj", c, d), IX("aw", 0, 96, "LL", LP + a, LP + b), X("narr", c, d), AL.mult)
+            act(X("narr", c, d), IX("aw", 0, 88, "LL", LN + a, LN + b), AF.Copy)
+            act(X("varr", c, d), IX("aw", 0, 88, "LL", LV + a, LV + b), AF.Identity, scale=296.0, bias=CB)
+            vtt(X("tj", c, d), IX("aw", 0, 88, "LL", LP + a, LP + b), X("narr", c, d), AL.mult)
             vtt(X("zj", c, c + n), X("tj", c, c + n), X("varr", c, c + n), AL.add)
             vts(X("hji", c, c + n), X("zj", c, c + n), 4, 4095, AL.arith_shift_right, AL.bitwise_and)
             if a == 0:
-                act(W("bj"), IX("aw", 0, 96, "LL", LV, LV + 13), AF.Copy)
                 vtt(W("hp"), X("hji", 0, 200), W("pack"), AL.add)
+
+    def join_b5(t):
+        act(W("bj"), IX("aw", 0, 96, "LL", LB, LB + 13), AF.Copy)
 
     def join(t):
         vtt(W("eq"), IX("aw", 0, 104, "LL", LA, LA + 13), W("bj"), AL.is_equal)
         act(X("neq", 0, 200), X("eq", 0, 200), AF.Identity, scale=-1.0, bias=1.0)
         vtt(W("ek"), X("eq", 0, 200), W("hp"), AL.mult)
-        vtt(W("t8"), X("aw", 96, 104), X("aw", 80, 88), AL.mult)
-        vtt(W("z8"), W("t8"), X("varr", 264, 272), AL.add)
-        vts(X("hji", 264, 272), W("z8"), 4, 4095, AL.arith_shift_right, AL.bitwise_and)
+        vtt(X("tj", 248, 264), X("aw", 88, 104), X("tj", 248, 264), AL.mult)
+        vts(X("varr", 264, 272), X("aw", 96, 104), 296.0, CB, AL.mult, AL.add)
+        vtt(X("zj", 248, 272), X("tj", 248, 272), X("varr", 248, 272), AL.add)
+        vts(X("hji", 248, 272), X("zj", 248, 272), 4, 4095, AL.arith_shift_right, AL.bitwise_and)
         vscan(W("scj"), X("neq", 0, 200), W("ek"), NONE, AL.mult, AL.add)
-        vcp(X("w16", 0, 8), X("scj", 23, 200, 25))
+        val = X("scj", 23, 200, 25)
+        vcp(X("w16", 0, 8), val)
+        vts(W("t8"), val, -16384.0, -1.0, AL.add, AL.mult)
         vts(X("w16", 8, 16), X("w16", 0, 8), (1 << 17) - 1, None, AL.bitwise_and)
-        vts(X("hji", 232, 240), X("w16", 0, 8), 4095, None, AL.bitwise_and)
+        vtt(W("t9"), W("t8"), X("hji", 264, 272), AL.min)
+        vts(W("z8"), X("w16", 0, 8), 4095, None, AL.bitwise_and)
+        vtt(X("hji", 264, 272), W("t9"), W("z8"), AL.max)
         vtt(W("aa"), IX("w16", 0, 16, "LM", 0, 5), W("thr"), AL.subtract)
         vtt(W("bb"), W("aa"), X("hji", 224, 304), AL.max)
         vts(W("off"), W("bb"), 4096.0, None, AL.min)
-        vts(W("hm"), IX("bb", 0, 80, "LL", LX, LX + 20), 4192.0, -2048.0, AL.min, AL.add)
 
     def lessen(t):
-        xv = OPT["xv"]
-        act(X("xr", xv, 1280), IX("tab", 0, TW, "off", xv // 16, 80), AF.Copy)
+        for a, b in ((0, 3), (3, 5)):
+            vcp(X("xr", 128 * a, 128 * b), IX("tab", 0, TW, "off", 8 * a, 8 * b))
+            act(X("xr", 128 * a + 640, 128 * b + 640), IX("tab", 0, TW, "off", 8 * a + 40, 8 * b + 40), AF.Copy)
         mark.append(len(ops) - 1)
-        vcp(X("xr", 0, xv), IX("tab", 0, TW, "off", 0, xv // 16))
+        for h in range(2):
+            vts(X("hm", 160 * h, 160 * h + 160), IX("bb", 0, 80, "LL", LX + 10 * h, LX + 10 * h + 10), 4192.0, -2048.0, AL.min, AL.add)
+            ops[-1]["mdep"] = [mark[-1] - 1]
         tot, cnt = X("pb0", 0, 128), X("pb1", 0, 8)
-        for k in range(10):
+        for k in (0, 1, 2, 5, 6, 7, 3, 4, 8, 9):
             mm([(tot, W("ibf"), X("xr", k * 128, k * 128 + 128), k == 0, k == 9)])
         vts(W("ge"), tot, W("thf"), None, AL.is_ge)
         mm([(cnt, X("selc", 128 * i, 128 * i + 128), X("ge", i, 128, 16), i == 0, i == 15) for i in range(16)])
         vts(W("u8"), cnt, -8.5, -4400.0, AL.add, AL.mult)
-        vtt(W("rep"), IX("u8", 0, 8, "LL", LH, LH + 20), W("hm"), AL.max)
         for c in range(0, 1280, 128):
             vts(X("nd1", c, c + 128), X("xr", c, c + 128), -0.25, -191.625, AL.mult, AL.add)
             vts(X("nd", c, c + 128), X("nd1", c, c + 128), 192.0, None, AL.add)
-        rep = X("rep", 0, 80)
-        mm([(X("pb5", 0, 80), W("ibf"), rep, True, False)])
         c0 = 0
-        parts = (("pb6", range(6), ()), ("pb7", (), range(4)), ("pb4", (), range(4, 8)), ("pb2", (), range(8, 12)), ("pb0", (), range(12, 16)),
-                 ("pb1", range(6, 8), ()))
-        for j, (bk, within, cross) in enumerate(parts):
-            l, s, c = [], [], 0
-            for d in within:
-                l.append((X(bk, c, c + 80), X("dw", d * 128, d * 128 + 128), rep, True, True))
-                s.append((X("pb5", 0, 80), X("tg", d * 128, d * 128 + 128), X("fl2", c0 + c, c0 + c + 80), False, d == 7))
-                c += 80
-            for i in cross:
-                o = X(bk, c, c + 120)
-                l += [(o, W("ibf"), X("rep", 80, 200), True, False), (o, X("nsb", i * 128, i * 128 + 128), X("rep", 200, 320), False, True)]
-                s += [(X("pb5", a, 80), W("i8k"), X("fl2", c0 + c + b, c0 + c + b + 80 - a), False, False) for a, b in ((20, 0), (40, 60), (60, 100))]
-                c += 120
-            mm(l)
-            if j < OPT["ns"]:
-                act(X("ab2", c0, c0 + c), X(bk, 0, c), AF.Abs)
-                act(X("fl2", c0, c0 + c), X("ab2", c0, c0 + c), AF.Relu, scale=-1.0, bias=1.0)
-            else:
-                vts(X("fl2", c0, c0 + c), X(bk, 0, c), 0.0, None, AL.is_equal)
-            late.append(s)
-            if j >= OPT["ns"]:
-                mm(late.pop())
-            c0 += c
-            if j == 4:
-                while late:
-                    mm(late.pop())
-        for c in range(4):
-            vts(X("offs", c, 80, 4), X("pb5", 20 * c, 20 * c + 20), 2048.0, X("du", c, c + 1), AL.add, AL.min)
+        for h, (zb, bks) in enumerate((("pb5", ("pb6", "pb7", "pb4")), ("pb2", ("pb0", "pb1", "pb3")))):
+            r0 = 160 * h
+            vtt(X("rep", r0, r0 + 160), IX("u8", 0, 8, "LL", LH + 10 * h, LH + 10 * h + 10), X("hm", r0, r0 + 160), AL.max)
+            rep, z = X("rep", r0, r0 + 40), X(zb, 0, 40)
+            mm([(z, W("ibf"), rep, True, False)])
+            sums = []
+            for j, (bk, within, cross) in enumerate(zip(bks, (range(8), (), ()), (range(2), range(2, 9), range(9, 16)))):
+                l, s, c = [], [], 0
+                for d in within:
+                    l.append((X(bk, c, c + 40), X("dw", d * 128, d * 128 + 128), rep, True, True))
+                    s.append((z, X("tg", d * 128, d * 128 + 128), X("fl2", c0 + c, c0 + c + 40), False, False))
+                    c += 40
+                for i in cross:
+                    o = X(bk, c, c + 60)
+                    l += [(o, W("ibf"), X("rep", r0 + 40, r0 + 100), True, False),
+                          (o, X("nsb", i * 128, i * 128 + 128), X("rep", r0 + 100, r0 + 160), False, True)]
+                    s += [(X(zb, a, 40), W("i8k"), X("fl2", c0 + c + b, c0 + c + b + 40 - a), False, (i, a) == (15, 30))
+                          for a, b in ((10, 0), (20, 30), (30, 50))]
+                    c += 60
+                mm(l)
+                if j < OPT["ns"][h]:
+                    act(X("ab2", c0, c0 + c), X(bk, 0, c), AF.Abs)
+                    act(X("fl2", c0, c0 + c), X("ab2", c0, c0 + c), AF.Relu, scale=-1.0, bias=1.0)
+                else:
+                    vts(X("fl2", c0, c0 + c), X(bk, 0, c), 0.0, None, AL.is_equal)
+                sums.append(s)
+                c0 += c
+            for s in sums:
+                mm(s)
+            for c in range(4):
+                vts(X("offs", 40 * h + c, 40 * h + 40, 4), X(zb, 10 * c, 10 * c + 10), 2048.0, X("du", c, c + 1), AL.add, AL.min)
+            if h == 0:
+                late.append(len(ops) - 1)
         for u in range(20):
             o = IX("tab", 0, TW, "offs", 4 * u, 4 * u + 4)
             a, b, l = X("xr", 64 * u, 64 * u + 64), X("nd", 64 * u, 64 * u + 64), X("offs", 4 * u, 4 * u + 4)
@@ -536,20 +586,22 @@ def program(g, core, T, topo):
 
     def rings(t):
         la = "la%d" % t
-        act(X("xa", 0, 640), IX("win", 0, 2048, la, 8, 48), AF.Copy)
+        act(X("xa", 0, 512), IX("win", 0, 2048, la, 8, 40), AF.Copy)
         ops[-1]["mdep"] = [mark[-1]]
-        act(X("xa", 768, 1536), IX("win", 0, 2048, la, 56, 104), AF.Copy)
+        act(X("xa", 640, 1536), IX("win", 0, 2048, la, 48, 104), AF.Copy)
         ops[-1]["mdep"] = [mark[-1]]
         vts(W("c8i"), X("w16", 0, 8), 14, None, AL.arith_shift_right)
+        ops[-1]["mdep"] = [mark[-1]]
         vcp(W("fl"), W("c8i"))
         vtt(W("of"), IX("tw", 0, 64, "fl", 0, 8), W("cf"), AL.add)
         vcp(W("ofu"), W("of"))
         for c in range(4):
             act(X("gy", c * 512, c * 512 + 512), IX("xa", 0, 1536, "ofu", c * 32, c * 32 + 32), AF.Copy)
-        y = X("pb3", 0, 128)
+        y = X("pb6", 0, 128)
         for c in range(4):
             mm([(y, X("selc", m * 128, m * 128 + 128), X("gy", m, 2048, 16), m == 0, m == 15) for m in range(c * 4, c * 4 + 4)])
         act(W("yo"), y, AF.Copy, scale=0.0625)
+        line.append(len(ops) - 1)
         dma((T.yr[:, t * 128:t * 128 + 128], [], 0), W("yo"))
 
     spread("S", "qa", 0, range(16))
@@ -561,7 +613,9 @@ def program(g, core, T, topo):
     for o in ops[i0:]:
         if o["e"] == "G":
             o["mdep"] = sent[-1:]
+            o["slack"] = 6.0
     for t in range(RO):
+        VB["aw"] = VB["aw%d" % t]
         first("b", t)
         first("a", t)
         if t + 1 < RO:
@@ -574,11 +628,26 @@ def program(g, core, T, topo):
                 if t == 0:
                     tolist()
                 join_early(t)
+                join_b5(t)
             step("a", t, a)
+        seq = [("a", t, 0)] + [(x, t, a) for a in range(1, 5) for x in "ba"]
+        ln = []
+        for k in range(1, OPT["halves"]):
+            who = {"x": seq[k], "y": seq[k - 1], "z": seq[k + 1] if k + 1 < len(seq) else None}
+            ln += [tags[who[w[0]] + (w[1:],)] for w in OPT["weave"].split() if who[w[0]] and who[w[0]] + (w[1:],) in tags]
+        for p, q in zip(ln, ln[1:]):
+            ops[q]["mdep"] = list(ops[q].get("mdep", ())) + [p]
         if OPT["pp"] == 1 and t + 1 < RO:
             prep(t + 1)
         join(t)
         lessen(t)
+        if OPT["pp"] == 2 and t + 1 < RO:
+            i0 = len(ops)
+            prep(t + 1)
+            for o in ops[i0:]:
+                if o["e"] == "V":
+                    o["mdep"] = [late[-1]]
+            ops[-2]["slack"] = OPT["ps"]
         rings(t)
 
     def meets(x, y):
@@ -595,7 +664,7 @@ def program(g, core, T, topo):
             for nm, lo, hi, s in regs:
                 for j, r2, w2 in seen.get(nm, ()):
                     if (rw or w2) and j != i and meets((lo, hi, s), r2):
-                        d[j] = d.get(j, False) or ops[j]["e"] != e or (e != "P" and bool(w2))
+                        d[j] = d.get(j, False) or ops[j]["e"] != e or e != "P"
         for nm in set(x[0] for x in o["r"] + o["w"] if x[0][:2] == "pb"):
             p = banks.get(nm)
             if p is not None:
@@ -616,63 +685,93 @@ def program(g, core, T, topo):
         npd = [0] * n
         for i, o in enumerate(ops):
             for j, need in pred[i] + [(j, ops[j]["e"] != o["e"]) for j in o.get("mdep", ())]:
-                succ[j].append((i, lam if need else 0.0))
+                succ[j].append((i, (lam if need else 0.0) + (ops[j].get("slack", 0.0) if o["e"] != "G" else 0.0)))
                 npd[i] += 1
-        pr = [0.0] * n
-        for i in range(n - 1, -1, -1):
-            pr[i] = ops[i]["c"] + ops[i].get("lat", 0) + max([pr[j] + w for j, w in succ[i]] or [0])
-        ready = [0.0] * n
-        cand = {e: [] for e in ("V", "S", "P", "G", "Y", "R")}
-        free = {e: 0.0 for e in cand}
-        for i in range(n):
-            if npd[i] == 0:
-                cand[ops[i]["e"]].append(i)
-        order = []
-
-        def soon(e, s):
-            out = [(ready[x], x) for x in cand[e] if ready[x] > s]
-            front = [(max(free[q], ready[x], s) + ops[x]["c"] + ops[x].get("lat", 0), x) for q in cand if q != e for x in cand[q]]
-            for _ in range(2):
-                nxt = []
-                for fin, x in front:
-                    for j, w in succ[x]:
-                        if npd[j] == 1 and fin < s + 1.5:
-                            r = max(ready[j], fin + w)
-                            if ops[j]["e"] == e:
-                                out.append((r, j))
-                            else:
-                                nxt.append((max(r, free[ops[j]["e"]]) + ops[j]["c"], j))
-                front = nxt
-            return out
-
-        while len(order) < n:
-            s, e = min((min(ready[i] for i in l) if e == "R" else max(free[e], min(ready[i] for i in l)), e) for e, l in cand.items() if l)
-            s += 1e-6
-            now = sorted((x for x in cand[e] if ready[x] <= s), key=lambda x: (-pr[x], x))
-            i = now[0]
-            if OPT["look"] and e in "VSP":
-                nx = [(r, j) for r, j in soon(e, s) if pr[j] > pr[i]]
-
-                def late_by(x, t0):
-                    t1 = t0 + ops[x]["c"]
-                    return max([t0 + pr[x]] + [t1 + pr[j] for j in now[:2] if j != x] + [max(r, t1) + pr[j] for r, j in nx if j != x])
-                if nx:
-                    i = min(now[:6], key=lambda x: (round(late_by(x, s) / OPT["look"]), -pr[x]))
-                    r, j = min(nx, key=lambda y: late_by(y[1], y[0]))
-                    if late_by(j, r) + OPT["look"] < late_by(i, s):
-                        free[e] = min(r, s + .03)
-                        continue
-            cand[e].remove(i)
-            order.append(i)
-            CACHE.setdefault("log", []).append((s, e, ops[i]["c"], pr[i], i))
-            free[e] = s + ops[i]["c"]
-            fin = s + ops[i]["c"] + ops[i].get("lat", 0)
+        left = list(npd)
+        topo_order = [i for i in range(n) if left[i] == 0]
+        for i in topo_order:
             for j, w in succ[i]:
-                npd[j] -= 1
-                ready[j] = max(ready[j], fin + w)
-                if npd[j] == 0:
-                    cand[ops[j]["e"]].append(j)
-        CACHE["order"] = order
+                left[j] -= 1
+                if left[j] == 0:
+                    topo_order.append(j)
+        assert len(topo_order) == n
+        cs = [o["c"] for o in ops]
+        es = [o["e"] for o in ops]
+        cl = [o["c"] + o.get("lat", 0) for o in ops]
+
+        def tails(order):
+            tl, nxt = [0.0] * n, {}
+            for i in reversed(order or topo_order):
+                tl[i] = cl[i] + max([tl[j] + w for j, w in succ[i]] or [0])
+                if order and es[i] != "R":
+                    if es[i] in nxt:
+                        tl[i] = max(tl[i], cs[i] + tl[nxt[es[i]]])
+                    nxt[es[i]] = i
+            return tl
+
+        def place(pr):
+            left, ready = list(npd), [0.0] * n
+            cand = {e: [] for e in ("V", "S", "P", "G", "Y", "R")}
+            free = {e: 0.0 for e in cand}
+            for i in range(n):
+                if left[i] == 0:
+                    cand[es[i]].append(i)
+            order = []
+
+            def soon(e, s):
+                out = [(ready[x], x) for x in cand[e] if ready[x] > s]
+                front = [(max(free[q], ready[x], s) + cl[x], x) for q in "VSP" if q != e for x in cand[q]]
+                for _ in range(2):
+                    nxt = []
+                    for fin, x in front:
+                        if fin < s + 1.5:
+                            for j, w in succ[x]:
+                                if left[j] == 1:
+                                    r = max(ready[j], fin + w)
+                                    if es[j] == e:
+                                        out.append((r, j))
+                                    else:
+                                        nxt.append((max(r, free[es[j]]) + cs[j], j))
+                    front = nxt
+                return out
+
+            while len(order) < n:
+                s, e = min((min(ready[i] for i in l) if e == "R" else max(free[e], min(ready[i] for i in l)), e) for e, l in cand.items() if l)
+                s += 1e-6
+                now = sorted((x for x in cand[e] if ready[x] <= s), key=lambda x: (-pr[x], x))
+                i = now[0]
+                if OPT["look"] and e in "VSP":
+                    nx = [(r, j) for r, j in soon(e, s) if pr[j] > pr[i]]
+
+                    def late_by(x, t0):
+                        t1 = t0 + cs[x]
+                        return max([t0 + pr[x]] + [t1 + pr[j] for j in now[:2] if j != x] + [max(r, t1) + pr[j] for r, j in nx if j != x])
+                    if nx:
+                        i = min(now[:6], key=lambda x: (round(late_by(x, s) / OPT["look"]), -pr[x]))
+                        r, j = min(nx, key=lambda y: late_by(y[1], y[0]))
+                        if late_by(j, r) + OPT["look"] < late_by(i, s):
+                            free[e] = min(r, s + .05)
+                            continue
+                cand[e].remove(i)
+                order.append(i)
+                free[e] = s + cs[i]
+                for j, w in succ[i]:
+                    left[j] -= 1
+                    ready[j] = max(ready[j], s + cl[i] + w)
+                    if left[j] == 0:
+                        cand[es[j]].append(j)
+            return order
+
+        CACHE["fn"] = (tails, place, ops)
+        pr, best = tails(None), None
+        for it in range(OPT["passes"]):
+            order = place(pr)
+            tl = tails(order)
+            if best is None or max(tl) < best[0]:
+                best = (max(tl), order)
+            CACHE.setdefault("log", []).append(round(max(tl), 1))
+            pr = [a + OPT["mix"] * (b - a) for a, b in zip(pr, tl)]
+        order = CACHE["order"] = best[1]
 
     qs = {"V": g.vector, "S": g.scalar, "P": g.tensor, "G": g, "Y": g.sync}
     known = {e: {} for e in qs}
@@ -715,6 +814,7 @@ def program(g, core, T, topo):
         g.wait_ge(T.sem["rq%d" % t], NE[t])
         g.wait_ge(T.sem["rs%d" % t], NE[t])
         g.wait_ge(T.sem["rb%d" % t], NB)
+        g.wait_ge(T.sem["rc%d" % t], NB)
     g.wait_ge(T.sem.ls, lsn)
 
 

import math
from concourse.bass import DstId, RemoteDMATransfer
from concourse.mybir import dt, AluOpType, AxisListType, ActivationFunctionType

AL = AluOpType
AF = ActivationFunctionType
RO, ST, N = 3, 5, 8
TW = 4176
F, B, H, I32, U16 = "float32", "bfloat16", "float16", "int32", "uint16"
PHYS = {F: "vf", B: "vb", H: "vh", I32: "vi", U16: "vu"}
SIZE = {F: 0, B: 0, H: 0, I32: 0, U16: 0}
VB = {}


def _sb(dtype, **kw):
    for k, n in kw.items():
        VB[k] = (PHYS[dtype], SIZE[dtype], n)
        SIZE[dtype] += (n + 31) // 32 * 32


NL = 128
_sb(B, tab=TW, qa=2048, qb0=2048, qb1=2048, qw=512, cfx=144, cg=128, cr=128, c8=128, ibf=128, negib=128, bigi=128, ind=128, indl=128,
    indh=128, ind6=128, ind6l=128, ind6h=128, dl=144, dh=144, gk=8, ngk=8, oneb=128, crow=128, selc=2048, nsb=2048, dw=1024, tg=1024,
    i8k=128, fl2=2560, ab2=2560, xr=1280, nd1=1280, nd=1280, lr=16 * NL, ge=128)
VB["cf"] = (VB["cfx"][0], VB["cfx"][1] + 8, 128)
_sb(H, i594=128, da=128, db=128, rep=320, gy=2048)
_sb(F, win=2048, xa=1536, pf=1, gf=1, fi=1, mlo=1, mhi=1, ncorr=1, c1=1, i7=1, du=4, thf=1, rs=128, rs0=128, dm=128,
    s8a=8, s8b=8, src8=8, tgt8=8, l6=8, pack=200, thr=80, fI=64, fL=64, t1w=64, t2w=64, t3w=64, tw=64,
    pm=128, cm=128, tp=128, aw=104, narr=320, varr=320, bj=208, tj=320, hp=200, eq=208, neq=208, ek=200, scj=200,
    t8=8, t9=8, i5=1, aa=80, bb=80, hm=320, u8=8, of=128, yo=128)
_sb(I32, nbi=2048, sti=64, stin0=64, stin1=64, stin2=64, pi=1, gi=1, thi=1, zpi=128, hpi=128, hji=320, zj=320, z8=8, w16=16, c8i=8)
_sb(U16, LL=NL, LM=6, off=80, offs=80, fl=8, ofu=128)
for _x in "ab":
    _sb(F, **{"t1" + _x: 128, "r" + _x: 128, "rr" + _x: 128, "sc" + _x: 128})
    _sb(I32, **{"zi" + _x: 128, "hi" + _x: 128})
    _sb(U16, **{"hl" + _x: 128})
    _sb(B, **{"pn" + _x: 640, "mk" + _x: 128, "dif" + _x: 2048, "ad" + _x: 2048, "xs" + _x: 2048})
    _sb(H, **{"dn" + _x: 128, "w" + _x: 128})
for _t in range(RO):
    _sb(B, **{"pn0%d" % _t: 128})
    _sb(H, **{"xa%d" % _t: 640, "xb%d" % _t: 640, "dn0%d" % _t: 128})
    _sb(F, **{"pa%d" % _t: 512, "pb_%d" % _t: 512, "aw%d" % _t: 104, "b5%d" % _t: 8})
    _sb(U16, **{"h0%d" % _t: 128, "la%d" % _t: 104, "lb%d" % _t: 48})
SCRATCH = {PHYS[d]: ("sbuf", [128, SIZE[d]], d) for d in PHYS}
for _i in range(8):
    SCRATCH["pb%d" % _i] = ("psum", [128, 512], F)
    VB["pb%d" % _i] = ("pb%d" % _i, 0, 512)
NDMA = 12
SEMAPHORES = ["sV", "sS", "sP", "sG", "ls"] + ["d%d" % i for i in range(NDMA)] + ["rq%d" % i for i in range(RO)] + \
    ["rs%d" % i for i in range(RO)] + ["rb%d" % i for i in range(RO)] + ["rc%d" % i for i in range(RO)]
CACHE = {}
BIG = 16777216.0
TOP = 100000.0
CB = -296.0 - 8388608.0
NONE = 63 * 16384.0 + 8192.0
OPT = dict(nv=640, nc=640, nv0=(512, 640), nvl=1024, ncl=1024, gat=1.56, lam=.15, ns=(0, 3), vs=3, ksp=0, look=.08, rl=4.0, rsp=1, bw=512, line=1, pp=2, ps=2.0,
           passes=1, mix=.3, cut=(96, 96, 256, 96, 96), cutl=(96, 96, 256, 128, 192), halves=9, penl=0,
           weave="xdn ymin xg0 yback xg1 yeq xg2 yw xb0 ysc xg3 yvl xg4 zt1 xr0 zzi xr1 zhi zhl")


def program(g, core, T, topo):
    rank = T.rank_of(core)
    ops = []
    dn = [0]
    GAT = OPT["gat"]

    def X(n, a, b, s=1, p=None):
        ph, o, _ = VB[n]
        ps = slice(None) if p is None else slice(p[0], p[1])
        cs = slice(o + a, o + b, s) if s > 1 else slice(o + a, o + b)
        return (T[ph][ps, cs], [(ph, o + a, o + b, s)], len(range(a, b, s)))

    def W(n):
        return X(n, 0, VB[n][2])

    def REV(n, m):
        ph, o, w = VB[n]
        return (T[ph][0:m, slice(o + w - 1, o - 1, -1)], [(ph, o, o + w, 1)], w)

    def IX(n, a, b, o, c, d):
        w, l = X(n, a, b), X(o, c, d)
        return (w[0].indirect(l[0]), w[1] + l[1], 16 * (d - c), "ix")

    def add(e, fn, r, w, c, **kw):
        ops.append(dict(e=e, fn=fn, r=[y for x in r for y in x[1]], w=[y for x in w for y in x[1]], c=c, **kw))
        return len(ops) - 1

    def sc(s):
        return (s[0], [s]) if isinstance(s, tuple) else (s, [])

    def cost(o, ins, k=None):
        if len(o) > 3:
            k = 3.8
        elif len(ins) and len(ins[0]) > 3:
            k = GAT
        elif k is None:
            k = .5 if all(x[1][0][0] in ("vb", "vh", "vu") for x in [o] + ins) else 1.0
        return max(64, o[2] * k) * .83e-3

    def vts(o, a, s1, s2, o0, o1=None):
        (v1, r1), (v2, r2) = sc(s1), sc(s2)
        if o1 is None:
            f = lambda: [g.vector.tensor_scalar(out=o[0], in0=a[0], scalar1=v1, scalar2=None, op0=o0)]
        else:
            f = lambda: [g.vector.tensor_scalar(out=o[0], in0=a[0], scalar1=v1, scalar2=v2, op0=o0, op1=o1)]
        add("V", f, [a] + r1 + r2, [o], .05 + cost(o, [a]))

    def vtt(o, a, b, op):
        k = 1.0 if "pb" in (a[1][0][0][:2], b[1][0][0][:2]) else 2.0
        add("V", lambda: [g.vector.tensor_tensor(out=o[0], in0=a[0], in1=b[0], op=op)], [a, b], [o], .05 + cost(o, [a, b], k))

    def vcp(o, a):
        add("V", lambda: [g.vector.tensor_copy(out=o[0], in_=a[0])], [a], [o], .05 + cost(o, [a]))

    def vms(o, v):
        add("V", lambda: [g.vector.memset(o[0], v)], [], [o], .05 + cost(o, []))

    def vscan(o, d0, d1, ini, o0, o1):
        add("V", lambda: [g.vector.tensor_tensor_scan(out=o[0], data0=d0[0], data1=d1[0], initial=ini, op0=o0, op1=o1)],
            [d0, d1], [o], .05 + cost(o, [d0, d1]))

    def act(o, a, fn, bias=None, scale=None):
        kw, r = {}, []
        if bias is not None:
            kw["bias"], rr = sc(bias)
            r = r + rr
        if scale is not None:
            kw["scale"], rr = sc(scale)
            r = r + rr
        add("S", lambda: [g.scalar.activation(out=o[0], in_=a[0], func=fn, **kw)], [a] + r, [o], .065 + cost(o, [a], 1.0))

    def mm(l):
        c = sum(max(min(64, a[2]), b[2]) for o, a, b, s, p in l)
        add("P", lambda: [g.tensor.matmul(out=o[0], lhsT=a[0], rhs=b[0], start=s, stop=p) for o, a, b, s, p in l],
            [x for m in l for x in m[1:3]], [m[0] for m in l], c * .42e-3)

    def iota(o, pat, base, cm=0):
        kw = {} if o[1][0][0] == "vi" else {"allow_small_or_imprecise_dtypes": True}
        add("G", lambda: [g.iota(o[0], pattern=pat, base=base, channel_multiplier=cm, **kw)], [], [o], .13 + 2 * o[2] * .83e-3)

    def keep(o, a, pat, cm, op=None, fill=0.0):
        op = AL.is_equal if op is None else op
        add("G", lambda: [g.affine_select(out=o[0], in_=a[0], pattern=pat, compare_op=op, fill=fill, base=0, channel_multiplier=cm)],
            [a], [o], .17 + 2 * o[2] * .83e-3)

    def dma(o, a, lat=2.5):
        i = dn[0]
        dn[0] += 1
        add("Y", lambda: [g.sync.dma_start(out=o[0], in_=a[0])], [a], [o], .1, lat=lat, sem="d%d" % i)

    def ext(n):
        return (T[n][:], [], 0)

    outq = [T.cores[(rank + 1 + t % (N - 1)) % N] for t in range(RO)]
    back = [T.cores[(rank - 1 - t % (N - 1)) % N] for t in range(RO)]
    NE = (2, 1, 1)
    NB = 4

    def engs(dst, first, n):
        m = 0
        for e in topo.engines(core, dst)[::2][first:first + n]:
            m |= 1 << e
        return m

    def exchange(ts):
        tr = []
        for t in ts:
            a = topo.addr(outq[t])
            for kind, src, dst in (("s", W("sti"), W("stin%d" % t)), ("q", X("qw", 0, 128), X("qw", 128 * t + 128, 128 * t + 256))):
                tr.append(RemoteDMATransfer(dst_ids=[DstId(rid=a[0], pnc=a[1])], dma_engine_mask=engs(outq[t], NE[t] * len(tr), NE[t]),
                                            remote_sem=T.sem["r%s%d" % (kind, t)], src=src[0], dst=dst[0]))
        g.remote_dma_fused(tr, local_sem=T.sem.ls)
        return []

    def sendb(t, dst, src, sem):
        a = topo.addr(back[t])
        g.remote_dma(out_ap=dst[0], in_ap=src[0], remote_sem=T.sem[sem], local_sem=T.sem.ls,
                     pid=a[1], routing_id=a[0], dma_engine_mask=engs(back[t], 0, NB))
        return []

    lsn = 2 * sum(NE) + 2 * NB * RO

    dma(X("sti", 0, 24), ext("st"), 2.0)
    dma(X("qw", 0, 128), ext("q"), 2.0)
    dma(W("nbi"), ext("nb"), 6.0)
    dma(X("tab", 0, 4096), ext("ang"), 9.0)
    dma(W("thi"), ext("th"), 9.0)
    for i in range(1, 5):
        ops[i]["mdep"] = [i - 1]
    vms(X("sti", 24, 64), 0)
    sent = []
    for ts in ((0,), (1, 2)):
        sent.append(len(ops))
        s = add("G", lambda ts=ts: exchange(ts), [W("sti"), X("qw", 0, 128)], [], 1.0 if ts[0] else 3.0)
        for t in ts:
            lat = 14.0 if t else 4.0
            add("R", None, [], [W("stin%d" % t)], lat, mdep=[s], sem="rs%d" % t, cnt=NE[t])
            add("R", None, [], [X("qw", 128 * t + 128, 128 * t + 256)], lat, mdep=[s], sem="rq%d" % t, cnt=NE[t])

    iota(W("pi"), [[0, 1]], 0, 1)
    iota(W("pf"), [[0, 1]], 0, 1)
    iota(W("cfx"), [[1, 144]], -8)
    iota(W("cg"), [[1, 8], [0, 16]], 0)
    iota(W("cr"), [[0, 8], [1, 16]], 0)
    iota(W("c8"), [[0, 16], [1, 8]], 0)
    act(X("win", 0, 128), W("cf"), AF.Copy)
    for c in (128, 256, 512, 1024):
        act(X("win", c, 2 * c), X("win", 0, c), AF.Identity, bias=float(c))
    P_, G_, I_ = W("pf"), W("gf"), W("fi")
    vts(W("gi"), W("pi"), 4, None, AL.arith_shift_right)
    vcp(G_, W("gi"))
    vts(I_, G_, -16.0, P_, AL.mult, AL.add)
    vts(W("mhi"), I_, 8.0, None, AL.is_ge)
    vts(W("mlo"), I_, 8.0, None, AL.is_lt)
    vts(W("ncorr"), I_, 8192.0, -122880.0, AL.mult, AL.add)
    vts(W("c1"), I_, 8192.0, -122879.5, AL.mult, AL.add)
    for n, v in (("ibf", 1.0), ("negib", -1.0), ("bigi", 131072.0), ("i594", 594.0), ("i8k", 8192.0)):
        vts(W(n), W("cf"), P_, v, AL.is_equal, AL.mult)
    for n, v in (("dl", W("mlo")), ("dh", W("mhi"))):
        vts(W(n), W("cfx"), P_, v, AL.is_equal, AL.mult)
    for n, v in (("ind", 1.0), ("indl", W("mlo")), ("indh", W("mhi")), ("ind6", 592.0)):
        vts(W(n), W("cg"), G_, v, AL.is_equal, AL.mult)
    vts(W("ind6l"), W("indl"), 592.0, None, AL.mult)
    vts(W("ind6h"), W("indh"), 592.0, None, AL.mult)
    vts(W("gk"), X("cg", 0, 128, 16), G_, 16.0, AL.is_equal, AL.mult)
    vts(W("ngk"), X("cg", 0, 128, 16), G_, -16.0, AL.is_equal, AL.mult)
    vms(W("oneb"), 1.0)
    vms(W("crow"), 1.0)
    vms(X("crow", 0, 128, 1, (0, 1)), -8388608.0)
    vms(X("tab", 4096, TW), 0.0)
    vts(W("rs"), W("cr"), 0.0, TOP, AL.is_equal, AL.mult)
    vts(W("rs0"), W("c8"), 0.0, TOP, AL.is_equal, AL.mult)
    vts(W("dm"), W("cr"), I_, BIG + 8192, AL.is_gt, AL.mult)
    vts(W("dm"), W("dm"), -BIG, None, AL.add)
    vcp(W("thf"), W("thi"))
    for t in range(RO):
        la = "la%d" % t
        vcp(X(la, 0, 8), X("sti", 8 * t, 8 * t + 8))
        vms(X(la, 40, 96), 0)
        vcp(X(la, 48, 56), X("sti", 8 * t, 8 * t + 8))
        vcp(X("lb%d" % t, 0, 8), X("stin%d" % t, 8 * t, 8 * t + 8))
    one1 = X("oneb", 0, 128, 1, (0, 1))

    def spread(e, dst, src, ks):
        for k in ks:
            o, a = X(dst, k, 2048, 16), X("qw", 128 * src, 128 * src + 128)
            if e == "G":
                keep(o, a, [[0, 128]], 0)
            elif e == "V":
                vcp(o, a)
            else:
                act(o, a, AF.Copy)

    def prep(t):
        la, lb = IX("win", 0, 2048, "la%d" % t, 48, 56), IX("win", 0, 2048, "lb%d" % t, 0, 8)
        xa, xb = X("xa%d" % t, 0, 128), X("xb%d" % t, 0, 128)
        act(xa, la, AF.Copy)
        act(xb, lb, AF.Copy)
        act(X("pa%d" % t, 0, 128), la, AF.Identity, scale=4.0, bias=2.0)
        act(X("pb_%d" % t, 0, 128), lb, AF.Identity, scale=4.0, bias=2.0)
        vtt(W("da"), IX("nbi", 0, 2048, "la%d" % t, 48, 56), xa, AL.subtract)
        vtt(W("db"), IX("nbi", 0, 2048, "lb%d" % t, 0, 8), xb, AL.subtract)
        xm, d, nm = X("pb5", 0, 128), X("pb5", 128, 256), X("pb4", 0, 128)
        lo, up, hi, dw_ = X("dl", 8, 136), X("dl", 0, 128), X("dh", 8, 136), X("dh", 16, 144)
        lx = [(0, lo, "xa%d" % t, 0), (0, hi, "xa%d" % t, 1), (64, lo, "xb%d" % t, 0), (64, hi, "xb%d" % t, 1)]
        ld = [(0, lo, "da", 0), (0, up, "da", 1), (64, dw_, "db", 0), (64, hi, "db", 1)]
        for o, l in ((xm, lx), (nm, lx + ld), (d, ld)):
            bk, c0 = o[1][0][0], o[1][0][1]
            mm([(X(bk, c0 + c, c0 + c + 64), a, X(b, par, 128, 2), i == 0, i == len(l) - 1) for i, (c, a, b, par) in enumerate(l)])
            if o is xm:
                act(W("pm"), xm, AF.Identity, scale=4.0, bias=2.0)
                act(W("cm"), xm, AF.Identity, scale=594.0, bias=-8388607.0)
        act(W("dn0%d" % t), d, AF.Copy)
        vtt(W("tp"), W("pm"), nm, AL.mult)
        vtt(W("zpi"), W("tp"), W("cm"), AL.add)
        vts(W("hpi"), W("zpi"), 4, 4095, AL.arith_shift_right, AL.bitwise_and)
        vcp(W("h0%d" % t), W("hpi"))
        vts(W("pn0%d" % t), W("dn0%d" % t), 0.0, None, AL.is_equal)

    rot, line, tags, at = [0], [], {}, [None]

    def tag(name):
        tags[at[0] + (name,)] = len(ops) - 1

    def inline(tot):
        ops[-1]["mdep"] = line[-1:]
        if tot == 2048:
            line.append(len(ops) - 1)

    def records(x, hl, h0, qx, tot, nv, nc):
        st = 2048 // tot
        ch = [(max(b - 512, nv), b) for b in range(tot, nv, -512)][::-1]
        for a, b in ch:
            act(X("xs" + x, a, b), IX("tab", 0, TW, hl, h0 + a // 16, h0 + b // 16), AF.Copy)
            inline(tot)
        cut = [0]
        for w in (OPT["cut"] if nv == sum(OPT["cut"]) and tot == 2048 else OPT["cutl"] if tot == 2048 else (nv,)):
            cut.append(cut[-1] + w)
        for j, (a, b) in enumerate(zip(cut, cut[1:])):
            vtt(X("dif" + x, a, b), IX("tab", 0, TW, hl, h0 + a // 16, h0 + b // 16), X(qx, a * st, b * st, st), AL.subtract)
            tag("g%d" % j)
        cut = (0, cut[len(cut) // 2], nc) if tot == 2048 else (0, nc)
        for j, (a, b) in enumerate(zip(cut, cut[1:])):
            vts(X("ad" + x, a, b), X("dif" + x, a, b), 0.0, 2.0, AL.max, AL.mult)
            tag("r%d" % j)
        if nv > nc:
            act(X("ad" + x, nc, nv), X("dif" + x, nc, nv), AF.Abs)
        for a, b in ch:
            rot[0] += 1
            o = X("pb%d" % (5 + rot[0] % 3), 0, b - a)
            mm([(o, W("negib"), X(qx, a * st, b * st, st), True, False)])
            mm([(o, W("ibf"), X("xs" + x, a, b), False, True)])
            act(X("ad" + x, a, b), o, AF.Abs)
            inline(tot)

    def keys(x, kb, pn, tot, nc):
        m = tot // 16
        key = X(kb, 0, 128, 1, (0, m))
        mm([(key, X("oneb", 0, m, 1, (0, 1)), X("cr", 0, 128, 1, (0, 1)), True, False)])
        e = len(pn) - (min(OPT["penl"], len(pn)) if m == 128 else 0)
        if e:
            mm([(key, p, W("bigi"), False, False) for p in pn[:e]])
        if nc:
            mm([(X(kb, k, 128, 16, (0, nc // 16)), X("dif" + x, k, nc, 16), W("ngk"), False, False) for k in range(16)])
        cut = (0, 96, 128) if m == 128 and OPT["ksp"] else (0, m)
        for a, b in zip(cut, cut[1:]):
            mm([(X(kb, k, 128, 16, (a, b)), X("ad" + x, 16 * a + k, 16 * b, 16), W("gk"), False, k == 15 and b == m and e == len(pn)) for k in range(16)])
        for p in pn[e:]:
            mm([(key, p, W("bigi"), False, p is pn[-1])])
        return key

    def choose(x, key, rs, d, m):
        r, mk = X("r" + x, 0, 128, 1, (0, m)), X("mk" + x, 0, 128, 1, (0, m))
        vscan(r, X(rs, 0, 128, 1, (0, m)), key, TOP, AL.max, AL.min)
        tag("min")
        vscan(REV("rr" + x, m), X(rs, 0, 128, 1, (0, m)), REV("r" + x, m), TOP, AL.max, AL.min)
        tag("back")
        vtt(mk, X("rr" + x, 0, 128, 1, (0, m)), key, AL.is_equal)
        tag("eq")
        m1 = X("pb%d" % "ab".index(x), 256, 256 + m)
        mm([(m1, mk, X("ibf", 0, m, 1, (0, m)), True, True)])
        vtt(X("w" + x, 0, m), m1, d, AL.mult)
        tag("w")

    def after(x, t, a):
        i = "ab".index(x)
        bb, xo = X("pb%d" % (2 + i), 0, 128), X("x%s%d" % (x, t), a * 128, a * 128 + 128)

        def sums(bk, c, ind):
            if a:
                mm([(X(bk, c, c + 128), W(ind), W("w" + x), False, True)])
            else:
                mm([(X(bk, c + par, c + 128, 2), W(ind + "lh"[par]), X("w" + x, 0, 64), False, par == 1) for par in range(2)])
        mm([(bb, W("ibf"), xo, True, False)])
        sums("pb%d" % (2 + i), 0, "ind")
        if a < 4:
            cc = X("pb%d" % i, 128, 256)
            mm([(cc, X("crow", 0, 128, 1, (0, 2)), X("oneb", 0, 128, 1, (0, 2)), True, False), (cc, W("i594"), xo, False, False)])
            sums("pb%d" % i, 128, "ind6")
        vscan(W("sc" + x), W("dm"), bb, 0.0, AL.add, AL.max)
        tag("sc")
        last = X("sc" + x, 15, 128, 16)
        if x == "a" and a == 4:
            vts(X("aw", 96, 104), last, W("c1"), 2.0, AL.add, AL.mult)
        c = 8 + 8 * a if x == "b" else 56 + 8 * a if a < 4 else 96
        if (x, a) == ("b", 4):
            vts(W("b5%d" % t), last, W("c1"), 2.0, AL.add, AL.mult)
        else:
            vts(X("l%s%d" % (x, t), c, c + 8), last, W("ncorr"), None, AL.add)
        tag("vl")
        if a < 4:
            act(X("x%s%d" % (x, t), (a + 1) * 128, (a + 2) * 128), bb, AF.Copy)
        if a < 3:
            act(X(("pa%d" if x == "a" else "pb_%d") % t, (a + 1) * 128, (a + 2) * 128), bb, AF.Identity, scale=4.0, bias=2.0)

    def first(x, t):
        i = "ab".index(x)
        at[0] = (x, t, 0)
        records(x, "h0%d" % t, 64 * i, "qa" if x == "a" else "qb%d" % (t % 2), 1024, OPT["nv0"][i], OPT["nv0"][i])
        key = keys(x, "pb%d" % i, [X("pn0%d" % t, 64 * i, 64 * i + 64)], 1024, OPT["nv0"][i])
        choose(x, key, "rs0", X("dn0%d" % t, 64 * i, 64 * i + 64), 64)
        after(x, t, 0)

    def step(x, t, a):
        i = "ab".index(x)
        xh, c = "x%s%d" % (x, t), (48 if x == "a" else 0) + 8 * a
        nb = IX("nbi", 0, 2048, "l%s%d" % (x, t), c, c + 8)
        xo, d = X(xh, a * 128, a * 128 + 128), W("dn" + x)
        at[0] = (x, t, a)
        vtt(W("t1" + x), nb, X(("pa%d" if x == "a" else "pb_%d") % t, (a - 1) * 128, a * 128), AL.mult)
        tag("t1")
        vtt(W("zi" + x), W("t1" + x), X("pb%d" % i, 128, 256), AL.add)
        tag("zi")
        vts(W("hi" + x), W("zi" + x), 4, 4095, AL.arith_shift_right, AL.bitwise_and)
        tag("hi")
        vcp(W("hl" + x), W("hi" + x))
        tag("hl")
        nv = nc = sum(OPT["cutl"] if (x, a) == ("a", 4) else OPT["cut"])
        records(x, "hl" + x, 0, "qa" if x == "a" else "qb%d" % (t % 2), 2048, nv, nc)
        vtt(d, nb, xo, AL.subtract)
        tag("dn")
        n, pd = min(a + 1, 4), "pb4"
        for m in range(n):
            o = X(pd, m * 128, m * 128 + 128)
            mm([(o, W("ibf"), xo, True, False), (o, W("ibf"), d, False, True)])
        for c0 in range(0, n * 128, OPT["bw"]):
            c1 = min(c0 + OPT["bw"], n * 128)
            vtt(X("pn" + x, c0, c1), X(xh, c0, c1), X(pd, c0, c1), AL.is_equal)
            tag("b%d" % (c0 // OPT["bw"]))
        if a == 4:
            vts(X("pn" + x, 512, 640), d, 0.0, None, AL.is_equal)
        key = keys(x, "pb%d" % i, [X("pn" + x, m * 128, m * 128 + 128) for m in range(a + 1)], 2048, nc)
        choose(x, key, "rs", d, 128)
        after(x, t, a)
        if x == "b" and a >= 3:
            dst, src, sem = (X("la%d" % t, 8, 40), X("lb%d" % t, 8, 40), "rb%d" % t) if a == 3 else \
                (X("aw", 88, 96), W("b5%d" % t), "rc%d" % t)
            s = add("G", lambda: sendb(t, dst, src, sem), [src], [], 1.0)
            add("R", None, [], [dst], OPT["rl"], mdep=[s], sem=sem, cnt=NB)

    LP, LV, LN, LA, LB, LX, LH = 0, 20, 40, 60, 74, 88, 108

    def late_constants():
        iota(W("selc"), [[0, 2048]], 0)
        for i in range(16):
            keep(X("selc", 129 * i, 129 * i + 113, 16), X("ind", 0, 128, 16), [[0, 8]], 0)
        iota(W("nsb"), [[0, 2048]], -1)
        keep(W("nsb"), W("nsb"), [[-1, 16], [-16, 8], [0, 16]], 1)
        iota(X("lr", 0, 16 * LX), [[0, 16 * LX]], 40)
        c = 0
        for h in range(2):
            for p0, n in ((0, 4), (1, 3), (2, 2), (3, 1), (0, 3), (0, 2), (0, 1)):
                iota(X("lr", 16 * LX + c, 16 * LX + c + 10 * n), [[1, n], [4, 10]], p0 + 40 * h)
                iota(X("lr", 16 * LH + c, 16 * LH + c + 10 * n), [[1, n], [0, 5], [4, 2]], p0)
                c += 10 * n
        byi, byj = [[1, 8], [-8, 5], [0, 5]], [[1, 8], [0, 5], [-8, 5]]
        for l, pat, base, tail in ((LP, byi, 80, ((0, 4, 0), (4, 2, 72), (6, 3, 48), (9, 1, 8))),
                                   (LV, byj, 40, ((0, 4, 8), (4, 1, 80), (6, 3, 56), (9, 1, 48))),
                                   (LN, byj, 32, ((0, 3, 16), (5, 1, 32), (6, 3, 64), (9, 1, 56))),
                                   (LA, byi, 88, ()), (LB, byj, 40, ())):
            iota(X("lr", 16 * l, 16 * l + 200), pat, base)
            if l in (LV, LB):
                iota(X("lr", 16 * l, 16 * l + 200, 5), [[1, 8], [-8 if l == LV else 0, 5]], 88)
            for c in range(5 if l == LA else 0):
                iota(X("lr", 16 * l + c, 16 * l + 200, 25), [[1, 8]], 96)
            for c in (0, 24) if l < LA else (24,):
                iota(X("lr", 16 * l + c, 16 * l + 200, 25), [[0, 8]], 40)
            for c, n, b in tail:
                iota(X("lr", 16 * l + 224 + 8 * c, 16 * l + 224 + 8 * (c + n)), [[1, 8 * n]], b)
        iota(W("pack"), [[0, 8], [8, 5], [1, 5]], 0)
        iota(X("pack", 24, 200, 25), [[0, 8]], 63)
        vts(W("pack"), W("pack"), 16384.0, 8192.0, AL.mult, AL.add)
        iota(X("thr", 0, 32), [[-16384, 4], [0, 8]], 4 << 14)
        for k, v in enumerate((1, 7, 4, 3, 2, 7)):
            iota(X("thr", 32 + 8 * k, 40 + 8 * k), [[0, 8]], v << 17)
        vts(W("i7"), W("mhi"), -8.0, I_, AL.mult, AL.add)
        vts(X("l6", 0, 6), X("cf", 0, 6), 2.0, 8.0, AL.is_lt, AL.mult)
        vts(W("LM"), X("l6", 0, 6), W("i7"), None, AL.add)
        vts(X("l6", 0, 4), X("cf", 0, 4), 16.0, 4112.0, AL.mult, AL.add)
        vts(W("du"), X("l6", 0, 4), I_, None, AL.add)
        dd = X("cf", 1, 9)
        vts(W("s8a"), dd, I_, 16.0, AL.is_gt, AL.mult)
        vtt(W("s8b"), W("s8a"), dd, AL.subtract)
        vts(W("src8"), W("s8b"), P_, None, AL.add)
        vts(W("s8a"), dd, I_, 15.0, AL.add, AL.is_le)
        vtt(W("s8b"), W("s8a"), dd, AL.mult)
        vts(W("tgt8"), W("s8b"), P_, None, AL.add)
        for d in range(8):
            vts(X("dw", d * 128, d * 128 + 128), W("cf"), X("src8", d, d + 1), -1.0, AL.is_equal, AL.mult)
            vts(X("tg", d * 128, d * 128 + 128), W("cf"), X("tgt8", d, d + 1), 8192.0, AL.is_equal, AL.mult)
        keep(W("dw"), W("dw"), [[0, 8], [-1, 128]], 1, AL.not_equal, 1.0)
        fI, fL, t1, t2, t3 = [W(n) for n in ("fI", "fL", "t1w", "t2w", "t3w")]
        iota(fI, [[-1, 8], [0, 8]], 5)
        iota(fL, [[-1, 8], [-1, 8]], 10)
        vts(t1, fL, I_, -5.0, AL.subtract, AL.add)
        vts(t2, fL, I_, None, AL.is_gt)
        vtt(t1, t1, t2, AL.mult)
        vts(W("i5"), I_, 5.0, 1.0, AL.is_ge, AL.add)
        vts(t2, t1, -1.0, I_, AL.mult, AL.add)
        vts(t2, t2, W("i5"), None, AL.add)
        vts(t3, fI, I_, None, AL.is_ge)
        vtt(t2, t2, t3, AL.mult)
        vtt(t1, t1, t2, AL.add)
        vts(W("tw"), t1, 4.0, 128.0, AL.add, AL.mult)
        vms(X("xa", 512, 640), -1.0)

    def tolist():
        o = X("pb5", 0, NL)
        mm([(o, X("selc", 128 * i, 128 * i + 128), X("lr", i, 16 * NL, 16), i == 0, i == 15) for i in range(16)])
        vts(W("LL"), o, 0.0625, None, AL.mult)

    def join_early(t):
        vts(X("aw", 0, 88), X("la%d" % t, 0, 88), 2.0, 1.0, AL.mult, AL.add)
        for a, b, n in ((0, 13, 200), (14, 19, 80)):
            c, d = 16 * a, 16 * b
            act(X("narr", c, d), IX("aw", 0, 88, "LL", LN + a, LN + b), AF.Copy)
            act(X("varr", c, d), IX("aw", 0, 88, "LL", LV + a, LV + b), AF.Identity, scale=296.0, bias=CB)
            vtt(X("tj", c, d), IX("aw", 0, 88, "LL", LP + a, LP + b), X("narr", c, d), AL.mult)
            vtt(X("zj", c, c + n), X("tj", c, c + n), X("varr", c, c + n), AL.add)
            vts(X("hji", c, c + n), X("zj", c, c + n), 4, 4095, AL.arith_shift_right, AL.bitwise_and)
            if a == 0:
                vtt(W("hp"), X("hji", 0, 200), W("pack"), AL.add)

    def join_b5(t):
        act(W("bj"), IX("aw", 0, 96, "LL", LB, LB + 13), AF.Copy)

    def join(t):
        vtt(W("eq"), IX("aw", 0, 104, "LL", LA, LA + 13), W("bj"), AL.is_equal)
        act(X("neq", 0, 200), X("eq", 0, 200), AF.Identity, scale=-1.0, bias=1.0)
        vtt(W("ek"), X("eq", 0, 200), W("hp"), AL.mult)
        vtt(X("tj", 248, 264), X("aw", 88, 104), X("tj", 248, 264), AL.mult)
        vts(X("varr", 264, 272), X("aw", 96, 104), 296.0, CB, AL.mult, AL.add)
        vtt(X("zj", 248, 272), X("tj", 248, 272), X("varr", 248, 272), AL.add)
        vts(X("hji", 248, 272), X("zj", 248, 272), 4, 4095, AL.arith_shift_right, AL.bitwise_and)
        vscan(W("scj"), X("neq", 0, 200), W("ek"), NONE, AL.mult, AL.add)
        val = X("scj", 23, 200, 25)
        vcp(X("w16", 0, 8), val)
        vts(W("t8"), val, -16384.0, -1.0, AL.add, AL.mult)
        vts(X("w16", 8, 16), X("w16", 0, 8), (1 << 17) - 1, None, AL.bitwise_and)
        vtt(W("t9"), W("t8"), X("hji", 264, 272), AL.min)
        vts(W("z8"), X("w16", 0, 8), 4095, None, AL.bitwise_and)
        vtt(X("hji", 264, 272), W("t9"), W("z8"), AL.max)
        vtt(W("aa"), IX("w16", 0, 16, "LM", 0, 5), W("thr"), AL.subtract)
        vtt(W("bb"), W("aa"), X("hji", 224, 304), AL.max)
        vts(W("off"), W("bb"), 4096.0, None, AL.min)

    def lessen(t):
        for a, b in ((0, 3), (3, 5)):
            vcp(X("xr", 128 * a, 128 * b), IX("tab", 0, TW, "off", 8 * a, 8 * b))
            act(X("xr", 128 * a + 640, 128 * b + 640), IX("tab", 0, TW, "off", 8 * a + 40, 8 * b + 40), AF.Copy)
        mark.append(len(ops) - 1)
        for h in range(2):
            vts(X("hm", 160 * h, 160 * h + 160), IX("bb", 0, 80, "LL", LX + 10 * h, LX + 10 * h + 10), 4192.0, -2048.0, AL.min, AL.add)
            ops[-1]["mdep"] = [mark[-1] - 1]
        tot, cnt = X("pb0", 0, 128), X("pb1", 0, 8)
        for k in (0, 1, 2, 5, 6, 7, 3, 4, 8, 9):
            mm([(tot, W("ibf"), X("xr", k * 128, k * 128 + 128), k == 0, k == 9)])
        vts(W("ge"), tot, W("thf"), None, AL.is_ge)
        mm([(cnt, X("selc", 128 * i, 128 * i + 128), X("ge", i, 128, 16), i == 0, i == 15) for i in range(16)])
        vts(W("u8"), cnt, -8.5, -4400.0, AL.add, AL.mult)
        for c in range(0, 1280, 128):
            vts(X("nd1", c, c + 128), X("xr", c, c + 128), -0.25, -191.625, AL.mult, AL.add)
            vts(X("nd", c, c + 128), X("nd1", c, c + 128), 192.0, None, AL.add)
        c0 = 0
        for h, (zb, bks) in enumerate((("pb5", ("pb6", "pb7", "pb4")), ("pb2", ("pb0", "pb1", "pb3")))):
            r0 = 160 * h
            vtt(X("rep", r0, r0 + 160), IX("u8", 0, 8, "LL", LH + 10 * h, LH + 10 * h + 10), X("hm", r0, r0 + 160), AL.max)
            rep, z = X("rep", r0, r0 + 40), X(zb, 0, 40)
            mm([(z, W("ibf"), rep, True, False)])
            sums = []
            for j, (bk, within, cross) in enumerate(zip(bks, (range(8), (), ()), (range(2), range(2, 9), range(9, 16)))):
                l, s, c = [], [], 0
                for d in within:
                    l.append((X(bk, c, c + 40), X("dw", d * 128, d * 128 + 128), rep, True, True))
                    s.append((z, X("tg", d * 128, d * 128 + 128), X("fl2", c0 + c, c0 + c + 40), False, False))
                    c += 40
                for i in cross:
                    o = X(bk, c, c + 60)
                    l += [(o, W("ibf"), X("rep", r0 + 40, r0 + 100), True, False),
                          (o, X("nsb", i * 128, i * 128 + 128), X("rep", r0 + 100, r0 + 160), False, True)]
                    s += [(X(zb, a, 40), W("i8k"), X("fl2", c0 + c + b, c0 + c + b + 40 - a), False, (i, a) == (15, 30))
                          for a, b in ((10, 0), (20, 30), (30, 50))]
                    c += 60
                mm(l)
                if j < OPT["ns"][h]:
                    act(X("ab2", c0, c0 + c), X(bk, 0, c), AF.Abs)
                    act(X("fl2", c0, c0 + c), X("ab2", c0, c0 + c), AF.Relu, scale=-1.0, bias=1.0)
                else:
                    vts(X("fl2", c0, c0 + c), X(bk, 0, c), 0.0, None, AL.is_equal)
                sums.append(s)
                c0 += c
            for s in sums:
                mm(s)
            for c in range(4):
                vts(X("offs", 40 * h + c, 40 * h + 40, 4), X(zb, 10 * c, 10 * c + 10), 2048.0, X("du", c, c + 1), AL.add, AL.min)
            if h == 0:
                late.append(len(ops) - 1)
        for u in range(20):
            o = IX("tab", 0, TW, "offs", 4 * u, 4 * u + 4)
            a, b, l = X("xr", 64 * u, 64 * u + 64), X("nd", 64 * u, 64 * u + 64), X("offs", 4 * u, 4 * u + 4)
            add("V", lambda o=o, a=a, b=b: [g.vector.tensor_tensor(out=o[0], in0=a[0], in1=b[0], op=AL.add)], [a, b, l], [X("tab", 0, TW)], .25)
        if t == RO - 1:
            dma((T.ye[:], [], 0), X("tab", 0, 4096), 6.0)

    mark, late = [], []

    def rings(t):
        la = "la%d" % t
        act(X("xa", 0, 512), IX("win", 0, 2048, la, 8, 40), AF.Copy)
        ops[-1]["mdep"] = [mark[-1]]
        act(X("xa", 640, 1536), IX("win", 0, 2048, la, 48, 104), AF.Copy)
        ops[-1]["mdep"] = [mark[-1]]
        vts(W("c8i"), X("w16", 0, 8), 14, None, AL.arith_shift_right)
        ops[-1]["mdep"] = [mark[-1]]
        vcp(W("fl"), W("c8i"))
        vtt(W("of"), IX("tw", 0, 64, "fl", 0, 8), W("cf"), AL.add)
        vcp(W("ofu"), W("of"))
        for c in range(4):
            act(X("gy", c * 512, c * 512 + 512), IX("xa", 0, 1536, "ofu", c * 32, c * 32 + 32), AF.Copy)
        y = X("pb6", 0, 128)
        for c in range(4):
            mm([(y, X("selc", m * 128, m * 128 + 128), X("gy", m, 2048, 16), m == 0, m == 15) for m in range(c * 4, c * 4 + 4)])
        act(W("yo"), y, AF.Copy, scale=0.0625)
        line.append(len(ops) - 1)
        dma((T.yr[:, t * 128:t * 128 + 128], [], 0), W("yo"))

    spread("S", "qa", 0, range(16))
    spread("V", "qb0", 1, range(0, 16, 2))
    spread("G", "qb0", 1, range(1, 16, 2))
    prep(0)
    i0 = len(ops)
    late_constants()
    for o in ops[i0:]:
        if o["e"] == "G":
            o["mdep"] = sent[-1:]
            o["slack"] = 6.0
    for t in range(RO):
        VB["aw"] = VB["aw%d" % t]
        first("b", t)
        first("a", t)
        if t + 1 < RO:
            if OPT["pp"] == 0:
                prep(t + 1)
            spread("G", "qb%d" % ((t + 1) % 2), t + 2, range(16))
        for a in range(1, 5):
            step("b", t, a)
            if a == 4:
                if t == 0:
                    tolist()
                join_early(t)
                join_b5(t)
            step("a", t, a)
        seq = [("a", t, 0)] + [(x, t, a) for a in range(1, 5) for x in "ba"]
        ln = []
        for k in range(1, OPT["halves"]):
            who = {"x": seq[k], "y": seq[k - 1], "z": seq[k + 1] if k + 1 < len(seq) else None}
            ln += [tags[who[w[0]] + (w[1:],)] for w in OPT["weave"].split() if who[w[0]] and who[w[0]] + (w[1:],) in tags]
        for p, q in zip(ln, ln[1:]):
            ops[q]["mdep"] = list(ops[q].get("mdep", ())) + [p]
        if OPT["pp"] == 1 and t + 1 < RO:
            prep(t + 1)
        join(t)
        lessen(t)
        if OPT["pp"] == 2 and t + 1 < RO:
            i0 = len(ops)
            prep(t + 1)
            for o in ops[i0:]:
                if o["e"] == "V":
                    o["mdep"] = [late[-1]]
            ops[-2]["slack"] = OPT["ps"]
        rings(t)

    def meets(x, y):
        (lo, hi, s), (l2, h2, s2) = x, y
        return l2 < hi and lo < h2 and (lo - l2) % math.gcd(s, s2) == 0

    n = len(ops)
    pred = [[] for _ in range(n)]
    seen, banks = {}, {}
    for i, o in enumerate(ops):
        e = o["e"]
        d = {}
        for rw, regs in ((0, o["r"]), (1, o["w"])):
            for nm, lo, hi, s in regs:
                for j, r2, w2 in seen.get(nm, ()):
                    if (rw or w2) and j != i and meets((lo, hi, s), r2):
                        d[j] = d.get(j, False) or ops[j]["e"] != e or e != "P"
        for nm in set(x[0] for x in o["r"] + o["w"] if x[0][:2] == "pb"):
            p = banks.get(nm)
            if p is not None:
                d[p] = d.get(p, False) or ops[p]["e"] != e
            banks[nm] = i
        for rw, regs in ((0, o["r"]), (1, o["w"])):
            for nm, lo, hi, s in regs:
                l = seen.setdefault(nm, [])
                if rw and s == 1:
                    l[:] = [x for x in l if not (lo <= x[1][0] and x[1][1] <= hi)]
                l.append((i, (lo, hi, s), rw))
        pred[i] = sorted(d.items())

    order = CACHE.get("order")
    if order is None:
        lam = OPT["lam"]
        succ = [[] for _ in range(n)]
        npd = [0] * n
        for i, o in enumerate(ops):
            for j, need in pred[i] + [(j, ops[j]["e"] != o["e"]) for j in o.get("mdep", ())]:
                succ[j].append((i, (lam if need else 0.0) + (ops[j].get("slack", 0.0) if o["e"] != "G" else 0.0)))
                npd[i] += 1
        left = list(npd)
        topo_order = [i for i in range(n) if left[i] == 0]
        for i in topo_order:
            for j, w in succ[i]:
                left[j] -= 1
                if left[j] == 0:
                    topo_order.append(j)
        assert len(topo_order) == n
        cs = [o["c"] for o in ops]
        es = [o["e"] for o in ops]
        cl = [o["c"] + o.get("lat", 0) for o in ops]

        def tails(order):
            tl, nxt = [0.0] * n, {}
            for i in reversed(order or topo_order):
                tl[i] = cl[i] + max([tl[j] + w for j, w in succ[i]] or [0])
                if order and es[i] != "R":
                    if es[i] in nxt:
                        tl[i] = max(tl[i], cs[i] + tl[nxt[es[i]]])
                    nxt[es[i]] = i
            return tl

        def place(pr):
            left, ready = list(npd), [0.0] * n
            cand = {e: [] for e in ("V", "S", "P", "G", "Y", "R")}
            free = {e: 0.0 for e in cand}
            for i in range(n):
                if left[i] == 0:
                    cand[es[i]].append(i)
            order = []

            def soon(e, s):
                out = [(ready[x], x) for x in cand[e] if ready[x] > s]
                front = [(max(free[q], ready[x], s) + cl[x], x) for q in "VSP" if q != e for x in cand[q]]
                for _ in range(2):
                    nxt = []
                    for fin, x in front:
                        if fin < s + 1.5:
                            for j, w in succ[x]:
                                if left[j] == 1:
                                    r = max(ready[j], fin + w)
                                    if es[j] == e:
                                        out.append((r, j))
                                    else:
                                        nxt.append((max(r, free[es[j]]) + cs[j], j))
                    front = nxt
                return out

            while len(order) < n:
                s, e = min((min(ready[i] for i in l) if e == "R" else max(free[e], min(ready[i] for i in l)), e) for e, l in cand.items() if l)
                s += 1e-6
                now = sorted((x for x in cand[e] if ready[x] <= s), key=lambda x: (-pr[x], x))
                i = now[0]
                if OPT["look"] and e in "VSP":
                    nx = [(r, j) for r, j in soon(e, s) if pr[j] > pr[i]]

                    def late_by(x, t0):
                        t1 = t0 + cs[x]
                        return max([t0 + pr[x]] + [t1 + pr[j] for j in now[:2] if j != x] + [max(r, t1) + pr[j] for r, j in nx if j != x])
                    if nx:
                        i = min(now[:6], key=lambda x: (round(late_by(x, s) / OPT["look"]), -pr[x]))
                        r, j = min(nx, key=lambda y: late_by(y[1], y[0]))
                        if late_by(j, r) + OPT["look"] < late_by(i, s):
                            free[e] = min(r, s + .05)
                            continue
                cand[e].remove(i)
                order.append(i)
                free[e] = s + cs[i]
                for j, w in succ[i]:
                    left[j] -= 1
                    ready[j] = max(ready[j], s + cl[i] + w)
                    if left[j] == 0:
                        cand[es[j]].append(j)
            return order

        CACHE["fn"] = (tails, place, ops)
        pr, best = tails(None), None
        for it in range(OPT["passes"]):
            order = place(pr)
            tl = tails(order)
            if best is None or max(tl) < best[0]:
                best = (max(tl), order)
            CACHE.setdefault("log", []).append(round(max(tl), 1))
            pr = [a + OPT["mix"] * (b - a) for a, b in zip(pr, tl)]
        order = CACHE["order"] = best[1]

    qs = {"V": g.vector, "S": g.scalar, "P": g.tensor, "G": g, "Y": g.sync}
    known = {e: {} for e in qs}
    cnt = {e: 0 for e in "VSPG"}
    done = {}
    for i in order:
        o = ops[i]
        e = o["e"]
        if e == "R":
            done[i] = (o["sem"], o["cnt"], {o["sem"]: o["cnt"]})
            continue
        kn = known[e]
        for j, need in sorted(pred[i], reverse=True):
            if not need:
                continue
            sm, c, snap = done[j]
            if c > kn.get(sm, 0):
                qs[e].wait_ge(T.sem[sm], c)
                for a, b in snap.items():
                    if b > kn.get(a, 0):
                        kn[a] = b
        ins = o["fn"]()
        if e == "Y":
            ins[0].then_inc(T.sem[o["sem"]], 16)
            sm, c = o["sem"], 16
        else:
            sm = "s" + e
            for x in ins:
                x.then_inc(T.sem[sm], 1)
            cnt[e] += len(ins)
            c = cnt[e]
        snap = dict(kn)
        snap[sm] = c
        done[i] = (sm, c, snap)
    for e in "VSPG":
        g.wait_ge(T.sem["s" + e], cnt[e])
    for i in range(dn[0]):
        g.wait_ge(T.sem["d%d" % i], 16)
    for t in range(RO):
        g.wait_ge(T.sem["rq%d" % t], NE[t])
        g.wait_ge(T.sem["rs%d" % t], NE[t])
        g.wait_ge(T.sem["rb%d" % t], NB)
        g.wait_ge(T.sem["rc%d" % t], NB)
    g.wait_ge(T.sem.ls, lsn)


def rank_program(g, core, T, topo):
    if T.rank_of(core) is not None:
        program(g, core, T, topo)
